import numpy as np, ml_dtypes
CORES = [2,3,42,43,82,83,122,123]
N = 8
import mx_ref
BF = ml_dtypes.bfloat16
def gcols(t, e):
    v = np.concatenate([t.reshape(8, 16, -1, 4), np.zeros((8, 16, 1, 4), BF)], axis=2)
    return np.ascontiguousarray(np.stack([v[g][:, e[g]] for g in range(8)])).reshape(128, -1)
def tile(rs):
    return np.stack(rs, axis=2).reshape(128, -1).astype(BF)
def pick(q, e):
    c = np.concatenate([q[0].reshape(128, -1, 4), np.zeros((128, 1, 4), np.uint8)], axis=1); s = np.concatenate([q[1], np.ones((16, 1), np.uint8)], axis=1)
    return (np.ascontiguousarray(c[:, e].reshape(128, -1)), np.ascontiguousarray(s[:, e]))
def join(*qs):
    return (np.concatenate([q[0] for q in qs], axis=1), np.concatenate([q[1] for q in qs], axis=1))
def put(q, e, v):
    c, s = q[0].reshape(128, -1, 4).copy(), q[1].copy(); c[:, e] = v[0].reshape(128, -1, 4); s[:, e] = v[1]
    return (c.reshape(128, -1), s)
def pk(c, s):
    return (np.ascontiguousarray(c), mx_ref.live(s))
def emit(q):
    return q[0], q[1]
def packed(v, rng):
    q = [mx_ref.quantize(np.ascontiguousarray(v[r])) for r in range(N)]
    return np.stack([a for a, b in q]), np.stack([mx_ref.plane(b, rng) for a, b in q])
def values_of_codes():
    e, c = np.zeros((128, 128, 4), np.float32), np.zeros((128, 2, 4), np.uint8)
    e[np.arange(128), np.arange(128), 0] = 1
    c[:127, :, 0] = np.arange(256).reshape(2, 128).T[:127]
    return mx_ref.matmul(mx_ref.quantize(e.reshape(128, 512).astype(BF)), (c.reshape(128, 8), np.full((16, 2), 127, np.uint8))).T.reshape(-1).astype(np.float64)
CODE_VALUE, SCALE_VALUE = values_of_codes(), 2.0 ** (np.arange(256) - 127.0)
def decode(q):
    return (CODE_VALUE[q[0]].reshape(16, 8, -1, 4) * SCALE_VALUE[q[1]][:, None, :, None] + 0.0).reshape(128, -1).astype(np.float32)
def f(rng, *shape):
    return mx_ref.flush((rng.standard_normal(shape, dtype=np.float32) * np.exp2(rng.integers(-2, 3, shape[:-1] + (1,)))).astype(BF))
def wide(rng, *shape, cols=0):
    v = rng.standard_normal(shape, dtype=np.float32) * np.exp2(rng.integers(-12, 13, shape)).astype(np.float32)
    if cols: v *= np.repeat(np.exp2(rng.integers(-cols, cols + 1, shape[:-2] + (1, shape[-1] // 4))) * (rng.random(shape[:-2] + (1, shape[-1] // 4)) > 0.0625), 4, axis=-1).astype(np.float32)
    return mx_ref.flush(v.astype(BF))
C, CAP = 384, 160
MASK = [1, 2, 4]
def big(v):
    v = v.astype(np.float32)
    v[np.abs(v) < np.float32(2.0 ** -16)] = 0
    return v.astype(BF)
def alike(u):
    return np.stack([np.reshape(u, (128, 512)).astype(np.float32).astype(BF)] * N)
def numbers_of(rng):
    return {"x": big(f(rng, N, 128, 4 * C)), "u": alike(f(rng, 128, 512)), "v": np.array(f(rng, N, 128, 512))}
def parts(d):
    u = d["u"][0].astype(np.float32).reshape(128, 128, 4)
    u[:, ::16] = 0
    u[:, 1::16] = 0
    return d["x"].astype(np.float32).reshape(N, 8, 16, C, 4), u
def back(x):
    return x.astype(np.float32).reshape(N, 128, 4 * C).astype(BF)
def weights(rng, still=[]):
    w = big(f(rng, N, 128, 2048)).reshape(N, 8, 16, 4, 8, 16, 4)
    for i in still:
        w[:, :, i] = 0
        w[:, :, :, :, :, i] = 0
    c, s = packed(w.reshape(N, 128, 2048), rng)
    return {"wc": c, "ws": s}
def setup_inputs(rng):
    return {**numbers_of(rng), **weights(rng)}
def setup_inputs_ties(rng):
    d = numbers_of(rng)
    x, u = parts(d)
    e = rng.permutation(N)
    k = rng.integers(0, 3, (N, 8, C))
    s = rng.integers(-1, 2, (N, 8, C))
    k[e[0]] = 0
    k[e[1]] *= -1
    k[e[3]] = np.arange(C) // 128
    s[e[0]] = 0
    s[e[2]] = 1
    s[e[3]] = -1
    x[:, :, :2] = 0
    x[:, :, 0, :, 0] = k
    x[:, :, 1, :, 0] = s
    for h in range(0, 128, 16):
        u[h, h, 0] = 1
        u[h + 1, h + 1, 0] = 1
    return {"x": back(x), "u": alike(u), "v": d["v"], **weights(rng, [0, 1])}
def setup_inputs_near(rng):
    d = numbers_of(rng)
    x, u = parts(d)
    x[:, :, 0] = 0
    x[:, :, 8:] = 0
    o = rng.permutation(8)
    s = rng.integers(0, 16, (N, 8, C))
    sign = rng.integers(-1, 2, (N, 8, C))
    for g in range(8):
        h, kind = 16 * g, o[g] // 2
        if kind < 3:
            c = 2.0 ** -30 if kind == 2 else 1.0
            x[:, g, 0, :, 0] = 1.0 if kind == 0 else -1.0 if kind == 1 else rng.integers(0, 2, (N, C)) * 2.0 - 1.0
            x[:, g, 8] = ((s[:, g, :, None] >> np.arange(4)) & 1) * np.exp2(np.arange(4) - 23.0)
            x[:, g, 11, :, 0] = 2.0 ** -10
            x[:, g, 9, :, 0] = sign[:, g] * 2.0 ** -23
            u[h, h, 0] = c
            u[h + 8, h] = c
            u[h + 11, h, 0] = c
            u[h + 9, h + 1, 0] = 2.0 ** -30
        else:
            t = s[:, g] // 4 % 2
            x[:, g, 10, :, 0] = np.where(s[:, g] < 8, -1.0, 1.0) * (1.0 + (s[:, g] % 4) * 0.125) * 2.0 ** -30
            x[:, g, 12, :, 0] = -t * (1.25 * 2.0 ** -30)
            x[:, g, 13, :, 0] = t * (1.125 * 2.0 ** -30)
            x[:, g, 9, :, 0] = sign[:, g] * (1.125 * 2.0 ** -30)
            x[:, g, 14, :, 0] = -sign[:, g] * (1.25 * 2.0 ** -30)
            u[h + 10, h, 0] = 2.0 ** -30
            u[h + 12, h, 0] = 2.0 ** -30
            u[h + 13, h, 0] = 1.125 * 2.0 ** -30
            u[h + 9, h + 1, 0] = 1.125 * 2.0 ** -30
            u[h + 14, h + 1, 0] = 2.0 ** -30
        if o[g] % 2:
            for r in range(N): x[r, g, 0 if kind < 3 else 10, rng.integers(C), 0] = 2.0 ** 29 * (rng.integers(0, 2) * 2.0 - 1.0)
    return {"x": back(x), "u": alike(u), "v": d["v"], **weights(rng, [0, 8, 9, 10, 11, 12, 13, 14, 15])}
def setup_inputs_caps(rng):
    d = numbers_of(rng)
    x, u = parts(d)
    k = rng.permutation([0, 1, CAP - 1, CAP, CAP + 1, 257, C - 1, C])
    x[:, :, 0] = 0
    x[:, :, 0, :, 0] = np.where(np.arange(C) < k[:, None], 1.0, -1.0) * (1.0 + 0.125 * rng.integers(0, 8, (N, 8, C)))
    x[:, :, 0, :, 1:3] = rng.integers(-3, 4, (N, 8, C, 2)) * 0.03125
    a = (1.125 + 0.25 * rng.integers(0, 4, (N, 8, C, 32))) * np.exp2(-rng.integers(8, 15, (N, 8, C, 32)).astype(np.float32))
    np.put_along_axis(a, rng.integers(0, 32, (N, 8, C, 1)), 1.96875, axis=3)
    a *= (rng.integers(0, 2, a.shape) * 2.0 - 1.0) * np.exp2(rng.integers(-3, 4, (N, 8, C, 1)).astype(np.float32))
    x[:, :, 8:] = a.reshape(N, 8, C, 8, 4).transpose(0, 1, 3, 2, 4)
    for h in range(0, 128, 16):
        u[h, h, :3] = 1
        u[h, h + 1, 0] = 1
    return {"x": back(x), "u": alike(u), "v": d["v"], **weights(rng, [0])}
def setup_inputs_huge(rng):
    d = numbers_of(rng)
    x, u = parts(d)
    h = rng.permutation(8)
    x = (0.75 + 0.2 * rng.random((N, 8, 16, C, 4))) * 2.0 ** 30
    x[:, h[:4]] *= -1.0
    x[:, h[4:]] *= rng.integers(0, 2, (N, 1, 1, C, 1)) * 2.0 - 1.0
    for i in range(8):
        g = 16 * h[i]
        for a in (h[:4] if i < 2 else h[4:] if i in (4, 5) else h[i:i + 1]): u[16 * a:16 * a + 16, g] = 2.0 ** 30 * (1.0 - 0.1 * rng.random((16, 4)))
        if i == 1:
            for a in h[4:]: u[16 * a:16 * a + 16, g] = 0.875 * 2.0 ** 30 * (1.0 - 0.1 * rng.random((16, 4)))
        a = 16 * h[4 + i % 4]
        u[a:a + 16, g + 1] = 2.0 ** 30 * (1.0 - 0.1 * rng.random((16, 4))) * (rng.integers(0, 2) * 2.0 - 1.0)
    w = np.zeros((N, 128, 4, 128, 4), np.float32)
    i = np.arange(128)
    for b in range(4): w[:, i, b, i, b] = -1
    c, s = packed(w.reshape(N, 128, 2048).astype(BF), rng)
    return {"x": back(x), "u": alike(u), "v": d["v"], "wc": c, "ws": s}
def setup_inputs_spread(rng):
    d = setup_inputs(rng)
    d["x"] = big(wide(rng, N, 128, 4 * C, cols=6))
    return d
def check_inputs(d):
    b = []
    for k in ("x", "u", "v"):
        a = np.abs(d[k].astype(np.float32))
        if not (np.isfinite(a).all() and ((a == 0) | (a >= 2.0 ** -30) & (a <= 2.0 ** 30)).all()): b.append("a value of " + k)
    if (d["u"].astype(np.float32) != d["u"][:1].astype(np.float32)).any(): b.append("u isn't the same on all ranks")
    none, least, most = [emit(mx_ref.quantize(np.full((128, 16), k, np.float32).astype(BF)))[1][0, 0] for k in (0.0, 2.0 ** -30, 2.0 ** 30)]
    for r in range(N):
        if ((d["wc"][r] == 0x7F) | (d["wc"][r] == 0xFF)).any(): b.append("wc: a code that is no number")
        s = mx_ref.live(d["ws"][r])
        if ((s != none) & ((s < least) | (s > most))).any(): b.append("ws: a scale out of range")
    return b
def reference(x, u, v, wc, ws):
    qu = [mx_ref.quantize(u[r]) for r in range(N)]
    lay = [pk(wc[r], ws[r]) for r in range(N)]
    now = [x[r] for r in range(N)]
    before = np.arange(C)[:, None] < np.arange(C)
    for m in MASK:
        q = [mx_ref.quantize(now[r]) for r in range(N)]
        tab, take = np.zeros((N, 8, C), np.int64), np.zeros((N, 8, C), bool)
        for r in range(N):
            s = mx_ref.matmul(qu[r], q[r])
            k = s[::16] + np.float32(0.0)
            tab[r] = np.count_nonzero((k[:, :, None] >= k[:, None, :]) & before, axis=1)
            want = s[1::16] > 0
            np.put_along_axis(take[r], np.argsort(~want, axis=1, kind="stable")[:, :CAP], True, axis=1)
            take[r] &= want
        e = np.arange(N) ^ m
        mixed = np.where(take, tab[e], tab)
        place = np.zeros((N, 8, C), np.int64)
        for i in range(C):
            place[:, :, :i] += place[:, :, :i] >= mixed[:, :, i:i + 1]
            place[:, :, i] = mixed[:, :, i]
        o = np.argsort(place, axis=2, kind="stable")
        name = o + C * np.take_along_axis(take, o, axis=2)
        made = []
        for r in range(N):
            z = gcols(np.concatenate([now[r], decode(q[e[r]]).astype(BF)], axis=1), name[r])
            qz = mx_ref.quantize(z)
            made.append(tile([mx_ref.matmul(pick(lay[r], np.arange(128 * b, 128 * b + 128)), qz) * np.float32(0.03125) + z[:, b::4].astype(np.float32) for b in range(4)]))
        now = made
    y, od = np.zeros((N, 128, C), np.float32), np.zeros((N, 8, C), np.float32)
    oc, osc = np.zeros((N, 128, 4 * C), np.uint8), np.zeros((N, 16, C), np.uint8)
    for r in range(N):
        q = mx_ref.quantize(now[r])
        y[r] = mx_ref.matmul(mx_ref.quantize(v[r]), q)
        od[r] = name[r]
        oc[r], osc[r] = emit(q)
    return {"y": y, "od": od, "oc": oc, "osc": osc}

@@ -1,0 +1,325 @@
+from concourse.mybir import dt, AluOpType, ActivationFunctionType
+
+C, CAP, MASK = 384, 160, [1, 2, 4]
+NB = C // 16
+FS = 784
+BIG = 2.0 ** 96
+CODES, PLANE = "float8_e4m3fn_x4", "uint8"
+F32, BF, U16, I32 = "float32", "bfloat16", "uint16", "int32"
+ACT_BLOCKS = 6
+FIRST = 256
+
+
+def _sb(n, d):
+    return ("sbuf", [128, n], d)
+
+
+SCRATCH = {
+    "win": _sb(8 * C, BF), "xb": _sb(4 * C, BF), "ub": _sb(512, BF), "vb": _sb(512, BF),
+    "uq": _sb(128, CODES), "us": _sb(128, PLANE), "upq": _sb(128, CODES), "ups": _sb(128, PLANE),
+    "vq": _sb(128, CODES), "vs": _sb(128, PLANE), "wq": _sb(512, CODES), "wsc": _sb(512, PLANE),
+    "tab": _sb(3 * NB, F32), "land": _sb(3 * NB, F32),
+    "sa": _sb(C, F32), "sb": _sb(C, F32), "madd": _sb(C, F32), "rst": _sb(C, BF),
+    "ct": _sb(6 * 4 * C, BF), "cq": _sb(6 * C, CODES), "cs": _sb(6 * C, PLANE), "sg": _sb(8 * C, BF),
+    "lt": _sb(C, F32), "wsg": _sb(C, BF), "want": _sb(C, BF), "cc": _sb(C + 4, F32), "cap": _sb(C, BF), "take": _sb(C, BF),
+    "val": _sb(C, F32), "num": _sb(C, F32), "tt": _sb(C, BF), "own": _sb(NB, F32), "m1": _sb(NB, F32), "mc": _sb(NB, F32),
+    "bc": _sb(C, F32), "ab": _sb(2 * C, F32), "c1": _sb(2 * C, BF), "fin": _sb(NB * FS, F32),
+    "pl": _sb(NB, U16), "nm": _sb(C + 16, F32), "nt": _sb(2 * C, F32), "off": _sb(32, U16),
+    "z": _sb(4 * C, BF), "zq": _sb(C, CODES), "zs": _sb(C, PLANE), "z32": _sb(4 * C, BF), "y32": _sb(4 * C, F32),
+    "ysb": _sb(C, F32),
+    "pi": _sb(4, I32), "pj": _sb(4, I32), "pf": _sb(4, F32), "pk": _sb(4, F32), "li": _sb(32, I32), "lu": _sb(32, U16),
+    "sel": _sb(2, U16), "rr": _sb(C, F32), "cg": _sb(512, BF), "kb": _sb(512, BF), "kq": _sb(128, CODES), "ks": _sb(128, PLANE),
+    "one": _sb(516, BF), "fb": _sb(516, BF), "eq": _sb(512, CODES), "es": _sb(512, PLANE),
+    "ps": ("psum", [128, 4096], F32),
+}
+for _t in range(4):
+    SCRATCH["xq%d" % _t] = _sb(C, CODES)
+    SCRATCH["xs%d" % _t] = _sb(C, PLANE)
+for _t in range(3):
+    SCRATCH["lq%d" % _t] = _sb(C, CODES)
+    SCRATCH["ls%d" % _t] = _sb(C, PLANE)
+
+SEMAPHORES = (["cV", "cA", "cP", "cG", "left", "dx", "du", "dv", "dw", "dz", "dod", "dout", "dy"]
+              + ["arrT%d" % t for t in range(3)] + ["arrQ%d" % t for t in range(3)])
+
+
+def rank_program(g, core, T, topo):
+    rank = T.rank_of(core)
+    if rank is None:
+        return
+    A, AF = AluOpType, ActivationFunctionType
+    Q = {"V": g.vector, "A": g.scalar, "P": g.tensor, "G": g, "S": g.sync}
+    know = {q: {} for q in Q}
+    count, wrote, read = {}, {}, {}
+
+    def need(q, deps):
+        top = {}
+        for src, n, snap in deps:
+            if know[q].get(src, 0) < n and top.get(src, (0,))[0] < n:
+                top[src] = (n, snap)
+        for src, (n, snap) in top.items():
+            if know[q].get(src, 0) < n:
+                Q[q].wait_ge(T.sem[src], n)
+                know[q][src] = n
+                for k, x in snap.items():
+                    if know[q].get(k, 0) < x:
+                        know[q][k] = x
+
+    def op(q, call, R, W, sem=None, total=None, group=False):
+        deps = [wrote[k] for k in list(R) + list(W) if k in wrote]
+        for k in W:
+            deps += read.get(k, [])
+        if group:
+            deps = [d for d in deps if d[0] != "cP"]
+        need(q, deps)
+        ins = call()
+        src, step = (sem, 16) if sem else ("c" + q, 1)
+        count[src] = count.get(src, 0) + step
+        ins.then_inc(T.sem[src], step)
+        me = (src, total or count[src], dict(know[q]))
+        for k in R:
+            read.setdefault(k, []).append(me)
+        for k in W:
+            wrote[k] = me
+            read[k] = []
+
+    def bank(k, a=0, b=C):
+        return T.ps[:, 512 * k + a:512 * k + b]
+
+    def ts(out, in0, s1, op0, R, W, s2=None, op1=None):
+        if op1 is None:
+            op("V", lambda: g.vector.tensor_scalar(out, in0, s1, None, op0), R, W)
+        else:
+            op("V", lambda: g.vector.tensor_scalar(out, in0, s1, s2, op0, op1), R, W)
+
+    def tt(out, in0, in1, o, R, W):
+        op("V", lambda: g.vector.tensor_tensor(out, in0, in1, o), R, W)
+
+    def cp(out, in_, R, W):
+        op("V", lambda: g.vector.tensor_copy(out, in_), R, W)
+
+    def fill(ap, x, W):
+        op("V", lambda: g.vector.memset(ap, x), [], W)
+
+    def scan(out, d0, d1, init, op0, op1, R, W):
+        op("V", lambda: g.vector.tensor_tensor_scan(out, d0, d1, init, op0, op1), R, W)
+
+    def turn(out, in_, R, W):
+        op("V", lambda: g.vector.transpose(out, in_), R, W)
+
+    def quant(q, s, in_, R, W):
+        op("V", lambda: g.vector.quantize_mx(q, s, in_), R, W)
+
+    def act(out, in_, f, R, W, **kw):
+        op("A", lambda: g.scalar.activation(out, in_, f, **kw), R, W)
+
+    def mm(k, wq, wsc, xq, xs, R, start=True, stop=True):
+        op("P", lambda: g.tensor.matmul_mx(bank(k), wq, wsc, xq, xs, start, stop), R, ["ps%d" % k], group=not start)
+
+    def iota(out, pat, base, cm, W):
+        op("G", lambda: g.iota(out, pat, base, cm, allow_small_or_imprecise_dtypes=True), [], W)
+
+    def dma(q, out, in_, R, W, sem, total=None):
+        op(q, lambda: Q[q].dma_start(out, in_), R, W, sem, total)
+
+    partners = [T.cores[rank ^ m] for m in MASK]
+    mask = topo.mask(core, partners[0])
+    for p in partners:
+        mask &= topo.mask(core, p)
+    width = len([e for e in topo.engines(core, partners[0]) if mask >> e & 1])
+
+    def send(t, out, in_, R, sem):
+        need("G", [wrote[k] for k in R])
+        rid, pid, _ = topo.addr(partners[t])
+        g.remote_dma(out, in_, T.sem[sem], T.sem.left, pid, rid, mask)
+        count["left"] = count.get("left", 0) + width
+
+    XK = ["x%d" % b for b in range(5)]
+    DK = ["d%d" % b for b in range(4)]
+    ZK = ["z%d" % b for b in range(4)]
+    h = C // 2
+
+    def lo(k):
+        return min(64 * k, C - 128)
+
+    dma("A", T.ub[:], T.u[:], [], ["ub"], "du")
+    dma("S", T.xb[:], T.x[:], [], XK, "dx")
+    iota(T.pi[:], [[0, 4]], 0, 1, ["pi"])
+    iota(T.li[:, 0:8], [[16, 8]], 0, 0, ["li0"])
+    iota(T.rr[:], [[0, NB], [1, 16]], 0, 0, ["rr"])
+    iota(T.li[:, 8:32], [[1, NB]], 0, 0, ["li1"])
+    iota(T.cg[:], [[1, 8], [0, 64]], 0, 0, ["cg"])
+    iota(T.num[:], [[1, C]], 0, 0, ["num"])
+    fill(T.z[:, 0:1024], 0.0, ZK)
+    fill(T.one[:], 1.0, ["one"])
+    for k in range(6):
+        fill(T.ct[:, 4 * C * k + 4 * lo(k):4 * C * k + 4 * (64 * k + 48)], 0.0, ["ct%d.%d" % (k, s) for s in range(4)])
+    quant(T.cq[:, 4 * C:4 * C + 256], T.cs[:, 4 * C:4 * C + 256], T.z[:, 0:1024], ZK, ["c0"])
+    op("G", lambda: g.affine_select(T.fb[:], T.one[:], [[1, 516]], A.is_equal, 0.0, -3, -4), ["one"], ["fb"])
+    for k in (1, 2, 3, 5):
+        dma("S", T.cq[:, C * k:C * k + lo(k)].bitcast(dt.uint8), T.cq[:, 4 * C:4 * C + lo(k)].bitcast(dt.uint8), ["c0"], ["cy%d" % k], "dz", 128)
+        dma("S", T.cs[:, C * k:C * k + lo(k)], T.cs[:, 4 * C:4 * C + lo(k)], ["c0"], ["cz%d" % k], "dz", 128)
+    fill(T.rst[:], 0.0, ["rst"])
+    ts(T.pj[:, 0:1], T.pi[:, 0:1], 15, A.bitwise_and, ["pi"], ["pj0"])
+    ts(T.pj[:, 1:2], T.pi[:, 1:2], 4, A.arith_shift_right, ["pi"], ["pj1"])
+    ts(T.pj[:, 2:3], T.pi[:, 2:3], 16, A.bitwise_and, ["pi"], ["pj2"])
+    ts(T.pj[:, 3:4], T.pi[:, 3:4], 1, A.bitwise_and, ["pi"], ["pj3"])
+    cp(T.lu[:, 0:8], T.li[:, 0:8], ["li0"], ["lu0"])
+    fill(T.rst[:, 0:C:16], -BIG, ["rst"])
+    cp(T.pf[:], T.pj[:], ["pj0", "pj1", "pj2", "pj3"], ["pf"])
+    fill(T.cap[:], float(CAP * C), ["cap"])
+    fill(T.cc[:, 0:4], 0.0, ["cc0"])
+    ts(T.madd[:], T.rr[:], T.pf[:, 0:1], A.not_equal, ["rr", "pf"], ["madd"], -BIG, A.mult)
+    ts(T.pk[:, 0:1], T.pf[:, 3:4], float(C - 16), A.mult, ["pf"], ["pk0"], T.pf[:, 2:3], A.add)
+    ts(T.pk[:, 2:3], T.pf[:, 2:3], -(2.0 ** 23 + 1), A.add, ["pf"], ["pk2"])
+    quant(T.uq[:], T.us[:], T.ub[:], ["ub"], ["uq"])
+    ts(T.pk[:, 1:2], T.pf[:, 0:1], 16.0, A.mult, ["pf", "pk0"], ["pk1"], T.pk[:, 0:1], A.add)
+    op("V", lambda: g.vector.tensor_copy(T.upq[:].bitcast(dt.uint32), T.uq[:].bitcast(dt.uint32).indirect(T.lu[:, 0:8])), ["uq", "lu0"], ["upq"])
+    act(T.ups[:], T.us[:].indirect(T.lu[:, 0:8]), AF.Copy, ["uq", "lu0"], ["ups"])
+    act(T.c1[:, 0:2 * C:2], T.madd[:], AF.Identity, ["madd"], ["c1a"], bias=2.0 ** 36, scale=2.0 ** -60)
+    act(T.c1[:, 1:2 * C:2], T.madd[:], AF.Identity, ["madd"], ["c1b"], bias=-2.0 ** 36, scale=-2.0 ** -60)
+    ts(T.sel[:, 0:1], T.pk[:, 1:2], 1.0, A.add, ["pk1"], ["sel0"])
+    ts(T.sel[:, 1:2], T.pk[:, 1:2], 257.0, A.add, ["pk1"], ["sel1"], float(2 * C - 1), A.min)
+    cp(T.lu[:, 8:32], T.li[:, 8:32], ["li1"], ["lu1"])
+    fill(T.nm[:], 0.0, ["nm"])
+    need("S", [wrote["x0"]])
+    dma("S", T.wq[:].bitcast(dt.uint8), T.wc[:], [], ["wq"], "dw", 32)
+    dma("S", T.wsc[:], T.ws[:], [], ["wsc"], "dw", 32)
+    dma("S", T.vb[:], T.v[:], [], ["vb"], "dv")
+
+    def ct(c):
+        k, s = (c + 1) // 4, (c + 1) % 4
+        return T.ct[:, 4 * C * k + 64 * (c + 1) + s:4 * C * (k + 1):4], "ct%d.%d" % (k, s)
+
+    for t in range(3):
+        xq, xs, lq, ls = T["xq%d" % t], T["xs%d" % t], T["lq%d" % t], T["ls%d" % t]
+        tab, land = T.tab[:, NB * t:NB * (t + 1)], T.land[:, NB * t:NB * (t + 1)]
+        quant(xq[:], xs[:], T.xb[:], XK, ["xq%d" % t])
+        send(t, lq[:, 0:FIRST].bitcast(dt.uint8), xq[:, 0:FIRST].bitcast(dt.uint8), ["xq%d" % t], "arrQ%d" % t)
+        mm(0, T.upq[:], T.ups[:], xq[:], xs[:], ["upq", "ups", "xq%d" % t])
+        mm(2, T.uq[:], T.us[:], xq[:], xs[:], ["uq", "xq%d" % t])
+        mm(1, T.upq[:], T.ups[:], xq[:], xs[:], ["upq", "ups", "xq%d" % t])
+        if t == 0:
+            ts(T.kb[:], T.cg[:], T.pf[:, 1:2], A.is_equal, ["cg", "pf"], ["kb"])
+        act(T.wsg[:], bank(2), AF.Sign, [], ["wsg", "ps2"])
+        act(T.want[:], T.wsg[:], AF.Relu, ["wsg"], ["want"], scale=float(C))
+        tt(T.sa[:], bank(0), T.madd[:], A.add, ["madd"], ["sa", "ps0"])
+        if t == 0:
+            quant(T.kq[:], T.ks[:], T.kb[:], ["kb"], ["kq"])
+        scan(T.sb[:], T.rst[:], T.sa[:], 0.0, A.add, A.max, ["rst", "sa"], ["sb"])
+
+        def sign(c):
+            n = C - 16 * (c + 1)
+            act(T.sg[:, C * c:C * c + n], bank(1, 16 * (c + 1)), AF.Sign, ["sb", "ps1"], ["sg%d" % c], bias=T.sb[:, 16 * c + 15:16 * c + 16], scale=-1.0)
+
+        def atleast(c):
+            n = C - 16 * (c + 1)
+            out, key = ct(c)
+            act(out, T.sg[:, C * c:C * c + n], AF.Sign, ["sg%d" % c], [key], bias=1.0)
+
+        sign(0)
+        for c in range(ACT_BLOCKS):
+            if c + 1 < ACT_BLOCKS:
+                sign(c + 1)
+            atleast(c)
+
+        def compare(c):
+            out, key = ct(c)
+            ts(out, bank(0, 16 * (c + 1)), T.sb[:, 16 * c + 15:16 * c + 16], A.is_le, ["sb", "ps0"], [key])
+
+        done = []
+
+        def tally(k):
+            a, b = C * k + lo(k), C * (k + 1)
+            quant(T.cq[:, a:b], T.cs[:, a:b], T.ct[:, 4 * a:4 * b], ["ct%d.%d" % (k, s) for s in range(4)], ["cq%d" % k])
+            mm(3, T.kq[:], T.ks[:], T.cq[:, C * k:b], T.cs[:, C * k:b], ["kq", "cq%d" % k, "c0", "cz5"], len(done) == 0, len(done) == 5)
+            done.append(k)
+
+        tt(T.ct[:, 0:4 * C:4], bank(0), T.sb[:], A.is_le, ["sb", "ps0"], ["ct0.0"])
+        for c in range(7, 15):
+            compare(c)
+        tally(2)
+        for c in range(15, 19):
+            compare(c)
+        tally(3)
+        for c in range(19, 23):
+            compare(c)
+        tally(0)
+        tally(4)
+        for c in range(ACT_BLOCKS, 7):
+            compare(c)
+        tally(5)
+        tally(1)
+        scan(T.cc[:, 4:C + 4], T.want[:], T.cap[:], 0.0, A.add, A.min, ["want", "cap"], ["cc"])
+        turn(T.lt[:], bank(3), [], ["lt", "ps3"])
+        cp(tab, T.lt[:, 0:C:16], ["lt"], ["tab%d" % t])
+        send(t, land, tab, ["tab%d" % t], "arrT%d" % t)
+        send(t, lq[:, FIRST:C].bitcast(dt.uint8), xq[:, FIRST:C].bitcast(dt.uint8), [], "arrQ%d" % t)
+        send(t, ls[:], xs[:], [], "arrQ%d" % t)
+        wrote["land%d" % t] = ("arrT%d" % t, width, {})
+        wrote["lq%d" % t] = ("arrQ%d" % t, 3 * width, {})
+        tt(T.take[:], T.cc[:, 4:C + 4], T.cc[:, 3:C + 3], A.subtract, ["cc", "cc0"], ["take"])
+        if t == 0:
+            for b in range(4):
+                quant(T.eq[:, 128 * b:128 * b + 128], T.es[:, 128 * b:128 * b + 128], T.fb[:, 3 - b:515 - b], ["fb"], ["e%d" % b])
+        if t == 2:
+            quant(T.vq[:], T.vs[:], T.vb[:], ["vb"], ["vq"])
+        turn(T.tt[:], T.take[:], ["take"], ["tt"])
+        tt(T.val[:], T.take[:], T.num[:], A.add, ["take", "num"], ["val"])
+        tt(T.own[:], tab, T.tt[:, 1:C:16], A.subtract, ["tab%d" % t, "tt"], ["own"])
+        tt(T.m1[:], land, T.tt[:, 1:C:16], A.min, ["land%d" % t, "tt"], ["m1"])
+        tt(T.mc[:], T.m1[:], T.own[:], A.max, ["m1", "own"], ["mc"])
+        act(T.bc[:, h:C], T.mc[:].indirect(T.lu[:, 20:32]), AF.Identity, ["mc", "lu1"], ["bc1"], bias=-0.5, scale=2.0)
+        ts(T.bc[:, 0:h], T.mc[:].indirect(T.lu[:, 8:20]), 2.0, A.mult, ["mc", "lu1"], ["bc0"], -0.5, A.add)
+        turn(T.ab[:, 1:2 * C:2], T.bc[:], ["bc0", "bc1"], ["ab1"])
+        act(T.ab[:, C:2 * C:2], T.ab[:, C + 1:2 * C:2], AF.Identity, ["ab1"], ["ab2"], bias=0.75, scale=-1.0)
+        ts(T.ab[:, 0:C:2], T.ab[:, 1:C:2], -1.0, A.mult, ["ab1"], ["ab0"], 0.75, A.add)
+        for b in range(4):
+            act(T.win[:, 2 * C * b:2 * C * b + C], T.xb[:, b:4 * C:4], AF.Copy, [XK[b], "x4"], ["p%d" % b])
+        for b in range(4):
+            mm(4 + b, T.eq[:, 128 * b:128 * b + 128], T.es[:, 128 * b:128 * b + 128], lq[:], ls[:], ["e%d" % b, "lq%d" % t])
+            act(T.win[:, 2 * C * b + C:2 * C * (b + 1)], bank(4 + b), AF.Copy, [], [DK[b], "ps%d" % (4 + b)])
+        s1 = NB * FS - 2 * C
+        FK = ["fin%d" % c for c in range(NB)]
+        scan(T.fin[:, s1:NB * FS], T.c1[:], T.ab[:], 2.0 ** 24, A.add, A.add, ["c1a", "c1b", "ab0", "ab1", "ab2"], [FK[-1]])
+        for c in range(NB - 1):
+            a, end = 16 * (c + 1), FS * (c + 1)
+            scan(T.fin[:, end - (C - a):end], T.ab[:, 2 * a:2 * C:2], T.ab[:, 2 * a + 1:2 * C:2],
+                 T.fin[:, s1 + 32 * c + 31:s1 + 32 * c + 32], A.add, A.add, [FK[-1], "ab0", "ab1", "ab2"], [FK[c]])
+        ts(T.pl[:], T.fin[:, FS - 1:NB * FS:FS], 0.5, A.mult, FK + ["pk2"], ["pl"], T.pk[:, 2:3], A.add)
+        cp(T.nm[:].indirect(T.pl[:]), T.val[:], ["val", "pl"], ["nm"])
+        turn(T.nt[:, 0:C], T.nm[:, 0:C], ["nm"], ["nt0"])
+        turn(T.nt[:, C:2 * C], T.nm[:, 16:C + 16], ["nm"], ["nt1"])
+        if t == 2:
+            dma("S", T.od[0:8:2, :], T.nm[1:128:32, 0:C], ["nm"], ["od0"], "dod", 32)
+            dma("S", T.od[1:8:2, :], T.nm[17:128:32, 16:C + 16], ["nm"], ["od1"], "dod", 32)
+        cp(T.off[:], T.nt[:].indirect(T.sel[:]), ["nt0", "nt1", "sel0", "sel1"], ["off"])
+        for b in (1, 0, 3, 2):
+            src = T.win[:, 2 * C * b:2 * C * (b + 1)].indirect(T.off[:, 0:NB])
+            if b % 2:
+                act(T.z[:, b:4 * C:4], src, AF.Copy, ["p%d" % b, DK[b], "off"], [ZK[b]])
+            else:
+                cp(T.z[:, b:4 * C:4], src, ["p%d" % b, DK[b], "off"], [ZK[b]])
+        quant(T.zq[:], T.zs[:], T.z[:], ZK, ["zq"])
+        for b in (1, 0):
+            act(T.z32[:, C * b:C * b + C], T.z[:, b:4 * C:4], AF.Copy, [ZK[b]], ["z32%d" % b], scale=32.0)
+        for b in (1, 0, 2, 3):
+            mm(4 + b, T.wq[:, 128 * b:128 * b + 128], T.wsc[:, 128 * b:128 * b + 128], T.zq[:], T.zs[:], ["wq", "wsc", "zq"])
+        for b in (2, 3):
+            ts(T.z32[:, C * b:C * b + C], T.z[:, b:4 * C:4], 32.0, A.mult, [ZK[b]], ["z32%d" % b])
+        for b in (1, 0, 2, 3):
+            tt(T.y32[:, C * b:C * b + C], bank(4 + b), T.z32[:, C * b:C * b + C], A.add, ["z32%d" % b], ["y32%d" % b, "ps%d" % (4 + b)])
+            if b != 3:
+                act(T.xb[:, b:4 * C:4], T.y32[:, C * b:C * b + C], AF.Copy, ["y32%d" % b], [XK[b]], scale=0.03125)
+        act(T.xb[:, 4 * h + 3:4 * C:4], T.y32[:, 3 * C + h:4 * C], AF.Copy, ["y323"], ["x4"], scale=0.03125)
+        ts(T.xb[:, 3:4 * h:4], T.y32[:, 3 * C:3 * C + h], 0.03125, A.mult, ["y323"], [XK[3]])
+
+    quant(T.xq3[:], T.xs3[:], T.xb[:], XK, ["xq3"])
+    mm(0, T.vq[:], T.vs[:], T.xq3[:], T.xs3[:], ["vq", "xq3"])
+    dma("S", T.oc[:], T.xq3[:].bitcast(dt.uint8), ["xq3"], ["oc"], "dout", 80)
+    for k in range(4):
+        dma("A" if k < 2 else "S", T.osc[4 * k:4 * k + 4, :], T.xs3[32 * k:32 * k + 4, :], ["xq3"], ["osc%d" % k], "dout", 80)
+    cp(T.ysb[:], bank(0), [], ["ysb", "ps0"])
+    dma("A", T.y[:], T.ysb[:], ["ysb"], ["y"], "dy")
+    for name in count:
+        g.wait_ge(T.sem[name], count[name])

@@ -6,8 +6,7 @@ FS = 784
 BIG = 2.0 ** 96
 CODES, PLANE = "float8_e4m3fn_x4", "uint8"
 F32, BF, U16, I32 = "float32", "bfloat16", "uint16", "int32"
-ACT_BLOCKS = 6
-FIRST = 256
+ACT_BLOCKS = 7
 
 
 def _sb(n, d):
@@ -18,15 +17,15 @@ SCRATCH = {
     "win": _sb(8 * C, BF), "xb": _sb(4 * C, BF), "ub": _sb(512, BF), "vb": _sb(512, BF),
     "uq": _sb(128, CODES), "us": _sb(128, PLANE), "upq": _sb(128, CODES), "ups": _sb(128, PLANE),
     "vq": _sb(128, CODES), "vs": _sb(128, PLANE), "wq": _sb(512, CODES), "wsc": _sb(512, PLANE),
-    "tab": _sb(3 * NB, F32), "land": _sb(3 * NB, F32),
+    "tab": _sb(6 * NB, F32), "land": _sb(6 * NB, F32),
     "sa": _sb(C, F32), "sb": _sb(C, F32), "madd": _sb(C, F32), "rst": _sb(C, BF),
     "ct": _sb(6 * 4 * C, BF), "cq": _sb(6 * C, CODES), "cs": _sb(6 * C, PLANE), "sg": _sb(8 * C, BF),
-    "lt": _sb(C, F32), "wsg": _sb(C, BF), "want": _sb(C, BF), "cc": _sb(C + 4, F32), "cap": _sb(C, BF), "take": _sb(C, BF),
-    "val": _sb(C, F32), "num": _sb(C, F32), "tt": _sb(C, BF), "own": _sb(NB, F32), "m1": _sb(NB, F32), "mc": _sb(NB, F32),
+    "lt": _sb(C, F32), "want": _sb(C, BF), "cc": _sb(C + 4, F32), "cap": _sb(C, BF), "take": _sb(C, BF),
+    "val": _sb(C, F32), "num": _sb(C, F32), "tt": _sb(C, BF), "own": _sb(2 * NB, F32), "mc": _sb(2 * NB, F32),
     "bc": _sb(C, F32), "ab": _sb(2 * C, F32), "c1": _sb(2 * C, BF), "fin": _sb(NB * FS, F32),
     "pl": _sb(NB, U16), "nm": _sb(C + 16, F32), "nt": _sb(2 * C, F32), "off": _sb(32, U16),
     "z": _sb(4 * C, BF), "zq": _sb(C, CODES), "zs": _sb(C, PLANE), "z32": _sb(4 * C, BF), "y32": _sb(4 * C, F32),
-    "ysb": _sb(C, F32),
+    "ysb": _sb(C, F32), "nil": _sb(512, BF),
     "pi": _sb(4, I32), "pj": _sb(4, I32), "pf": _sb(4, F32), "pk": _sb(4, F32), "li": _sb(32, I32), "lu": _sb(32, U16),
     "sel": _sb(2, U16), "rr": _sb(C, F32), "cg": _sb(512, BF), "kb": _sb(512, BF), "kq": _sb(128, CODES), "ks": _sb(128, PLANE),
     "one": _sb(516, BF), "fb": _sb(516, BF), "eq": _sb(512, CODES), "es": _sb(512, PLANE),
@@ -39,7 +38,7 @@ for _t in range(3):
     SCRATCH["lq%d" % _t] = _sb(C, CODES)
     SCRATCH["ls%d" % _t] = _sb(C, PLANE)
 
-SEMAPHORES = (["cV", "cA", "cP", "cG", "left", "dx", "du", "dv", "dw", "dz", "dod", "dout", "dy"]
+SEMAPHORES = (["cV", "cA", "cP", "cG", "left", "dx", "dx2", "du", "dv", "dw", "dz", "dod", "dout", "dy", "dn", "dval", "dy2", "do2"]
               + ["arrT%d" % t for t in range(3)] + ["arrQ%d" % t for t in range(3)])
 
 
@@ -113,8 +112,8 @@ def rank_program(g, core, T, topo):
     def act(out, in_, f, R, W, **kw):
         op("A", lambda: g.scalar.activation(out, in_, f, **kw), R, W)
 
-    def mm(k, wq, wsc, xq, xs, R, start=True, stop=True):
-        op("P", lambda: g.tensor.matmul_mx(bank(k), wq, wsc, xq, xs, start, stop), R, ["ps%d" % k], group=not start)
+    def mm(k, wq, wsc, xq, xs, R, start=True, stop=True, n=C):
+        op("P", lambda: g.tensor.matmul_mx(bank(k, 0, n), wq, wsc, xq, xs, start, stop), R, ["ps%d" % k], group=not start)
 
     def iota(out, pat, base, cm, W):
         op("G", lambda: g.iota(out, pat, base, cm, allow_small_or_imprecise_dtypes=True), [], W)
@@ -126,7 +125,7 @@ def rank_program(g, core, T, topo):
     mask = topo.mask(core, partners[0])
     for p in partners:
         mask &= topo.mask(core, p)
-    width = len([e for e in topo.engines(core, partners[0]) if mask >> e & 1])
+    width = len([k for k in topo.engines(core, partners[0]) if mask >> k & 1])
 
     def send(t, out, in_, R, sem):
         need("G", [wrote[k] for k in R])
@@ -138,51 +137,43 @@ def rank_program(g, core, T, topo):
     DK = ["d%d" % b for b in range(4)]
     ZK = ["z%d" % b for b in range(4)]
     h = C // 2
+    e = 128
 
     def lo(k):
         return min(64 * k, C - 128)
 
     dma("A", T.ub[:], T.u[:], [], ["ub"], "du")
-    dma("S", T.xb[:], T.x[:], [], XK, "dx")
+    dma("S", T.xb[:, 0:4 * h], T.x[:, 0:4 * h], [], XK[:4], "dx")
+    dma("S", T.xb[:, 4 * h:4 * C], T.x[:, 4 * h:4 * C], [], XK[4:], "dx2")
     iota(T.pi[:], [[0, 4]], 0, 1, ["pi"])
     iota(T.li[:, 0:8], [[16, 8]], 0, 0, ["li0"])
     iota(T.rr[:], [[0, NB], [1, 16]], 0, 0, ["rr"])
-    iota(T.li[:, 8:32], [[1, NB]], 0, 0, ["li1"])
     iota(T.cg[:], [[1, 8], [0, 64]], 0, 0, ["cg"])
-    iota(T.num[:], [[1, C]], 0, 0, ["num"])
-    fill(T.z[:, 0:1024], 0.0, ZK)
-    fill(T.one[:], 1.0, ["one"])
-    for k in range(6):
-        fill(T.ct[:, 4 * C * k + 4 * lo(k):4 * C * k + 4 * (64 * k + 48)], 0.0, ["ct%d.%d" % (k, s) for s in range(4)])
-    quant(T.cq[:, 4 * C:4 * C + 256], T.cs[:, 4 * C:4 * C + 256], T.z[:, 0:1024], ZK, ["c0"])
-    op("G", lambda: g.affine_select(T.fb[:], T.one[:], [[1, 516]], A.is_equal, 0.0, -3, -4), ["one"], ["fb"])
-    for k in (1, 2, 3, 5):
-        dma("S", T.cq[:, C * k:C * k + lo(k)].bitcast(dt.uint8), T.cq[:, 4 * C:4 * C + lo(k)].bitcast(dt.uint8), ["c0"], ["cy%d" % k], "dz", 128)
-        dma("S", T.cs[:, C * k:C * k + lo(k)], T.cs[:, 4 * C:4 * C + lo(k)], ["c0"], ["cz%d" % k], "dz", 128)
-    fill(T.rst[:], 0.0, ["rst"])
+    iota(T.li[:, 8:32], [[2, NB]], 1, 0, ["li1"])
+    fill(T.nil[:], 0.0, ["nil"])
     ts(T.pj[:, 0:1], T.pi[:, 0:1], 15, A.bitwise_and, ["pi"], ["pj0"])
     ts(T.pj[:, 1:2], T.pi[:, 1:2], 4, A.arith_shift_right, ["pi"], ["pj1"])
+    quant(T.cq[:, 2 * C:2 * C + 128], T.cs[:, 2 * C:2 * C + 128], T.nil[:], ["nil"], ["c0"])
     ts(T.pj[:, 2:3], T.pi[:, 2:3], 16, A.bitwise_and, ["pi"], ["pj2"])
     ts(T.pj[:, 3:4], T.pi[:, 3:4], 1, A.bitwise_and, ["pi"], ["pj3"])
+    act(T.rst[:], T.nil[:, 0:C], AF.Copy, ["nil"], ["rst"])
     cp(T.lu[:, 0:8], T.li[:, 0:8], ["li0"], ["lu0"])
-    fill(T.rst[:, 0:C:16], -BIG, ["rst"])
     cp(T.pf[:], T.pj[:], ["pj0", "pj1", "pj2", "pj3"], ["pf"])
-    fill(T.cap[:], float(CAP * C), ["cap"])
-    fill(T.cc[:, 0:4], 0.0, ["cc0"])
+    for k in (3, 4, 5):
+        quant(T.cq[:, C * k:C * k + 128], T.cs[:, C * k:C * k + 128], T.nil[:], ["nil"], ["c0%d" % k])
+    fill(T.rst[:, 0:C:16], -BIG, ["rst"])
     ts(T.madd[:], T.rr[:], T.pf[:, 0:1], A.not_equal, ["rr", "pf"], ["madd"], -BIG, A.mult)
-    ts(T.pk[:, 0:1], T.pf[:, 3:4], float(C - 16), A.mult, ["pf"], ["pk0"], T.pf[:, 2:3], A.add)
-    ts(T.pk[:, 2:3], T.pf[:, 2:3], -(2.0 ** 23 + 1), A.add, ["pf"], ["pk2"])
-    quant(T.uq[:], T.us[:], T.ub[:], ["ub"], ["uq"])
-    ts(T.pk[:, 1:2], T.pf[:, 0:1], 16.0, A.mult, ["pf", "pk0"], ["pk1"], T.pk[:, 0:1], A.add)
-    op("V", lambda: g.vector.tensor_copy(T.upq[:].bitcast(dt.uint32), T.uq[:].bitcast(dt.uint32).indirect(T.lu[:, 0:8])), ["uq", "lu0"], ["upq"])
-    act(T.ups[:], T.us[:].indirect(T.lu[:, 0:8]), AF.Copy, ["uq", "lu0"], ["ups"])
-    act(T.c1[:, 0:2 * C:2], T.madd[:], AF.Identity, ["madd"], ["c1a"], bias=2.0 ** 36, scale=2.0 ** -60)
-    act(T.c1[:, 1:2 * C:2], T.madd[:], AF.Identity, ["madd"], ["c1b"], bias=-2.0 ** 36, scale=-2.0 ** -60)
-    ts(T.sel[:, 0:1], T.pk[:, 1:2], 1.0, A.add, ["pk1"], ["sel0"])
-    ts(T.sel[:, 1:2], T.pk[:, 1:2], 257.0, A.add, ["pk1"], ["sel1"], float(2 * C - 1), A.min)
-    cp(T.lu[:, 8:32], T.li[:, 8:32], ["li1"], ["lu1"])
-    fill(T.nm[:], 0.0, ["nm"])
-    need("S", [wrote["x0"]])
+    for k in range(6):
+        a, b = 4 * lo(k), 4 * (64 * k + 48)
+        act(T.ct[:, 4 * C * k + a:4 * C * k + b], T.nil[:, 0:b - a], AF.Copy, ["nil"], ["ct%d.%d" % (k, s) for s in range(4)])
+        if k == 2:
+            quant(T.uq[:], T.us[:], T.ub[:], ["ub"], ["uq"])
+            op("V", lambda: g.vector.tensor_copy(T.upq[:].bitcast(dt.uint32), T.uq[:].bitcast(dt.uint32).indirect(T.lu[:, 0:8])), ["uq", "lu0"], ["upq"])
+            act(T.ups[:], T.us[:].indirect(T.lu[:, 0:8]), AF.Copy, ["uq", "lu0"], ["ups"])
+    need("S", [wrote["x0"], wrote["x4"]])
+    for k, a, n in ((3, 128, 64), (4, 128, 128), (5, 128, 128), (1, 0, 64)):
+        dma("S", T.cq[:, C * k + a:C * k + a + n].bitcast(dt.uint8), T.cq[:, 2 * C:2 * C + n].bitcast(dt.uint8), ["c0"], ["cy%d" % k], "dz", 128)
+        dma("S", T.cs[:, C * k + a:C * k + a + n], T.cs[:, 2 * C:2 * C + n], ["c0", "c03", "c04", "c05"], ["cz%d" % k], "dz", 128)
     dma("S", T.wq[:].bitcast(dt.uint8), T.wc[:], [], ["wq"], "dw", 32)
     dma("S", T.wsc[:], T.ws[:], [], ["wsc"], "dw", 32)
     dma("S", T.vb[:], T.v[:], [], ["vb"], "dv")
@@ -191,103 +182,130 @@ def rank_program(g, core, T, topo):
         k, s = (c + 1) // 4, (c + 1) % 4
         return T.ct[:, 4 * C * k + 64 * (c + 1) + s:4 * C * (k + 1):4], "ct%d.%d" % (k, s)
 
+    def sign(c):
+        n = C - 16 * (c + 1)
+        act(T.sg[:, C * c:C * c + n], bank(1, 16 * (c + 1)), AF.Sign, ["sb0", "ps1"], ["sg%d" % c], bias=T.sb[:, 16 * c + 15:16 * c + 16], scale=-1.0)
+
+    def atleast(c):
+        n = C - 16 * (c + 1)
+        out, key = ct(c)
+        act(out, T.sg[:, C * c:C * c + n], AF.Sign, ["sg%d" % c], [key], bias=1.0)
+
+    def compare(a, b):
+        for c in range(a, b):
+            out, key = ct(c)
+            ts(out, bank(0, 16 * (c + 1)), T.sb[:, 16 * c + 15:16 * c + 16], A.is_le, ["sb0" if 16 * c < e else "sb", "ps0"], [key])
+
+    def tally(k, first=False, last=False):
+        a, b = C * k + lo(k), C * (k + 1)
+        quant(T.cq[:, a:b], T.cs[:, a:b], T.ct[:, 4 * a:4 * b], ["ct%d.%d" % (k, s) for s in range(4)] + ["cte"], ["cq%d" % k])
+        mm(3, T.kq[:], T.ks[:], T.cq[:, C * k:b], T.cs[:, C * k:b], ["kq", "cq%d" % k, "c0"] + ([] if first else ["cz1"]), first, last)
+
+    def unit(t, b):
+        if t == 0:
+            quant(T.eq[:, 128 * b:128 * b + 128], T.es[:, 128 * b:128 * b + 128], T.fb[:, 3 - b:515 - b], ["fb"], ["e%d" % b])
+
     for t in range(3):
         xq, xs, lq, ls = T["xq%d" % t], T["xs%d" % t], T["lq%d" % t], T["ls%d" % t]
-        tab, land = T.tab[:, NB * t:NB * (t + 1)], T.land[:, NB * t:NB * (t + 1)]
-        quant(xq[:], xs[:], T.xb[:], XK, ["xq%d" % t])
-        send(t, lq[:, 0:FIRST].bitcast(dt.uint8), xq[:, 0:FIRST].bitcast(dt.uint8), ["xq%d" % t], "arrQ%d" % t)
+        t0, t1 = 2 * NB * t, 2 * NB * (t + 1)
+        quant(xq[:, 0:h], xs[:, 0:h], T.xb[:, 0:4 * h], XK[:4], ["xh%d" % t])
+        mm(3, T.upq[:], T.ups[:], xq[:, 0:h], xs[:, 0:h], ["upq", "ups", "xh%d" % t], n=h)
+        send(t, lq[:, 0:h].bitcast(dt.uint8), xq[:, 0:h].bitcast(dt.uint8), ["xh%d" % t], "arrQ%d" % t)
+        quant(xq[:, h:C], xs[:, h:C], T.xb[:, 4 * h:4 * C], XK, ["xq%d" % t])
+        mm(1, T.upq[:], T.ups[:], xq[:], xs[:], ["upq", "ups", "xq%d" % t])
         mm(0, T.upq[:], T.ups[:], xq[:], xs[:], ["upq", "ups", "xq%d" % t])
         mm(2, T.uq[:], T.us[:], xq[:], xs[:], ["uq", "xq%d" % t])
-        mm(1, T.upq[:], T.ups[:], xq[:], xs[:], ["upq", "ups", "xq%d" % t])
+        if t == 0:
+            iota(T.one[:], [[0, 516]], 1, 0, ["one"])
+            op("G", lambda: g.affine_select(T.fb[:], T.one[:], [[1, 516]], A.is_equal, 0.0, -3, -4), ["one"], ["fb"])
+            iota(T.num[:], [[1, C]], 0, 0, ["num"])
+            iota(T.val[:], [[1, C]], 0, 0, ["val"])
+        tt(T.sa[:, 0:e], bank(3, 0, e), T.madd[:, 0:e], A.add, ["madd", "ps3"], ["sa0"])
+        scan(T.sb[:, 0:e], T.rst[:, 0:e], T.sa[:, 0:e], 0.0, A.add, A.max, ["rst", "sa0"], ["sb0"])
         if t == 0:
             ts(T.kb[:], T.cg[:], T.pf[:, 1:2], A.is_equal, ["cg", "pf"], ["kb"])
-        act(T.wsg[:], bank(2), AF.Sign, [], ["wsg", "ps2"])
-        act(T.want[:], T.wsg[:], AF.Relu, ["wsg"], ["want"], scale=float(C))
-        tt(T.sa[:], bank(0), T.madd[:], A.add, ["madd"], ["sa", "ps0"])
+        tt(T.ct[:, 0:4 * e:4], bank(3, 0, e), T.sb[:, 0:e], A.is_le, ["sb0", "ps3"], ["cte"])
+        tt(T.sa[:, e:C], bank(0, e), T.madd[:, e:C], A.add, ["madd", "ps0"], ["sa"])
+        compare(ACT_BLOCKS, 8)
+        scan(T.sb[:, e:C], T.rst[:, e:C], T.sa[:, e:C], 0.0, A.add, A.max, ["rst", "sa"], ["sb"])
         if t == 0:
             quant(T.kq[:], T.ks[:], T.kb[:], ["kb"], ["kq"])
-        scan(T.sb[:], T.rst[:], T.sa[:], 0.0, A.add, A.max, ["rst", "sa"], ["sb"])
-
-        def sign(c):
-            n = C - 16 * (c + 1)
-            act(T.sg[:, C * c:C * c + n], bank(1, 16 * (c + 1)), AF.Sign, ["sb", "ps1"], ["sg%d" % c], bias=T.sb[:, 16 * c + 15:16 * c + 16], scale=-1.0)
-
-        def atleast(c):
-            n = C - 16 * (c + 1)
-            out, key = ct(c)
-            act(out, T.sg[:, C * c:C * c + n], AF.Sign, ["sg%d" % c], [key], bias=1.0)
-
         sign(0)
         for c in range(ACT_BLOCKS):
             if c + 1 < ACT_BLOCKS:
                 sign(c + 1)
             atleast(c)
-
-        def compare(c):
-            out, key = ct(c)
-            ts(out, bank(0, 16 * (c + 1)), T.sb[:, 16 * c + 15:16 * c + 16], A.is_le, ["sb", "ps0"], [key])
-
-        done = []
-
-        def tally(k):
-            a, b = C * k + lo(k), C * (k + 1)
-            quant(T.cq[:, a:b], T.cs[:, a:b], T.ct[:, 4 * a:4 * b], ["ct%d.%d" % (k, s) for s in range(4)], ["cq%d" % k])
-            mm(3, T.kq[:], T.ks[:], T.cq[:, C * k:b], T.cs[:, C * k:b], ["kq", "cq%d" % k, "c0", "cz5"], len(done) == 0, len(done) == 5)
-            done.append(k)
-
-        tt(T.ct[:, 0:4 * C:4], bank(0), T.sb[:], A.is_le, ["sb", "ps0"], ["ct0.0"])
-        for c in range(7, 15):
-            compare(c)
-        tally(2)
-        for c in range(15, 19):
-            compare(c)
+        if t == 0:
+            act(T.tab[:], T.nil[:, 0:6 * NB], AF.Copy, ["nil"], ["tab0", "tab1", "tab2"])
+            act(T.cap[:], T.nil[:, 0:C], AF.Identity, ["nil"], ["cap"], bias=float(CAP * C))
+            act(T.cc[:, 0:4], T.nil[:, 0:4], AF.Copy, ["nil"], ["cc0"])
+            act(T.c1[:, 0:2 * C:2], T.madd[:], AF.Identity, ["madd"], ["c1a"], bias=2.0 ** 36, scale=2.0 ** -60)
+            act(T.c1[:, 1:2 * C:2], T.madd[:], AF.Identity, ["madd"], ["c1b"], bias=-2.0 ** 36, scale=-2.0 ** -60)
+        tt(T.ct[:, 4 * e:4 * C:4], bank(0, e), T.sb[:, e:C], A.is_le, ["sb", "ps0"], ["ct0.0"])
+        compare(8, 15)
+        tally(2, first=True)
+        compare(15, 19)
         tally(3)
-        for c in range(19, 23):
-            compare(c)
         tally(0)
+        compare(19, 23)
         tally(4)
-        for c in range(ACT_BLOCKS, 7):
-            compare(c)
         tally(5)
-        tally(1)
-        scan(T.cc[:, 4:C + 4], T.want[:], T.cap[:], 0.0, A.add, A.min, ["want", "cap"], ["cc"])
+        tally(1, last=True)
+        ts(T.want[:], bank(2), 0.0, A.is_gt, [], ["want", "ps2"], float(C), A.mult)
         turn(T.lt[:], bank(3), [], ["lt", "ps3"])
-        cp(tab, T.lt[:, 0:C:16], ["lt"], ["tab%d" % t])
-        send(t, land, tab, ["tab%d" % t], "arrT%d" % t)
-        send(t, lq[:, FIRST:C].bitcast(dt.uint8), xq[:, FIRST:C].bitcast(dt.uint8), [], "arrQ%d" % t)
+        cp(T.tab[:, t0 + 1:t1:2], T.lt[:, 0:C:16], ["lt"], ["tab%d" % t])
+        send(t, T.land[:, t0:t1], T.tab[:, t0:t1], ["tab%d" % t], "arrT%d" % t)
+        send(t, lq[:, h:C].bitcast(dt.uint8), xq[:, h:C].bitcast(dt.uint8), ["xq%d" % t], "arrQ%d" % t)
         send(t, ls[:], xs[:], [], "arrQ%d" % t)
         wrote["land%d" % t] = ("arrT%d" % t, width, {})
         wrote["lq%d" % t] = ("arrQ%d" % t, 3 * width, {})
+        scan(T.cc[:, 4:C + 4], T.want[:], T.cap[:], 0.0, A.add, A.min, ["want", "cap"], ["cc"])
+        if t == 0:
+            ts(T.pk[:, 0:1], T.pf[:, 3:4], float(C - 16), A.mult, ["pf"], ["pk0"], T.pf[:, 2:3], A.add)
+            ts(T.pk[:, 2:3], T.pf[:, 2:3], -(2.0 ** 23 + 1), A.add, ["pf"], ["pk2"])
         tt(T.take[:], T.cc[:, 4:C + 4], T.cc[:, 3:C + 3], A.subtract, ["cc", "cc0"], ["take"])
         if t == 0:
-            for b in range(4):
-                quant(T.eq[:, 128 * b:128 * b + 128], T.es[:, 128 * b:128 * b + 128], T.fb[:, 3 - b:515 - b], ["fb"], ["e%d" % b])
+            cp(T.lu[:, 8:32], T.li[:, 8:32], ["li1"], ["lu1"])
+            ts(T.pk[:, 1:2], T.pf[:, 0:1], 16.0, A.mult, ["pf", "pk0"], ["pk1"], T.pk[:, 0:1], A.add)
         if t == 2:
             quant(T.vq[:], T.vs[:], T.vb[:], ["vb"], ["vq"])
         turn(T.tt[:], T.take[:], ["take"], ["tt"])
-        tt(T.val[:], T.take[:], T.num[:], A.add, ["take", "num"], ["val"])
-        tt(T.own[:], tab, T.tt[:, 1:C:16], A.subtract, ["tab%d" % t, "tt"], ["own"])
-        tt(T.m1[:], land, T.tt[:, 1:C:16], A.min, ["land%d" % t, "tt"], ["m1"])
-        tt(T.mc[:], T.m1[:], T.own[:], A.max, ["m1", "own"], ["mc"])
+        if t == 0:
+            ts(T.sel[:, 0:1], T.pk[:, 1:2], 1.0, A.add, ["pk1"], ["sel0"])
+            ts(T.sel[:, 1:2], T.pk[:, 1:2], 257.0, A.add, ["pk1"], ["sel1"], float(2 * C - 1), A.min)
+        op("G", lambda: g.dma_start(T.val[1:128:16, :], T.take[1:128:16, :], accum_op=A.add), ["take"], ["val"], "dval")
+        act(T.own[:, 0:2 * NB:2], T.tt[:, 1:C:16], AF.Copy, ["tt"], ["own0"])
+        tt(T.own[:, 1:2 * NB:2], T.tab[:, t0 + 1:t1:2], T.tt[:, 1:C:16], A.subtract, ["tab%d" % t, "tt"], ["own1"])
+        unit(t, 0)
+        scan(T.mc[:], T.land[:, t0:t1], T.own[:], 0.0, A.min, A.max, ["land%d" % t, "own0", "own1"], ["mc"])
+        unit(t, 1)
+        s1 = NB * FS - 2 * C
+        FK = ["fin%d" % c for c in range(NB)]
         act(T.bc[:, h:C], T.mc[:].indirect(T.lu[:, 20:32]), AF.Identity, ["mc", "lu1"], ["bc1"], bias=-0.5, scale=2.0)
         ts(T.bc[:, 0:h], T.mc[:].indirect(T.lu[:, 8:20]), 2.0, A.mult, ["mc", "lu1"], ["bc0"], -0.5, A.add)
-        turn(T.ab[:, 1:2 * C:2], T.bc[:], ["bc0", "bc1"], ["ab1"])
-        act(T.ab[:, C:2 * C:2], T.ab[:, C + 1:2 * C:2], AF.Identity, ["ab1"], ["ab2"], bias=0.75, scale=-1.0)
-        ts(T.ab[:, 0:C:2], T.ab[:, 1:C:2], -1.0, A.mult, ["ab1"], ["ab0"], 0.75, A.add)
+        unit(t, 2)
+        for k in range(2):
+            turn(T.ab[:, C * k + 1:C * (k + 1):2], T.bc[:, h * k:h * (k + 1)], ["bc%d" % k], ["b%d" % k])
+            act(T.ab[:, C * k:C * (k + 1):2], T.ab[:, C * k + 1:C * (k + 1):2], AF.Identity, ["b%d" % k], ["a%d" % k], bias=0.75, scale=-1.0)
+        unit(t, 3)
+        for k in range(2):
+            scan(T.fin[:, s1 + C * k:s1 + C * (k + 1)], T.c1[:, C * k:C * (k + 1)], T.ab[:, C * k:C * (k + 1)], 2.0 ** 24, A.add, A.add,
+                 ["c1a", "c1b", "a%d" % k, "b%d" % k], ["s%d" % k])
+        if t == 0:
+            act(T.nm[:], T.nil[:, 0:C + 16], AF.Copy, ["nil"], ["nm"])
         for b in range(4):
             act(T.win[:, 2 * C * b:2 * C * b + C], T.xb[:, b:4 * C:4], AF.Copy, [XK[b], "x4"], ["p%d" % b])
         for b in range(4):
             mm(4 + b, T.eq[:, 128 * b:128 * b + 128], T.es[:, 128 * b:128 * b + 128], lq[:], ls[:], ["e%d" % b, "lq%d" % t])
             act(T.win[:, 2 * C * b + C:2 * C * (b + 1)], bank(4 + b), AF.Copy, [], [DK[b], "ps%d" % (4 + b)])
-        s1 = NB * FS - 2 * C
-        FK = ["fin%d" % c for c in range(NB)]
-        scan(T.fin[:, s1:NB * FS], T.c1[:], T.ab[:], 2.0 ** 24, A.add, A.add, ["c1a", "c1b", "ab0", "ab1", "ab2"], [FK[-1]])
         for c in range(NB - 1):
             a, end = 16 * (c + 1), FS * (c + 1)
             scan(T.fin[:, end - (C - a):end], T.ab[:, 2 * a:2 * C:2], T.ab[:, 2 * a + 1:2 * C:2],
-                 T.fin[:, s1 + 32 * c + 31:s1 + 32 * c + 32], A.add, A.add, [FK[-1], "ab0", "ab1", "ab2"], [FK[c]])
-        ts(T.pl[:], T.fin[:, FS - 1:NB * FS:FS], 0.5, A.mult, FK + ["pk2"], ["pl"], T.pk[:, 2:3], A.add)
+                 T.fin[:, s1 + 32 * c + 31:s1 + 32 * c + 32], A.add, A.add, ["s%d" % (c // 12), "a0", "a1", "b0", "b1"], [FK[c]])
+        ts(T.pl[:], T.fin[:, FS - 1:NB * FS:FS], 0.5, A.mult, FK + ["pk2", "s1"], ["pl"], T.pk[:, 2:3], A.add)
         cp(T.nm[:].indirect(T.pl[:]), T.val[:], ["val", "pl"], ["nm"])
+        if t < 2:
+            dma("S", T.val[1:128:16, :], T.num[1:128:16, :], ["num"], ["val"], "dn")
         turn(T.nt[:, 0:C], T.nm[:, 0:C], ["nm"], ["nt0"])
         turn(T.nt[:, C:2 * C], T.nm[:, 16:C + 16], ["nm"], ["nt1"])
         if t == 2:
@@ -307,19 +325,43 @@ def rank_program(g, core, T, topo):
             mm(4 + b, T.wq[:, 128 * b:128 * b + 128], T.wsc[:, 128 * b:128 * b + 128], T.zq[:], T.zs[:], ["wq", "wsc", "zq"])
         for b in (2, 3):
             ts(T.z32[:, C * b:C * b + C], T.z[:, b:4 * C:4], 32.0, A.mult, [ZK[b]], ["z32%d" % b])
-        for b in (1, 0, 2, 3):
-            tt(T.y32[:, C * b:C * b + C], bank(4 + b), T.z32[:, C * b:C * b + C], A.add, ["z32%d" % b], ["y32%d" % b, "ps%d" % (4 + b)])
-            if b != 3:
-                act(T.xb[:, b:4 * C:4], T.y32[:, C * b:C * b + C], AF.Copy, ["y32%d" % b], [XK[b]], scale=0.03125)
-        act(T.xb[:, 4 * h + 3:4 * C:4], T.y32[:, 3 * C + h:4 * C], AF.Copy, ["y323"], ["x4"], scale=0.03125)
-        ts(T.xb[:, 3:4 * h:4], T.y32[:, 3 * C:3 * C + h], 0.03125, A.mult, ["y323"], [XK[3]])
+        if t < 2:
+            for b in (1, 0, 2, 3):
+                tt(T.y32[:, C * b:C * b + C], bank(4 + b), T.z32[:, C * b:C * b + C], A.add, ["z32%d" % b], ["y32%d" % b, "ps%d" % (4 + b)])
+                if b != 3:
+                    act(T.xb[:, b:4 * C:4], T.y32[:, C * b:C * b + C], AF.Copy, ["y32%d" % b], [XK[b]], scale=0.03125)
+            act(T.xb[:, 4 * h + 3:4 * C:4], T.y32[:, 3 * C + h:4 * C], AF.Copy, ["y323"], ["x4"], scale=0.03125)
+            ts(T.xb[:, 3:4 * h:4], T.y32[:, 3 * C:3 * C + h], 0.03125, A.mult, ["y323"], [XK[3]])
 
-    quant(T.xq3[:], T.xs3[:], T.xb[:], XK, ["xq3"])
-    mm(0, T.vq[:], T.vs[:], T.xq3[:], T.xs3[:], ["vq", "xq3"])
-    dma("S", T.oc[:], T.xq3[:].bitcast(dt.uint8), ["xq3"], ["oc"], "dout", 80)
+    runs = ((0, 256), (256, C))
+
+    def add(k, b):
+        a, z = runs[k]
+        tt(T.y32[:, C * b + a:C * b + z], bank(4 + b, a, z), T.z32[:, C * b + a:C * b + z], A.add, ["z32%d" % b, "ps%d" % (4 + b)], ["y%d.%d" % (k, b)])
+        if k == 0 or b != 3:
+            act(T.xb[:, 4 * a + b:4 * z:4], T.y32[:, C * b + a:C * b + z], AF.Copy, ["y%d.%d" % (k, b), "p3"], ["f%d.%d" % (k, b)], scale=0.03125)
+        else:
+            ts(T.xb[:, 4 * a + b:4 * z:4], T.y32[:, C * b + a:C * b + z], 0.03125, A.mult, ["y%d.%d" % (k, b), "p3"], ["f%d.%d" % (k, b)])
+
+    def pack(k):
+        a, z = runs[k]
+        quant(T.xq3[:, a:z], T.xs3[:, a:z], T.xb[:, 4 * a:4 * z], ["f%d.%d" % (k, b) for b in range(4)], ["xq3%d" % k])
+        mm(k, T.vq[:], T.vs[:], T.xq3[:, a:z], T.xs3[:, a:z], ["vq", "xq3%d" % k], n=z - a)
+        dma("S", T.oc[:, 4 * a:4 * z], T.xq3[:, a:z].bitcast(dt.uint8), ["xq3%d" % k], ["oc%d" % k], ("do2", "dout")[k], (16, 80)[k])
+
+    for b in (1, 0, 2, 3):
+        add(0, b)
+    add(1, 1)
+    add(1, 0)
+    pack(0)
+    add(1, 2)
+    add(1, 3)
+    act(T.ysb[:, 0:256], bank(0, 0, 256), AF.Copy, [], ["ysb0", "ps0"])
+    dma("A", T.y[:, 0:256], T.ysb[:, 0:256], ["ysb0"], ["y0"], "dy2")
+    pack(1)
+    cp(T.ysb[:, 256:C], bank(1, 0, C - 256), [], ["ysb1", "ps1"])
     for k in range(4):
-        dma("A" if k < 2 else "S", T.osc[4 * k:4 * k + 4, :], T.xs3[32 * k:32 * k + 4, :], ["xq3"], ["osc%d" % k], "dout", 80)
-    cp(T.ysb[:], bank(0), [], ["ysb", "ps0"])
-    dma("A", T.y[:], T.ysb[:], ["ysb"], ["y"], "dy")
+        dma("A" if k < 2 else "S", T.osc[4 * k:4 * k + 4, :], T.xs3[32 * k:32 * k + 4, :], ["xq30", "xq31"], ["osc%d" % k], "dout", 80)
+    dma("A", T.y[:, 256:C], T.ysb[:, 256:C], ["ysb1"], ["y1"], "dy")
     for name in count:
         g.wait_ge(T.sem[name], count[name])

@@ -1,12 +1,17 @@
 from concourse.mybir import dt, AluOpType, ActivationFunctionType
 
 C, CAP, MASK = 384, 160, [1, 2, 4]
-NB = C // 16
-FS = 784
+H = C // 2
+NH = H // 16
+TK = 256
+PL = 1088
+XL, DL, LS, XU, DU = 0, TK, 448, 640, 640 + TK
 BIG = 2.0 ** 96
 CODES, PLANE = "float8_e4m3fn_x4", "uint8"
 F32, BF, U16, I32 = "float32", "bfloat16", "uint16", "int32"
-ACT_BLOCKS = 7
+CT = 4 * 448
+SAME, OTHER, LOCAL, REMOTE = 300.0, 200.0, 2000.0, 1500.0
+URGE = {}
 
 
 def _sb(n, d):
@@ -14,20 +19,21 @@ def _sb(n, d):
 
 
 SCRATCH = {
-    "win": _sb(8 * C, BF), "xb": _sb(4 * C, BF), "ub": _sb(512, BF), "vb": _sb(512, BF),
+    "win": _sb(4 * PL, BF), "xb": _sb(4 * C, BF), "ub": _sb(512, BF), "vb": _sb(512, BF),
     "uq": _sb(128, CODES), "us": _sb(128, PLANE), "upq": _sb(128, CODES), "ups": _sb(128, PLANE),
-    "vq": _sb(128, CODES), "vs": _sb(128, PLANE), "wq": _sb(512, CODES), "wsc": _sb(512, PLANE),
-    "tab": _sb(6 * NB, F32), "land": _sb(6 * NB, F32),
-    "sa": _sb(C, F32), "sb": _sb(C, F32), "madd": _sb(C, F32), "rst": _sb(C, BF),
-    "ct": _sb(6 * 4 * C, BF), "cq": _sb(6 * C, CODES), "cs": _sb(6 * C, PLANE), "sg": _sb(8 * C, BF),
-    "lt": _sb(C, F32), "want": _sb(C, BF), "cc": _sb(C + 4, F32), "cap": _sb(C, BF), "take": _sb(C, BF),
-    "val": _sb(C, F32), "num": _sb(C, F32), "tt": _sb(C, BF), "own": _sb(2 * NB, F32), "mc": _sb(2 * NB, F32),
-    "bc": _sb(C, F32), "ab": _sb(2 * C, F32), "c1": _sb(2 * C, BF), "fin": _sb(NB * FS, F32),
-    "pl": _sb(NB, U16), "nm": _sb(C + 16, F32), "nt": _sb(2 * C, F32), "off": _sb(32, U16),
-    "z": _sb(4 * C, BF), "zq": _sb(C, CODES), "zs": _sb(C, PLANE), "z32": _sb(4 * C, BF), "y32": _sb(4 * C, F32),
-    "ysb": _sb(C, F32), "nil": _sb(512, BF),
-    "pi": _sb(4, I32), "pj": _sb(4, I32), "pf": _sb(4, F32), "pk": _sb(4, F32), "li": _sb(32, I32), "lu": _sb(32, U16),
-    "sel": _sb(2, U16), "rr": _sb(C, F32), "cg": _sb(512, BF), "kb": _sb(512, BF), "kq": _sb(128, CODES), "ks": _sb(128, PLANE),
+    "uwq": _sb(128, CODES), "uws": _sb(128, PLANE), "vq": _sb(128, CODES), "vs": _sb(128, PLANE), "wq": _sb(512, CODES), "wsc": _sb(512, PLANE),
+    "tab": _sb(12 * NH, F32), "land": _sb(12 * NH, F32),
+    "sa": _sb(C, F32), "sb": _sb(C, F32), "madd": _sb(H, F32), "rst": _sb(H, BF),
+    "ct": _sb(2 * CT, BF), "cq": _sb(6 * H, CODES), "cs": _sb(6 * H, PLANE),
+    "sg": _sb(12 * H, BF), "rt": _sb(12 * H, BF), "rq": _sb(3 * H, CODES), "rs": _sb(3 * H, PLANE),
+    "lt": _sb(C, F32), "w1": _sb(C + 2, BF), "w2": _sb(C, BF), "raw": _sb(C, BF), "src": _sb(C, BF), "tt": _sb(C, BF),
+    "own": _sb(4 * NH, F32), "mc": _sb(4 * NH, F32), "bc": _sb(C, F32), "ab": _sb(2 * C, F32), "c1": _sb(C, BF), "fin": _sb(2 * NH * C, F32),
+    "pl": _sb(2 * NH, U16), "nl": _sb(H + 16, BF), "nm": _sb(C + 16, BF), "nu": _sb(C + 16, BF), "pre": _sb(C + 16, BF), "keep": _sb(C + 16, BF),
+    "nt": _sb(3 * C, BF), "pick": _sb(12 * NH, F32), "off": _sb(48, U16),
+    "z": _sb(4 * C, BF), "zq": _sb(C, CODES), "zs": _sb(C, PLANE), "z32": _sb(4 * C, BF),
+    "nw": _sb(1152, F32), "odr": _sb(C, F32), "ysb": _sb(C, F32), "nil": _sb(512, BF),
+    "pi": _sb(8, I32), "pj": _sb(8, I32), "pf": _sb(8, F32), "pk": _sb(16, F32), "li": _sb(32, I32), "lu": _sb(32, U16),
+    "sel": _sb(4, U16), "rr": _sb(H, F32), "cg": _sb(512, BF), "kb": _sb(512, BF), "kq": _sb(128, CODES), "ks": _sb(128, PLANE),
     "one": _sb(516, BF), "fb": _sb(516, BF), "eq": _sb(512, CODES), "es": _sb(512, PLANE),
     "ps": ("psum", [128, 4096], F32),
 }
@@ -38,8 +44,43 @@ for _t in range(3):
     SCRATCH["lq%d" % _t] = _sb(C, CODES)
     SCRATCH["ls%d" % _t] = _sb(C, PLANE)
 
-SEMAPHORES = (["cV", "cA", "cP", "cG", "left", "dx", "dx2", "du", "dv", "dw", "dz", "dod", "dout", "dy", "dn", "dval", "dy2", "do2"]
-              + ["arrT%d" % t for t in range(3)] + ["arrQ%d" % t for t in range(3)])
+SEMAPHORES = (["cV", "cA", "cP", "cG", "left", "dx", "dx2", "du", "dv", "dw", "dod", "dout", "dy", "dn", "dy2", "do2"]
+              + ["arr%s%d" % (k, t) for t in range(3) for k in ("T0", "T1", "Q0", "Q1")])
+
+
+def arrange(calls):
+    def gap(a, b):
+        return 0.0 if a["lag"] or (b["group"] and a["q"] == "P") else SAME if a["q"] == b["q"] else OTHER
+
+    for c in calls:
+        c["next"] = []
+    for c in calls:
+        for d in c["deps"]:
+            d["next"].append(c)
+
+    def sweep(before, after, way, back):
+        free, order, left, at, end = {}, [], {c["n"]: len(c[before]) for c in calls}, {}, {}
+        ready = [c for c in calls if not c[before]]
+        for c in ready:
+            at[c["n"]] = c["lag"] if back else 0.0
+        while ready:
+            c = min(ready, key=lambda c: (int(max(at[c["n"]], free.get(c["q"], 0.0))), -way[c["n"]]))
+            ready.remove(c)
+            order.append(c)
+            free[c["q"]] = max(at[c["n"]], free.get(c["q"], 0.0)) + c["cost"]
+            end[c["n"]] = free[c["q"]] + (0.0 if back else c["lag"])
+            for n in c[after]:
+                left[n["n"]] -= 1
+                if not left[n["n"]]:
+                    at[n["n"]] = max(end[d["n"]] + (gap(n, d) + n["lag"] if back else gap(d, n)) for d in n[before])
+                    ready.append(n)
+        return order, end
+
+    way = {}
+    for c in reversed(calls):
+        way[c["n"]] = c["cost"] + c["lag"] + max([gap(c, n) + way[n["n"]] for n in c["next"]] + [0.0])
+    way = sweep("next", "deps", sweep("deps", "next", way, False)[1], True)[1]
+    return sweep("deps", "next", {c["n"]: way[c["n"]] + URGE.get(c["tag"], 0) for c in calls}, False)[0]
 
 
 def rank_program(g, core, T, topo):
@@ -48,78 +89,66 @@ def rank_program(g, core, T, topo):
         return
     A, AF = AluOpType, ActivationFunctionType
     Q = {"V": g.vector, "A": g.scalar, "P": g.tensor, "G": g, "S": g.sync}
-    know = {q: {} for q in Q}
-    count, wrote, read = {}, {}, {}
+    calls, wrote, read, stage = [], {}, {}, ["start"]
 
-    def need(q, deps):
-        top = {}
-        for src, n, snap in deps:
-            if know[q].get(src, 0) < n and top.get(src, (0,))[0] < n:
-                top[src] = (n, snap)
-        for src, (n, snap) in top.items():
-            if know[q].get(src, 0) < n:
-                Q[q].wait_ge(T.sem[src], n)
-                know[q][src] = n
-                for k, x in snap.items():
-                    if know[q].get(k, 0) < x:
-                        know[q][k] = x
-
-    def op(q, call, R, W, sem=None, total=None, group=False):
+    def op(q, call, R, W, cost, lag=0.0, sem=None, total=None, group=False, far=False):
         deps = [wrote[k] for k in list(R) + list(W) if k in wrote]
         for k in W:
             deps += read.get(k, [])
-        if group:
-            deps = [d for d in deps if d[0] != "cP"]
-        need(q, deps)
-        ins = call()
-        src, step = (sem, 16) if sem else ("c" + q, 1)
-        count[src] = count.get(src, 0) + step
-        ins.then_inc(T.sem[src], step)
-        me = (src, total or count[src], dict(know[q]))
+        me = {"q": q, "call": call, "cost": cost, "lag": lag, "sem": sem, "total": total, "group": group, "far": far, "n": len(calls),
+              "tag": W[0].rstrip("0123456789.") + ":" + stage[0]}
+        me["deps"] = list({d["n"]: d for d in deps}.values())
+        calls.append(me)
         for k in R:
             read.setdefault(k, []).append(me)
         for k in W:
             wrote[k] = me
             read[k] = []
 
-    def bank(k, a=0, b=C):
+    def cyc(n):
+        return 0.83 * max(64, n)
+
+    def picked(n):
+        return 60 + 1.25 * n
+
+    def bank(k, a=0, b=H):
         return T.ps[:, 512 * k + a:512 * k + b]
 
-    def ts(out, in0, s1, op0, R, W, s2=None, op1=None):
+    def ts(out, in0, s1, op0, R, W, s2=None, op1=None, c=53.0):
         if op1 is None:
-            op("V", lambda: g.vector.tensor_scalar(out, in0, s1, None, op0), R, W)
+            op("V", lambda: g.vector.tensor_scalar(out, in0, s1, None, op0), R, W, c)
         else:
-            op("V", lambda: g.vector.tensor_scalar(out, in0, s1, s2, op0, op1), R, W)
+            op("V", lambda: g.vector.tensor_scalar(out, in0, s1, s2, op0, op1), R, W, c)
 
-    def tt(out, in0, in1, o, R, W):
-        op("V", lambda: g.vector.tensor_tensor(out, in0, in1, o), R, W)
+    def tt(out, in0, in1, o, R, W, c=53.0):
+        op("V", lambda: g.vector.tensor_tensor(out, in0, in1, o), R, W, c)
 
-    def cp(out, in_, R, W):
-        op("V", lambda: g.vector.tensor_copy(out, in_), R, W)
+    def cp(out, in_, R, W, c=53.0):
+        op("V", lambda: g.vector.tensor_copy(out, in_), R, W, c)
 
-    def fill(ap, x, W):
-        op("V", lambda: g.vector.memset(ap, x), [], W)
+    def fill(ap, x, W, c=53.0):
+        op("V", lambda: g.vector.memset(ap, x), [], W, c)
 
-    def scan(out, d0, d1, init, op0, op1, R, W):
-        op("V", lambda: g.vector.tensor_tensor_scan(out, d0, d1, init, op0, op1), R, W)
+    def scan(out, d0, d1, init, op0, op1, R, W, c=53.0):
+        op("V", lambda: g.vector.tensor_tensor_scan(out, d0, d1, init, op0, op1), R, W, c)
 
-    def turn(out, in_, R, W):
-        op("V", lambda: g.vector.transpose(out, in_), R, W)
+    def turn(out, in_, R, W, c):
+        op("V", lambda: g.vector.transpose(out, in_), R, W, c)
 
-    def quant(q, s, in_, R, W):
-        op("V", lambda: g.vector.quantize_mx(q, s, in_), R, W)
+    def quant(q, s, in_, R, W, n):
+        op("V", lambda: g.vector.quantize_mx(q, s, in_), R, W, 12 + 0.88 * n)
 
-    def act(out, in_, f, R, W, **kw):
-        op("A", lambda: g.scalar.activation(out, in_, f, **kw), R, W)
+    def act(out, in_, f, R, W, c, **kw):
+        op("A", lambda: g.scalar.activation(out, in_, f, **kw), R, W, c)
 
-    def mm(k, wq, wsc, xq, xs, R, start=True, stop=True, n=C):
-        op("P", lambda: g.tensor.matmul_mx(bank(k, 0, n), wq, wsc, xq, xs, start, stop), R, ["ps%d" % k], group=not start)
+    def mm(k, wq, wsc, xq, xs, R, start=True, stop=True, n=H):
+        op("P", lambda: g.tensor.matmul_mx(bank(k, 0, n), wq, wsc, xq, xs, start, stop), R, ["ps%d" % k], 0.5 * (n + 16), group=not start)
 
-    def iota(out, pat, base, cm, W):
-        op("G", lambda: g.iota(out, pat, base, cm, allow_small_or_imprecise_dtypes=True), [], W)
+    def iota(out, pat, base, cm, W, n):
+        op("G", lambda: g.iota(out, pat, base, cm, allow_small_or_imprecise_dtypes=True), [], W, 130 + 1.66 * n)
 
     def dma(q, out, in_, R, W, sem, total=None):
-        op(q, lambda: Q[q].dma_start(out, in_), R, W, sem, total)
+        op(q, lambda: Q[q].dma_start(out, in_), R, W, 60.0, LOCAL, sem, total)
 
     partners = [T.cores[rank ^ m] for m in MASK]
     mask = topo.mask(core, partners[0])
@@ -127,241 +156,268 @@ def rank_program(g, core, T, topo):
         mask &= topo.mask(core, p)
     width = len([k for k in topo.engines(core, partners[0]) if mask >> k & 1])
 
-    def send(t, out, in_, R, sem):
-        need("G", [wrote[k] for k in R])
+    def send(t, out, in_, R, W, sem, writes=1, lag=REMOTE):
         rid, pid, _ = topo.addr(partners[t])
-        g.remote_dma(out, in_, T.sem[sem], T.sem.left, pid, rid, mask)
-        count["left"] = count.get("left", 0) + width
+        op("G", lambda: g.remote_dma(out, in_, T.sem[sem], T.sem.left, pid, rid, mask), R, W, 300.0, lag, sem, writes * width, far=True)
 
-    XK = ["x%d" % b for b in range(5)]
-    DK = ["d%d" % b for b in range(4)]
-    ZK = ["z%d" % b for b in range(4)]
-    h = C // 2
-    e = 128
+    def col(k):
+        return T.pk[:, k:k + 1]
 
-    def lo(k):
-        return min(64 * k, C - 128)
+    def pf(k):
+        return T.pf[:, k:k + 1]
+
+    def plane(b, a, n=H):
+        return T.win[:, PL * b + a:PL * b + a + n]
+
+    def keys(name, k):
+        return ["%s%d.%d" % (name, k, b) for b in range(4)]
+
+    def zero(out, n, W):
+        act(out, T.nil[:, 0:n], AF.Copy, ["nil"], W, cyc(n))
+
+    TH, AC, C1, RHO, INI, HI, E3, PRE, KI, PK, S0, S1, PR2, S2, S3, S4 = range(16)
+    tile0 = (0, 4 * H, 4 * H + 512)
 
     dma("A", T.ub[:], T.u[:], [], ["ub"], "du")
-    dma("S", T.xb[:, 0:4 * h], T.x[:, 0:4 * h], [], XK[:4], "dx")
-    dma("S", T.xb[:, 4 * h:4 * C], T.x[:, 4 * h:4 * C], [], XK[4:], "dx2")
-    iota(T.pi[:], [[0, 4]], 0, 1, ["pi"])
-    iota(T.li[:, 0:8], [[16, 8]], 0, 0, ["li0"])
-    iota(T.rr[:], [[0, NB], [1, 16]], 0, 0, ["rr"])
-    iota(T.cg[:], [[1, 8], [0, 64]], 0, 0, ["cg"])
-    iota(T.li[:, 8:32], [[2, NB]], 1, 0, ["li1"])
-    fill(T.nil[:], 0.0, ["nil"])
-    ts(T.pj[:, 0:1], T.pi[:, 0:1], 15, A.bitwise_and, ["pi"], ["pj0"])
+    dma("S", T.xb[:, 0:4 * H], T.x[:, 0:4 * H], [], keys("x", 0) + ["in0"], "dx")
+    dma("S", T.xb[:, 4 * H:4 * C], T.x[:, 4 * H:4 * C], [], keys("x", 1) + ["in1"], "dx2")
+    dma("S", T.wq[:].bitcast(dt.uint8), T.wc[:], ["in0", "in1"], ["wq"], "dw", 32)
+    dma("S", T.wsc[:], T.ws[:], ["in0", "in1"], ["wsc"], "dw", 32)
+    dma("S", T.vb[:], T.v[:], ["in0", "in1"], ["vb"], "dv")
+    iota(T.pi[:], [[0, 8]], 0, 1, ["pi"], 8)
+    iota(T.li[:, 0:8], [[16, 8]], 0, 0, ["li0"], 8)
+    iota(T.rr[:], [[0, NH], [1, 16]], 0, 0, ["rr"], H)
+    iota(T.cg[:], [[1, 8], [0, 64]], 0, 0, ["cg"], 512)
+    iota(T.li[:, 8:20], [[2, NH]], 1, 0, ["li1"], NH)
+    iota(T.nw[:, 0:512], [[C, 2], [1, TK]], 0, 0, ["nw0"], 512)
+    iota(T.nw[:, XU:XU + 512], [[C, 2], [1, TK]], H, 0, ["nw2"], 512)
+    fill(T.nil[:], 0.0, ["nil"], cyc(256))
+    fill(T.one[:], 1.0, ["one"], cyc(258))
+    fill(T.rst[:], 0.0, ["rst"], cyc(96))
+    fill(T.rst[:, 0:H:16], -BIG, ["rst"])
+    fill(T.w1[:, 0:2], 0.0, ["w10"])
+    op("G", lambda: g.affine_select(T.fb[:], T.one[:], [[1, 516]], A.is_equal, 0.0, -3, -4), ["one"], ["fb"], 1030.0)
     ts(T.pj[:, 1:2], T.pi[:, 1:2], 4, A.arith_shift_right, ["pi"], ["pj1"])
-    quant(T.cq[:, 2 * C:2 * C + 128], T.cs[:, 2 * C:2 * C + 128], T.nil[:], ["nil"], ["c0"])
-    ts(T.pj[:, 2:3], T.pi[:, 2:3], 16, A.bitwise_and, ["pi"], ["pj2"])
-    ts(T.pj[:, 3:4], T.pi[:, 3:4], 1, A.bitwise_and, ["pi"], ["pj3"])
-    act(T.rst[:], T.nil[:, 0:C], AF.Copy, ["nil"], ["rst"])
+    for k, bits in ((0, 15), (2, 16), (3, 12), (4, 1)):
+        ts(T.pj[:, k:k + 1], T.pi[:, k:k + 1], bits, A.bitwise_and, ["pi"], ["pj%d" % k])
+    cp(T.pf[:, 0:2], T.pj[:, 0:2], ["pj0", "pj1"], ["pf"])
+    cp(T.pf[:, 2:5], T.pj[:, 2:5], ["pj%d" % k for k in range(2, 5)], ["pg"])
     cp(T.lu[:, 0:8], T.li[:, 0:8], ["li0"], ["lu0"])
-    cp(T.pf[:], T.pj[:], ["pj0", "pj1", "pj2", "pj3"], ["pf"])
-    for k in (3, 4, 5):
-        quant(T.cq[:, C * k:C * k + 128], T.cs[:, C * k:C * k + 128], T.nil[:], ["nil"], ["c0%d" % k])
-    fill(T.rst[:, 0:C:16], -BIG, ["rst"])
-    ts(T.madd[:], T.rr[:], T.pf[:, 0:1], A.not_equal, ["rr", "pf"], ["madd"], -BIG, A.mult)
-    for k in range(6):
-        a, b = 4 * lo(k), 4 * (64 * k + 48)
-        act(T.ct[:, 4 * C * k + a:4 * C * k + b], T.nil[:, 0:b - a], AF.Copy, ["nil"], ["ct%d.%d" % (k, s) for s in range(4)])
-        if k == 2:
-            quant(T.uq[:], T.us[:], T.ub[:], ["ub"], ["uq"])
-            op("V", lambda: g.vector.tensor_copy(T.upq[:].bitcast(dt.uint32), T.uq[:].bitcast(dt.uint32).indirect(T.lu[:, 0:8])), ["uq", "lu0"], ["upq"])
-            act(T.ups[:], T.us[:].indirect(T.lu[:, 0:8]), AF.Copy, ["uq", "lu0"], ["ups"])
-    need("S", [wrote["x0"], wrote["x4"]])
-    for k, a, n in ((3, 128, 64), (4, 128, 128), (5, 128, 128), (1, 0, 64)):
-        dma("S", T.cq[:, C * k + a:C * k + a + n].bitcast(dt.uint8), T.cq[:, 2 * C:2 * C + n].bitcast(dt.uint8), ["c0"], ["cy%d" % k], "dz", 128)
-        dma("S", T.cs[:, C * k + a:C * k + a + n], T.cs[:, 2 * C:2 * C + n], ["c0", "c03", "c04", "c05"], ["cz%d" % k], "dz", 128)
-    dma("S", T.wq[:].bitcast(dt.uint8), T.wc[:], [], ["wq"], "dw", 32)
-    dma("S", T.wsc[:], T.ws[:], [], ["wsc"], "dw", 32)
-    dma("S", T.vb[:], T.v[:], [], ["vb"], "dv")
+    cp(T.lu[:, 8:20], T.li[:, 8:20], ["li1"], ["lu1"])
+    ts(T.madd[:], T.rr[:], pf(0), A.not_equal, ["rr", "pf"], ["madd"], -BIG, A.mult, cyc(H))
+    ts(T.kb[:], T.cg[:], pf(1), A.is_equal, ["cg", "pf"], ["kb"], c=cyc(256))
+    quant(T.kq[:], T.ks[:], T.kb[:], ["kb"], ["kq"], 128)
+    for k in range(2):
+        for j, n in enumerate((192, 192, 448)):
+            zero(T.ct[:, CT * k + tile0[j]:CT * k + tile0[j] + n], n, ["ct%d.%d" % (k, 4 * j + s) for s in range(4)])
+            if j:
+                a = H * (3 * k + j)
+                quant(T.cq[:, a:a + 128], T.cs[:, a:a + 128], T.nil[:], ["nil"], ["cq%d.%d" % (k, j)], 128)
+    zero(T.tab[:], 12 * NH, ["tab%d.%d" % (i, k) for i in range(3) for k in range(2)])
+    zero(T.nl[:], H + 16, ["nl"])
+    for k, a in enumerate((XL + H, XU + H)):
+        for b in range(4):
+            zero(plane(b, a, TK - H), TK - H, ["pad%d.%d" % (k, b)])
+    ts(col(TH), pf(3), 8.0, A.not_equal, ["pg"], ["th"], -BIG, A.mult)
+    ts(col(AC), pf(3), 8.0, A.is_equal, ["pg"], ["ac"], -float(TK * 256), A.mult)
+    ts(col(C1), pf(3), 8.0, A.not_equal, ["pg", "ac"], ["c1c"], col(AC), A.add)
+    ts(col(RHO), col(AC), 255.0 / (TK * 65536.0), A.mult, ["ac"], ["rho"])
+    ts(col(INI), col(AC), ((256 - CAP - 1) * TK - H) / (TK * 256.0), A.mult, ["ac"], ["ini"], -float(H), A.add)
+    ts(col(S0), pf(3), -TK / 4.0, A.mult, ["pg"], ["s0"], 3.0 * TK, A.add)
+    ts(col(S1), pf(3), float(TK), A.mult, ["pg"], ["s1"], -3.0 * TK, A.add)
+    tt(col(HI), col(S0), col(S1), A.min, ["s0", "s1"], ["hi"])
+    ts(col(E3), pf(3), 12.0, A.is_equal, ["pg"], ["e3"])
+    ts(col(PRE), pf(3), TK / 2.0, A.mult, ["pg"], ["pre0"], -3.0 * TK, A.add)
+    ts(col(PR2), col(E3), col(PRE), A.min, ["e3", "pre0"], ["pre1"])
+    ts(col(PK), pf(2), -(2.0 ** 23 + 1), A.add, ["pg"], ["pk"])
+    ts(col(KI), pf(2), -1.0, A.mult, ["pg"], ["ki"], -float(H + 1), A.add)
+    ts(col(S2), pf(4), 2.0 * NH - 2, A.mult, ["pg"], ["s2"], 1.0, A.add)
+    ts(col(S3), pf(0), 2.0, A.mult, ["pf", "s2"], ["s3"], col(S2), A.add)
+    ts(col(S4), col(S3), 4.0 * NH - 3, A.min, ["s3"], ["s4"])
+    ts(T.sel[:, 0:1], pf(2), 0.125, A.mult, ["pg", "s4"], ["sel"], col(S4), A.add)
+    act(T.c1[:, 0:C:2], T.madd[:], AF.Identity, ["madd"], ["c1a"], cyc(H), bias=2.0 ** 36, scale=2.0 ** -60)
+    act(T.c1[:, 1:C:2], T.madd[:], AF.Identity, ["madd"], ["c1b"], cyc(H), bias=-2.0 ** 36, scale=-2.0 ** -60)
+    act(T.keep[:], T.nil[:, 0:C + 16], AF.Identity, ["nil", "e3"], ["keep"], cyc(C + 16), bias=col(E3))
+    act(T.pre[:], T.nil[:, 0:C + 16], AF.Identity, ["nil", "pre1"], ["pre"], cyc(C + 16), bias=col(PR2))
+    for b in range(4):
+        quant(T.eq[:, 128 * b:128 * b + 128], T.es[:, 128 * b:128 * b + 128], T.fb[:, 3 - b:515 - b], ["fb"], ["e%d" % b], 128)
+    quant(T.uq[:], T.us[:], T.ub[:], ["ub"], ["uq"], 128)
+    quant(T.vq[:], T.vs[:], T.vb[:], ["vb"], ["vq"], 128)
+    cp(T.upq[:].bitcast(dt.uint32), T.uq[:].bitcast(dt.uint32).indirect(T.lu[:, 0:8]), ["uq", "lu0"], ["upq"], picked(128))
+    act(T.ups[:], T.us[:].indirect(T.lu[:, 0:8]), AF.Copy, ["uq", "lu0"], ["ups"], picked(128))
+    ts(T.lu[:, 20:28], T.li[:, 0:8], 1.0, A.add, ["li0"], ["lu2"])
+    cp(T.uwq[:].bitcast(dt.uint32), T.uq[:].bitcast(dt.uint32).indirect(T.lu[:, 20:28]), ["uq", "lu2"], ["uwq"], picked(128))
+    act(T.uws[:], T.us[:].indirect(T.lu[:, 20:28]), AF.Copy, ["uq", "lu2"], ["uws"], picked(128))
+    for k in range(2):
+        for b in range(4):
+            act(plane(b, (XL, XU)[k]), T.xb[:, 4 * H * k + b:4 * H * (k + 1):4], AF.Copy, keys("x", k), ["p%d.%d" % (k, b)], cyc(H), scale=32.0)
 
-    def ct(c):
-        k, s = (c + 1) // 4, (c + 1) % 4
-        return T.ct[:, 4 * C * k + 64 * (c + 1) + s:4 * C * (k + 1):4], "ct%d.%d" % (k, s)
+    def score(k, c):
+        return T.sb[:, H * k + 16 * c + 15:H * k + 16 * c + 16]
 
-    def sign(c):
-        n = C - 16 * (c + 1)
-        act(T.sg[:, C * c:C * c + n], bank(1, 16 * (c + 1)), AF.Sign, ["sb0", "ps1"], ["sg%d" % c], bias=T.sb[:, 16 * c + 15:16 * c + 16], scale=-1.0)
+    def pack(t, k):
+        a, b = H * k, H * (k + 1)
+        quant(T["xq%d" % t][:, a:b], T["xs%d" % t][:, a:b], T.xb[:, 4 * a:4 * b], keys("x", k), ["xq%d.%d" % (t, k)], H)
 
-    def atleast(c):
-        n = C - 16 * (c + 1)
-        out, key = ct(c)
-        act(out, T.sg[:, C * c:C * c + n], AF.Sign, ["sg%d" % c], [key], bias=1.0)
+    def triangle(k, first):
+        a, z = H * k, H * (k + 1)
+        tt(T.sa[:, a:z], bank(k), T.madd[:], A.add, ["madd", "ps%d" % k], ["sa%d" % k], cyc(H))
+        scan(T.sb[:, a:z], T.rst[:], T.sa[:, a:z], 0.0, A.add, A.max, ["rst", "sa%d" % k], ["sb%d" % k], cyc(H))
+        tt(T.ct[:, CT * k:CT * k + 4 * H:4], bank(k), T.sb[:, a:z], A.is_le, ["sb%d" % k, "ps%d" % k], ["ct%d.0" % k], cyc(H))
+        for c in range(1, NH):
+            j = c // 4
+            at = CT * k + tile0[j] - (256 if j else 0)
+            ts(T.ct[:, at + 64 * c + c % 4:at + 4 * H:4], bank(k, 16 * c), score(k, c - 1), A.is_le, ["sb%d" % k, "ps%d" % k], ["ct%d.%d" % (k, c)], c=cyc(H - 16 * c))
+        for j in range(3):
+            a, n = H * (3 * k + j), (128 if j else H)
+            quant(T.cq[:, a + H - n:a + H], T.cs[:, a + H - n:a + H], T.ct[:, CT * k + tile0[j]:CT * k + tile0[j] + 4 * n],
+                  ["ct%d.%d" % (k, 4 * j + s) for s in range(4)], ["cq%d.%d" % (k, j)], n)
+            mm(4 + k, T.kq[:], T.ks[:], T.cq[:, a:a + H], T.cs[:, a:a + H], ["kq", "cq%d.%d" % (k, j)], j == 0, first and j == 2)
 
-    def compare(a, b):
-        for c in range(a, b):
-            out, key = ct(c)
-            ts(out, bank(0, 16 * (c + 1)), T.sb[:, 16 * c + 15:16 * c + 16], A.is_le, ["sb0" if 16 * c < e else "sb", "ps0"], [key])
+    def rectangle():
+        for j in range(3):
+            a, z = 4 * H * j, 4 * H * (j + 1)
+            for s in range(4):
+                act(T.sg[:, a + s:z:4], bank(2), AF.Sign, ["sb0", "ps2"], ["sg%d.%d" % (j, s)], cyc(H), bias=score(0, 4 * j + s), scale=-1.0)
+            act(T.rt[:, a:z], T.sg[:, a:z], AF.Sign, keys("sg", j), ["rt%d" % j], cyc(4 * H), bias=1.0)
+            a, z = H * j, H * (j + 1)
+            quant(T.rq[:, a:z], T.rs[:, a:z], T.rt[:, 4 * a:4 * z], ["rt%d" % j], ["rq%d" % j], H)
+            mm(5, T.kq[:], T.ks[:], T.rq[:, a:z], T.rs[:, a:z], ["kq", "rq%d" % j], False, j == 2)
 
-    def tally(k, first=False, last=False):
-        a, b = C * k + lo(k), C * (k + 1)
-        quant(T.cq[:, a:b], T.cs[:, a:b], T.ct[:, 4 * a:4 * b], ["ct%d.%d" % (k, s) for s in range(4)] + ["cte"], ["cq%d" % k])
-        mm(3, T.kq[:], T.ks[:], T.cq[:, C * k:b], T.cs[:, C * k:b], ["kq", "cq%d" % k, "c0"] + ([] if first else ["cz1"]), first, last)
+    def taken():
+        ts(T.w1[:, 2:C + 2], bank(3, 0, C), col(TH), A.is_gt, ["th", "c1c"], ["w1", "ps3"], col(C1), A.mult, cyc(C))
+        ts(T.w2[:], T.w1[:, 2:C + 2], col(RHO), A.mult, ["w1", "rho"], ["w2"], c=cyc(H))
+        scan(T.raw[:], T.w1[:, 1:C + 1], T.w2[:], col(INI), A.add, A.add, ["w1", "w10", "w2", "ini"], ["raw"], cyc(H))
+        ts(T.src[:], T.raw[:], col(TH), A.max, ["raw", "th", "hi"], ["src"], col(HI), A.min, cyc(H))
+        turn(T.tt[:], T.src[:], ["src"], ["tt"], cyc(H))
+        ts(T.own[:, 0:4 * NH:2], T.tt[:, 8:C:16], 2.0, A.mult, ["tt"], ["own"])
 
-    def unit(t, b):
-        if t == 0:
-            quant(T.eq[:, 128 * b:128 * b + 128], T.es[:, 128 * b:128 * b + 128], T.fb[:, 3 - b:515 - b], ["fb"], ["e%d" % b])
+    def table(t, k):
+        a, b = 2 * NH * k, 2 * NH * (2 * t + k)
+        turn(T.lt[:, H * k:H * (k + 1)], bank(4 + k), [], ["lt%d" % k, "ps%d" % (4 + k)], cyc(H))
+        cp(T.tab[:, b + 1:b + 2 * NH:2], T.lt[:, H * k:H * (k + 1):16], ["lt%d" % k], ["tab%d.%d" % (t, k)])
+        send(t, T.land[:, b:b + 2 * NH], T.tab[:, b:b + 2 * NH], ["tab%d.%d" % (t, k)], ["land%d.%d" % (t, k)], "arrT%d%d" % (k, t))
+        tt(T.own[:, a + 1:a + 2 * NH:2], T.lt[:, H * k:H * (k + 1):16], T.own[:, a:a + 2 * NH:2], A.subtract, ["lt%d" % k, "own"], ["own%d" % k])
+
+    def places(t, k):
+        a, b, f = 2 * NH * k, 2 * NH * (2 * t + k), NH * C * k
+        scan(T.mc[:, a:a + 2 * NH], T.land[:, b:b + 2 * NH], T.own[:, a:a + 2 * NH], 0.0, A.min, A.max, ["land%d.%d" % (t, k), "own", "own%d" % k], ["mc%d" % k])
+        act(T.bc[:, H * k:H * (k + 1)], T.mc[:, a:a + 2 * NH].indirect(T.lu[:, 8:20]), AF.Identity, ["mc%d" % k, "lu1"], ["bc%d" % k], picked(H), bias=-0.5, scale=2.0)
+        turn(T.ab[:, C * k + 1:C * (k + 1):2], T.bc[:, H * k:H * (k + 1)], ["bc%d" % k], ["b%d" % k], cyc(H))
+        act(T.ab[:, C * k:C * (k + 1):2], T.ab[:, C * k + 1:C * (k + 1):2], AF.Identity, ["b%d" % k], ["a%d" % k], cyc(H), bias=0.75, scale=-1.0)
+        s1 = f + (NH - 1) * C
+        for j, (a, z) in enumerate(((0, 128), (128, C))):
+            scan(T.fin[:, s1 + a:s1 + z], T.c1[:, a:z], T.ab[:, C * k + a:C * k + z], 2.0 ** 24, A.add, A.add, ["c1a", "c1b", "a%d" % k, "b%d" % k], ["s%d.%d" % (k, j)], cyc(z - a))
+        for c in range(NH - 1):
+            a, end = 16 * (c + 1), f + C * (c + 1)
+            scan(T.fin[:, end - (H - a):end], T.ab[:, C * k + 2 * a:C * (k + 1):2], T.ab[:, C * k + 2 * a + 1:C * (k + 1):2],
+                 T.fin[:, s1 + 32 * c + 31:s1 + 32 * c + 32], A.add, A.add, ["s%d.%d" % (k, c > 3), "a%d" % k, "b%d" % k], ["fin%d.%d" % (k, c)], cyc(H - a))
+        ts(T.pl[:, NH * k:NH * (k + 1)], T.fin[:, f + C - 1:f + NH * C:C], 0.5, A.mult, ["fin%d.%d" % (k, c) for c in range(NH - 1)] + ["pk", "s%d.1" % k], ["pl%d" % k], col(PK), A.add)
+
+    def choose(k, row, a, key):
+        turn(T.nt[:, C * k:C * k + H], row[:, a:a + H], [key], ["nt0.%d" % k], cyc(H // 2))
+        turn(T.nt[:, C * k + H:C * (k + 1)], row[:, a + 16:a + H + 16], [key], ["nt1.%d" % k], cyc(H // 2))
+        a = 4 * NH * k
+        scan(T.pick[:, a:a + 4 * NH], T.nt[:, C * k:C * (k + 1):8], T.nt[:, C * k + 4:C * (k + 1):8], 0.0, A.add, A.max, ["nt0.%d" % k, "nt1.%d" % k], ["pick%d" % k])
+        ts(T.off[:, 16 * k:16 * (k + 1)], T.pick[:, a:a + 4 * NH].indirect(T.sel[:, 0:1]), float(H), A.add, ["pick%d" % k, "sel"], ["off%d" % k], c=picked(16))
+
+    def unpack(t, k):
+        lq, ls = T["lq%d" % t], T["ls%d" % t]
+        for b, bk in enumerate((6, 7, 6, 7)):
+            mm(bk, T.eq[:, 128 * b:128 * b + 128], T.es[:, 128 * b:128 * b + 128], lq[:, H * k:H * (k + 1)], ls[:, H * k:H * (k + 1)], ["e%d" % b, "ls%d" % t, "lq%d.0" % t, "lq%d.%d" % (t, k)])
+            act(plane(b, (DL, DU)[k]), bank(bk), AF.Copy, [], ["d%d.%d" % (k, b), "ps%d" % bk], cyc(H), scale=32.0)
+
+    def scaled(q, out, in_, by, R, W, c):
+        if q == "A":
+            act(out, in_, AF.Copy, R, W, c, scale=by)
+        else:
+            ts(out, in_, by, A.mult, R, W, c=c)
 
     for t in range(3):
         xq, xs, lq, ls = T["xq%d" % t], T["xs%d" % t], T["lq%d" % t], T["ls%d" % t]
-        t0, t1 = 2 * NB * t, 2 * NB * (t + 1)
-        quant(xq[:, 0:h], xs[:, 0:h], T.xb[:, 0:4 * h], XK[:4], ["xh%d" % t])
-        mm(3, T.upq[:], T.ups[:], xq[:, 0:h], xs[:, 0:h], ["upq", "ups", "xh%d" % t], n=h)
-        send(t, lq[:, 0:h].bitcast(dt.uint8), xq[:, 0:h].bitcast(dt.uint8), ["xh%d" % t], "arrQ%d" % t)
-        quant(xq[:, h:C], xs[:, h:C], T.xb[:, 4 * h:4 * C], XK, ["xq%d" % t])
-        mm(1, T.upq[:], T.ups[:], xq[:], xs[:], ["upq", "ups", "xq%d" % t])
-        mm(0, T.upq[:], T.ups[:], xq[:], xs[:], ["upq", "ups", "xq%d" % t])
-        mm(2, T.uq[:], T.us[:], xq[:], xs[:], ["uq", "xq%d" % t])
-        if t == 0:
-            iota(T.one[:], [[0, 516]], 1, 0, ["one"])
-            op("G", lambda: g.affine_select(T.fb[:], T.one[:], [[1, 516]], A.is_equal, 0.0, -3, -4), ["one"], ["fb"])
-            iota(T.num[:], [[1, C]], 0, 0, ["num"])
-            iota(T.val[:], [[1, C]], 0, 0, ["val"])
-        tt(T.sa[:, 0:e], bank(3, 0, e), T.madd[:, 0:e], A.add, ["madd", "ps3"], ["sa0"])
-        scan(T.sb[:, 0:e], T.rst[:, 0:e], T.sa[:, 0:e], 0.0, A.add, A.max, ["rst", "sa0"], ["sb0"])
-        if t == 0:
-            ts(T.kb[:], T.cg[:], T.pf[:, 1:2], A.is_equal, ["cg", "pf"], ["kb"])
-        tt(T.ct[:, 0:4 * e:4], bank(3, 0, e), T.sb[:, 0:e], A.is_le, ["sb0", "ps3"], ["cte"])
-        tt(T.sa[:, e:C], bank(0, e), T.madd[:, e:C], A.add, ["madd", "ps0"], ["sa"])
-        compare(ACT_BLOCKS, 8)
-        scan(T.sb[:, e:C], T.rst[:, e:C], T.sa[:, e:C], 0.0, A.add, A.max, ["rst", "sa"], ["sb"])
-        if t == 0:
-            quant(T.kq[:], T.ks[:], T.kb[:], ["kb"], ["kq"])
-        sign(0)
-        for c in range(ACT_BLOCKS):
-            if c + 1 < ACT_BLOCKS:
-                sign(c + 1)
-            atleast(c)
-        if t == 0:
-            act(T.tab[:], T.nil[:, 0:6 * NB], AF.Copy, ["nil"], ["tab0", "tab1", "tab2"])
-            act(T.cap[:], T.nil[:, 0:C], AF.Identity, ["nil"], ["cap"], bias=float(CAP * C))
-            act(T.cc[:, 0:4], T.nil[:, 0:4], AF.Copy, ["nil"], ["cc0"])
-            act(T.c1[:, 0:2 * C:2], T.madd[:], AF.Identity, ["madd"], ["c1a"], bias=2.0 ** 36, scale=2.0 ** -60)
-            act(T.c1[:, 1:2 * C:2], T.madd[:], AF.Identity, ["madd"], ["c1b"], bias=-2.0 ** 36, scale=-2.0 ** -60)
-        tt(T.ct[:, 4 * e:4 * C:4], bank(0, e), T.sb[:, e:C], A.is_le, ["sb", "ps0"], ["ct0.0"])
-        compare(8, 15)
-        tally(2, first=True)
-        compare(15, 19)
-        tally(3)
-        tally(0)
-        compare(19, 23)
-        tally(4)
-        tally(5)
-        tally(1, last=True)
-        ts(T.want[:], bank(2), 0.0, A.is_gt, [], ["want", "ps2"], float(C), A.mult)
-        turn(T.lt[:], bank(3), [], ["lt", "ps3"])
-        cp(T.tab[:, t0 + 1:t1:2], T.lt[:, 0:C:16], ["lt"], ["tab%d" % t])
-        send(t, T.land[:, t0:t1], T.tab[:, t0:t1], ["tab%d" % t], "arrT%d" % t)
-        send(t, lq[:, h:C].bitcast(dt.uint8), xq[:, h:C].bitcast(dt.uint8), ["xq%d" % t], "arrQ%d" % t)
-        send(t, ls[:], xs[:], [], "arrQ%d" % t)
-        wrote["land%d" % t] = ("arrT%d" % t, width, {})
-        wrote["lq%d" % t] = ("arrQ%d" % t, 3 * width, {})
-        scan(T.cc[:, 4:C + 4], T.want[:], T.cap[:], 0.0, A.add, A.min, ["want", "cap"], ["cc"])
-        if t == 0:
-            ts(T.pk[:, 0:1], T.pf[:, 3:4], float(C - 16), A.mult, ["pf"], ["pk0"], T.pf[:, 2:3], A.add)
-            ts(T.pk[:, 2:3], T.pf[:, 2:3], -(2.0 ** 23 + 1), A.add, ["pf"], ["pk2"])
-        tt(T.take[:], T.cc[:, 4:C + 4], T.cc[:, 3:C + 3], A.subtract, ["cc", "cc0"], ["take"])
-        if t == 0:
-            cp(T.lu[:, 8:32], T.li[:, 8:32], ["li1"], ["lu1"])
-            ts(T.pk[:, 1:2], T.pf[:, 0:1], 16.0, A.mult, ["pf", "pk0"], ["pk1"], T.pk[:, 0:1], A.add)
-        if t == 2:
-            quant(T.vq[:], T.vs[:], T.vb[:], ["vb"], ["vq"])
-        turn(T.tt[:], T.take[:], ["take"], ["tt"])
-        if t == 0:
-            ts(T.sel[:, 0:1], T.pk[:, 1:2], 1.0, A.add, ["pk1"], ["sel0"])
-            ts(T.sel[:, 1:2], T.pk[:, 1:2], 257.0, A.add, ["pk1"], ["sel1"], float(2 * C - 1), A.min)
-        op("G", lambda: g.dma_start(T.val[1:128:16, :], T.take[1:128:16, :], accum_op=A.add), ["take"], ["val"], "dval")
-        act(T.own[:, 0:2 * NB:2], T.tt[:, 1:C:16], AF.Copy, ["tt"], ["own0"])
-        tt(T.own[:, 1:2 * NB:2], T.tab[:, t0 + 1:t1:2], T.tt[:, 1:C:16], A.subtract, ["tab%d" % t, "tt"], ["own1"])
-        unit(t, 0)
-        scan(T.mc[:], T.land[:, t0:t1], T.own[:], 0.0, A.min, A.max, ["land%d" % t, "own0", "own1"], ["mc"])
-        unit(t, 1)
-        s1 = NB * FS - 2 * C
-        FK = ["fin%d" % c for c in range(NB)]
-        act(T.bc[:, h:C], T.mc[:].indirect(T.lu[:, 20:32]), AF.Identity, ["mc", "lu1"], ["bc1"], bias=-0.5, scale=2.0)
-        ts(T.bc[:, 0:h], T.mc[:].indirect(T.lu[:, 8:20]), 2.0, A.mult, ["mc", "lu1"], ["bc0"], -0.5, A.add)
-        unit(t, 2)
         for k in range(2):
-            turn(T.ab[:, C * k + 1:C * (k + 1):2], T.bc[:, h * k:h * (k + 1)], ["bc%d" % k], ["b%d" % k])
-            act(T.ab[:, C * k:C * (k + 1):2], T.ab[:, C * k + 1:C * (k + 1):2], AF.Identity, ["b%d" % k], ["a%d" % k], bias=0.75, scale=-1.0)
-        unit(t, 3)
+            stage[0] = "LU"[k]
+            pack(t, k)
+        for k, bk in ((0, 0), (1, 2), (1, 1)):
+            mm(bk, T.upq[:], T.ups[:], xq[:, H * k:H * (k + 1)], xs[:, H * k:H * (k + 1)], ["upq", "ups", "xq%d.%d" % (t, k)])
+        mm(3, T.uwq[:], T.uws[:], xq[:], xs[:], ["uwq", "uws", "xq%d.0" % t, "xq%d.1" % t], n=C)
+        send(t, lq[:, 0:H].bitcast(dt.uint8), xq[:, 0:H].bitcast(dt.uint8), ["xq%d.0" % t], ["lq%d.0" % t], "arrQ0%d" % t, 2, 2 * REMOTE)
+        send(t, ls[:], xs[:], ["xq%d.0" % t, "xq%d.1" % t], ["ls%d" % t], "arrQ0%d" % t, 2, 2 * REMOTE)
+        send(t, lq[:, H:C].bitcast(dt.uint8), xq[:, H:C].bitcast(dt.uint8), ["xq%d.1" % t], ["lq%d.1" % t], "arrQ1%d" % t, 1, 2 * REMOTE)
+        stage[0] = "x"
+        taken()
+        stage[0] = "L"
+        triangle(0, True)
+        table(t, 0)
+        stage[0] = "U"
+        triangle(1, False)
+        rectangle()
+        table(t, 1)
+        stage[0] = "L"
+        places(t, 0)
+        cp(T.nl[:].indirect(T.pl[:, 0:NH]), T.src[:, 0:H], ["src", "pl0"], ["nl"], 50 + 2.5 * H)
+        choose(2, T.nl, 0, "nl")
+        unpack(t, 0)
+        for b in range(4):
+            act(plane(b, LS), plane(b, XL, LS).indirect(T.off[:, 32:32 + NH]), AF.Copy, ["p0.%d" % b, "d0.%d" % b, "pad0.%d" % b, "off2"], ["ls.%d" % b], picked(H))
+        stage[0] = "U"
+        unpack(t, 1)
+        dma("S", T.nm[:], T.pre[:], ["pre"], ["nm"], "dn")
+        places(t, 1)
+        cp(T.nm[:].indirect(T.pl[:, NH:2 * NH]), T.src[:, H:C], ["src", "pl1"], ["nm"], 50 + 2.5 * H)
+        scan(T.nu[:], T.keep[:], T.nm[:], col(KI), A.mult, A.add, ["keep", "nm", "ki"], ["nu"], cyc(H + 8))
         for k in range(2):
-            scan(T.fin[:, s1 + C * k:s1 + C * (k + 1)], T.c1[:, C * k:C * (k + 1)], T.ab[:, C * k:C * (k + 1)], 2.0 ** 24, A.add, A.add,
-                 ["c1a", "c1b", "a%d" % k, "b%d" % k], ["s%d" % k])
-        if t == 0:
-            act(T.nm[:], T.nil[:, 0:C + 16], AF.Copy, ["nil"], ["nm"])
-        for b in range(4):
-            act(T.win[:, 2 * C * b:2 * C * b + C], T.xb[:, b:4 * C:4], AF.Copy, [XK[b], "x4"], ["p%d" % b])
-        for b in range(4):
-            mm(4 + b, T.eq[:, 128 * b:128 * b + 128], T.es[:, 128 * b:128 * b + 128], lq[:], ls[:], ["e%d" % b, "lq%d" % t])
-            act(T.win[:, 2 * C * b + C:2 * C * (b + 1)], bank(4 + b), AF.Copy, [], [DK[b], "ps%d" % (4 + b)])
-        for c in range(NB - 1):
-            a, end = 16 * (c + 1), FS * (c + 1)
-            scan(T.fin[:, end - (C - a):end], T.ab[:, 2 * a:2 * C:2], T.ab[:, 2 * a + 1:2 * C:2],
-                 T.fin[:, s1 + 32 * c + 31:s1 + 32 * c + 32], A.add, A.add, ["s%d" % (c // 12), "a0", "a1", "b0", "b1"], [FK[c]])
-        ts(T.pl[:], T.fin[:, FS - 1:NB * FS:FS], 0.5, A.mult, FK + ["pk2", "s1"], ["pl"], T.pk[:, 2:3], A.add)
-        cp(T.nm[:].indirect(T.pl[:]), T.val[:], ["val", "pl"], ["nm"])
-        if t < 2:
-            dma("S", T.val[1:128:16, :], T.num[1:128:16, :], ["num"], ["val"], "dn")
-        turn(T.nt[:, 0:C], T.nm[:, 0:C], ["nm"], ["nt0"])
-        turn(T.nt[:, C:2 * C], T.nm[:, 16:C + 16], ["nm"], ["nt1"])
-        if t == 2:
-            dma("S", T.od[0:8:2, :], T.nm[1:128:32, 0:C], ["nm"], ["od0"], "dod", 32)
-            dma("S", T.od[1:8:2, :], T.nm[17:128:32, 16:C + 16], ["nm"], ["od1"], "dod", 32)
-        cp(T.off[:], T.nt[:].indirect(T.sel[:]), ["nt0", "nt1", "sel0", "sel1"], ["off"])
-        for b in (1, 0, 3, 2):
-            src = T.win[:, 2 * C * b:2 * C * (b + 1)].indirect(T.off[:, 0:NB])
-            if b % 2:
-                act(T.z[:, b:4 * C:4], src, AF.Copy, ["p%d" % b, DK[b], "off"], [ZK[b]])
-            else:
-                cp(T.z[:, b:4 * C:4], src, ["p%d" % b, DK[b], "off"], [ZK[b]])
-        quant(T.zq[:], T.zs[:], T.z[:], ZK, ["zq"])
-        for b in (1, 0):
-            act(T.z32[:, C * b:C * b + C], T.z[:, b:4 * C:4], AF.Copy, [ZK[b]], ["z32%d" % b], scale=32.0)
-        for b in (1, 0, 2, 3):
-            mm(4 + b, T.wq[:, 128 * b:128 * b + 128], T.wsc[:, 128 * b:128 * b + 128], T.zq[:], T.zs[:], ["wq", "wsc", "zq"])
-        for b in (2, 3):
-            ts(T.z32[:, C * b:C * b + C], T.z[:, b:4 * C:4], 32.0, A.mult, [ZK[b]], ["z32%d" % b])
-        if t < 2:
-            for b in (1, 0, 2, 3):
-                tt(T.y32[:, C * b:C * b + C], bank(4 + b), T.z32[:, C * b:C * b + C], A.add, ["z32%d" % b], ["y32%d" % b, "ps%d" % (4 + b)])
-                if b != 3:
-                    act(T.xb[:, b:4 * C:4], T.y32[:, C * b:C * b + C], AF.Copy, ["y32%d" % b], [XK[b]], scale=0.03125)
-            act(T.xb[:, 4 * h + 3:4 * C:4], T.y32[:, 3 * C + h:4 * C], AF.Copy, ["y323"], ["x4"], scale=0.03125)
-            ts(T.xb[:, 3:4 * h:4], T.y32[:, 3 * C:3 * C + h], 0.03125, A.mult, ["y323"], [XK[3]])
+            stage[0] = "ab"[k]
+            choose(k, T.nu, H * k, "nu")
+        for k in range(2):
+            a, z = H * k, H * (k + 1)
+            stage[0] = "LU"[k]
+            for b in range(4):
+                scaled("VA"[b % 2], T.z[:, 4 * a + b:4 * z:4], plane(b, LS, PL - LS).indirect(T.off[:, 16 * k:16 * k + NH]), 0.03125,
+                       ["ls.%d" % b, "p1.%d" % b, "d1.%d" % b, "pad1.%d" % b, "off%d" % k], ["z%d.%d" % (k, b)], picked(H))
+            quant(T.zq[:, a:z], T.zs[:, a:z], T.z[:, 4 * a:4 * z], keys("z", k), ["zq%d" % k], H)
+            scaled("VA"[k], T.z32[:, 4 * a:4 * z], T.z[:, 4 * a:4 * z], 32.0, keys("z", k), ["z32%d" % k], cyc(2 * H * (k + 1)))
+        for k in range(2):
+            a, z = H * k, H * (k + 1)
+            stage[0] = "LU"[k]
+            for b in range(4):
+                mm(4 * k + b, T.wq[:, 128 * b:128 * b + 128], T.wsc[:, 128 * b:128 * b + 128], T.zq[:, a:z], T.zs[:, a:z], ["wq", "wsc", "zq%d" % k])
+                tt(plane(b, (XL, XU)[k]), bank(4 * k + b), T.z32[:, 4 * a + b:4 * z:4], A.add, ["z32%d" % k, "ps%d" % (4 * k + b)], ["p%d.%d" % (k, b)], cyc(H))
+                q = "V" if k and b > 1 else "A"
+                scaled(q, T.xb[:, 4 * a + b:4 * z:4], plane(b, (XL, XU)[k]), 0.03125, ["p%d.%d" % (k, b)], ["x%d.%d" % (k, b)], cyc(H if q == "A" else H // 2))
 
-    runs = ((0, 256), (256, C))
-
-    def add(k, b):
-        a, z = runs[k]
-        tt(T.y32[:, C * b + a:C * b + z], bank(4 + b, a, z), T.z32[:, C * b + a:C * b + z], A.add, ["z32%d" % b, "ps%d" % (4 + b)], ["y%d.%d" % (k, b)])
-        if k == 0 or b != 3:
-            act(T.xb[:, 4 * a + b:4 * z:4], T.y32[:, C * b + a:C * b + z], AF.Copy, ["y%d.%d" % (k, b), "p3"], ["f%d.%d" % (k, b)], scale=0.03125)
-        else:
-            ts(T.xb[:, 4 * a + b:4 * z:4], T.y32[:, C * b + a:C * b + z], 0.03125, A.mult, ["y%d.%d" % (k, b), "p3"], ["f%d.%d" % (k, b)])
-
-    def pack(k):
-        a, z = runs[k]
-        quant(T.xq3[:, a:z], T.xs3[:, a:z], T.xb[:, 4 * a:4 * z], ["f%d.%d" % (k, b) for b in range(4)], ["xq3%d" % k])
-        mm(k, T.vq[:], T.vs[:], T.xq3[:, a:z], T.xs3[:, a:z], ["vq", "xq3%d" % k], n=z - a)
-        dma("S", T.oc[:, 4 * a:4 * z], T.xq3[:, a:z].bitcast(dt.uint8), ["xq3%d" % k], ["oc%d" % k], ("do2", "dout")[k], (16, 80)[k])
-
-    for b in (1, 0, 2, 3):
-        add(0, b)
-    add(1, 1)
-    add(1, 0)
-    pack(0)
-    add(1, 2)
-    add(1, 3)
-    act(T.ysb[:, 0:256], bank(0, 0, 256), AF.Copy, [], ["ysb0", "ps0"])
-    dma("A", T.y[:, 0:256], T.ysb[:, 0:256], ["ysb0"], ["y0"], "dy2")
-    pack(1)
-    cp(T.ysb[:, 256:C], bank(1, 0, C - 256), [], ["ysb1", "ps1"])
+    stage[0] = "end"
+    act(T.nw[:, LS:LS + H], T.nw[:, 0:LS].indirect(T.off[:, 32:32 + NH]), AF.Copy, ["nw0", "off2"], ["nw1"], picked(H))
+    for k in range(2):
+        act(T.odr[:, H * k:H * (k + 1)], T.nw[:, LS:PL].indirect(T.off[:, 16 * k:16 * k + NH]), AF.Copy, ["nw1", "nw2", "off%d" % k], ["odr%d" % k], picked(H))
+    dma("S", T.od[:], T.odr[0:128:16, :], ["odr0", "odr1"], ["od"], "dod")
+    for k in range(2):
+        a, z = H * k, H * (k + 1)
+        pack(3, k)
+        mm(k, T.vq[:], T.vs[:], T.xq3[:, a:z], T.xs3[:, a:z], ["vq", "xq3.%d" % k])
+        dma("S", T.oc[:, 4 * a:4 * z], T.xq3[:, a:z].bitcast(dt.uint8), ["xq3.%d" % k], ["oc%d" % k], ("do2", "dout")[k], (16, 80)[k])
+        scaled("AV"[k], T.ysb[:, a:z], bank(k), 1.0, [], ["ysb%d" % k, "ps%d" % k], cyc(H))
+        dma("AS"[k], T.y[:, a:z], T.ysb[:, a:z], ["ysb%d" % k], ["y%d" % k], ("dy2", "dy")[k])
     for k in range(4):
-        dma("A" if k < 2 else "S", T.osc[4 * k:4 * k + 4, :], T.xs3[32 * k:32 * k + 4, :], ["xq30", "xq31"], ["osc%d" % k], "dout", 80)
-    dma("A", T.y[:, 256:C], T.ysb[:, 256:C], ["ysb1"], ["y1"], "dy")
+        dma("A" if k < 3 else "S", T.osc[4 * k:4 * k + 4, :], T.xs3[32 * k:32 * k + 4, :], ["xq3.0", "xq3.1"], ["osc%d" % k], "dout", 80)
+
+    know, count = {q: {} for q in Q}, {}
+    for c in arrange(calls):
+        q = c["q"]
+        for src, n, snap in sorted([d["mark"] for d in c["deps"] if not (c["group"] and d["q"] == "P")], key=lambda m: -m[1]):
+            if know[q].get(src, 0) < n:
+                Q[q].wait_ge(T.sem[src], n)
+                know[q][src] = n
+                for k, x in snap.items():
+                    know[q][k] = max(know[q].get(k, 0), x)
+        ins = c["call"]()
+        if c["far"]:
+            count["left"] = count.get("left", 0) + width
+            c["mark"] = (c["sem"], c["total"], {})
+            continue
+        src, step = (c["sem"], 16) if c["sem"] else ("c" + q, 1)
+        count[src] = count.get(src, 0) + step
+        ins.then_inc(T.sem[src], step)
+        c["mark"] = (src, c["total"] or count[src], dict(know[q]))
     for name in count:
         g.wait_ge(T.sem[name], count[name])

@@ -10,8 +10,14 @@ BIG = 2.0 ** 96
 CODES, PLANE = "float8_e4m3fn_x4", "uint8"
 F32, BF, U16, I32 = "float32", "bfloat16", "uint16", "int32"
 CT = 4 * 448
-SAME, OTHER, LOCAL, REMOTE = 300.0, 200.0, 2000.0, 1500.0
-URGE = {}
+SAME, OTHER, LOCAL, REMOTE = 240.0, 250.0, 2000.0, 1700.0
+LONG = 350.0
+TIMES32 = "VVVVAAAA"
+BY32 = "AAAAAAVV"
+SPREAD = "AAAA"
+PARTS = "VAVAVAVA"
+SORTS = "AAAA"
+URGE = {'cq:start': 1000, 'e:start': -3000, 'w:L': 2000, 'lt:L': 1000, 'sx:U': 3000, 'ct:L': 1000, 'cq:L': 3000, 'w:U': -1000, 'sb:U': 1000, 'ct:U': -1000, 'pj:start': 2000, 'ki:start': 2000, 'uwq:start': -2000, 'sa:U': -1000, 'one:start': 500, 'th:start': -3000, 'w:start': -1000, 'cq:U': -2000, 'pg:start': 5000, 'raw:L': -2000, 'src:U': -2000, 'nt:b': -3000, 'sx:L': 1000, 'rst:start': -1000, 'nt:L': -2000, 'p:U': 2000, 'hi:start': -1000, 'fin:U': -500}
 
 
 def _sb(n, d):
@@ -21,18 +27,18 @@ def _sb(n, d):
 SCRATCH = {
     "win": _sb(4 * PL, BF), "xb": _sb(4 * C, BF), "ub": _sb(512, BF), "vb": _sb(512, BF),
     "uq": _sb(128, CODES), "us": _sb(128, PLANE), "upq": _sb(128, CODES), "ups": _sb(128, PLANE),
-    "uwq": _sb(128, CODES), "uws": _sb(128, PLANE), "vq": _sb(128, CODES), "vs": _sb(128, PLANE), "wq": _sb(512, CODES), "wsc": _sb(512, PLANE),
+    "uwq": _sb(136, CODES), "uws": _sb(136, PLANE), "vq": _sb(128, CODES), "vs": _sb(128, PLANE), "wq": _sb(512, CODES), "wsc": _sb(512, PLANE),
     "tab": _sb(12 * NH, F32), "land": _sb(12 * NH, F32),
     "sa": _sb(C, F32), "sb": _sb(C, F32), "madd": _sb(H, F32), "rst": _sb(H, BF),
     "ct": _sb(2 * CT, BF), "cq": _sb(6 * H, CODES), "cs": _sb(6 * H, PLANE),
-    "sg": _sb(12 * H, BF), "rt": _sb(12 * H, BF), "rq": _sb(3 * H, CODES), "rs": _sb(3 * H, PLANE),
-    "lt": _sb(C, F32), "w1": _sb(C + 2, BF), "w2": _sb(C, BF), "raw": _sb(C, BF), "src": _sb(C, BF), "tt": _sb(C, BF),
+    "sg": _sb(12 * H, BF), "rt": _sb(12 * H, BF), "su": _sb(H, F32), "rc": _sb(NH, F32), "ueq": _sb(256, CODES), "ues": _sb(256, PLANE),
+    "lt": _sb(C, F32), "w1": _sb(C + 2, BF), "w0": _sb(C, BF), "w2": _sb(C, BF), "raw": _sb(C, BF), "src": _sb(C, BF), "tt": _sb(C, BF),
     "own": _sb(4 * NH, F32), "mc": _sb(4 * NH, F32), "bc": _sb(C, F32), "ab": _sb(2 * C, F32), "c1": _sb(C, BF), "fin": _sb(2 * NH * C, F32),
     "pl": _sb(2 * NH, U16), "nl": _sb(H + 16, BF), "nm": _sb(C + 16, BF), "nu": _sb(C + 16, BF), "pre": _sb(C + 16, BF), "keep": _sb(C + 16, BF),
     "nt": _sb(3 * C, BF), "pick": _sb(12 * NH, F32), "off": _sb(48, U16),
     "z": _sb(4 * C, BF), "zq": _sb(C, CODES), "zs": _sb(C, PLANE), "z32": _sb(4 * C, BF),
     "nw": _sb(1152, F32), "odr": _sb(C, F32), "ysb": _sb(C, F32), "nil": _sb(512, BF),
-    "pi": _sb(8, I32), "pj": _sb(8, I32), "pf": _sb(8, F32), "pk": _sb(16, F32), "li": _sb(32, I32), "lu": _sb(32, U16),
+    "pi": _sb(8, I32), "pj": _sb(8, I32), "pf": _sb(8, F32), "pk": _sb(16, F32), "li": _sb(32, I32), "lu": _sb(44, U16),
     "sel": _sb(4, U16), "rr": _sb(H, F32), "cg": _sb(512, BF), "kb": _sb(512, BF), "kq": _sb(128, CODES), "ks": _sb(128, PLANE),
     "one": _sb(516, BF), "fb": _sb(516, BF), "eq": _sb(512, CODES), "es": _sb(512, PLANE),
     "ps": ("psum", [128, 4096], F32),
@@ -80,7 +86,7 @@ def arrange(calls):
     for c in reversed(calls):
         way[c["n"]] = c["cost"] + c["lag"] + max([gap(c, n) + way[n["n"]] for n in c["next"]] + [0.0])
     way = sweep("next", "deps", sweep("deps", "next", way, False)[1], True)[1]
-    return sweep("deps", "next", {c["n"]: way[c["n"]] + URGE.get(c["tag"], 0) for c in calls}, False)[0]
+    return sweep("deps", "next", {c["n"]: way[c["n"]] + URGE.get(c["tag"], 0) for c in calls}, False)
 
 
 def rank_program(g, core, T, topo):
@@ -144,11 +150,11 @@ def rank_program(g, core, T, topo):
     def mm(k, wq, wsc, xq, xs, R, start=True, stop=True, n=H):
         op("P", lambda: g.tensor.matmul_mx(bank(k, 0, n), wq, wsc, xq, xs, start, stop), R, ["ps%d" % k], 0.5 * (n + 16), group=not start)
 
-    def iota(out, pat, base, cm, W, n):
-        op("G", lambda: g.iota(out, pat, base, cm, allow_small_or_imprecise_dtypes=True), [], W, 130 + 1.66 * n)
+    def iota(out, pat, base, cm, W, n, R=()):
+        op("G", lambda: g.iota(out, pat, base, cm, allow_small_or_imprecise_dtypes=True), R, W, 130 + 1.66 * n)
 
     def dma(q, out, in_, R, W, sem, total=None):
-        op(q, lambda: Q[q].dma_start(out, in_), R, W, 60.0, LOCAL, sem, total)
+        op(q, lambda: Q[q].dma_start(out, in_), R, W, 60.0, LOCAL * (1.2 if sem in ("dx", "dx2") else 1.0), sem, total)
 
     partners = [T.cores[rank ^ m] for m in MASK]
     mask = topo.mask(core, partners[0])
@@ -175,7 +181,7 @@ def rank_program(g, core, T, topo):
     def zero(out, n, W):
         act(out, T.nil[:, 0:n], AF.Copy, ["nil"], W, cyc(n))
 
-    TH, AC, C1, RHO, INI, HI, E3, PRE, KI, PK, S0, S1, PR2, S2, S3, S4 = range(16)
+    TH, AC, C1, NTH, INI, HI, E3, PRE, KI, PK, S0, S1, PR2, S2, S3, S4 = range(16)
     tile0 = (0, 4 * H, 4 * H + 512)
 
     dma("A", T.ub[:], T.u[:], [], ["ub"], "du")
@@ -185,12 +191,10 @@ def rank_program(g, core, T, topo):
     dma("S", T.wsc[:], T.ws[:], ["in0", "in1"], ["wsc"], "dw", 32)
     dma("S", T.vb[:], T.v[:], ["in0", "in1"], ["vb"], "dv")
     iota(T.pi[:], [[0, 8]], 0, 1, ["pi"], 8)
-    iota(T.li[:, 0:8], [[16, 8]], 0, 0, ["li0"], 8)
+    iota(T.li[:, 0:NH], [[1, NH]], 0, 0, ["li"], NH)
+    iota(T.li[:, 16:32], [[16, 2], [32, 4], [0, 2]], 0, 0, ["lj"], 16)
     iota(T.rr[:], [[0, NH], [1, 16]], 0, 0, ["rr"], H)
     iota(T.cg[:], [[1, 8], [0, 64]], 0, 0, ["cg"], 512)
-    iota(T.li[:, 8:20], [[2, NH]], 1, 0, ["li1"], NH)
-    iota(T.nw[:, 0:512], [[C, 2], [1, TK]], 0, 0, ["nw0"], 512)
-    iota(T.nw[:, XU:XU + 512], [[C, 2], [1, TK]], H, 0, ["nw2"], 512)
     fill(T.nil[:], 0.0, ["nil"], cyc(256))
     fill(T.one[:], 1.0, ["one"], cyc(258))
     fill(T.rst[:], 0.0, ["rst"], cyc(96))
@@ -202,8 +206,9 @@ def rank_program(g, core, T, topo):
         ts(T.pj[:, k:k + 1], T.pi[:, k:k + 1], bits, A.bitwise_and, ["pi"], ["pj%d" % k])
     cp(T.pf[:, 0:2], T.pj[:, 0:2], ["pj0", "pj1"], ["pf"])
     cp(T.pf[:, 2:5], T.pj[:, 2:5], ["pj%d" % k for k in range(2, 5)], ["pg"])
-    cp(T.lu[:, 0:8], T.li[:, 0:8], ["li0"], ["lu0"])
-    cp(T.lu[:, 8:20], T.li[:, 8:20], ["li1"], ["lu1"])
+    ts(T.lu[:, 0:8], T.li[:, 0:8], 16.0, A.mult, ["li"], ["lu0"])
+    ts(T.lu[:, 8:20], T.li[:, 0:NH], 2.0, A.mult, ["li"], ["lu1"], 1.0, A.add)
+    cp(T.lu[:, 28:44], T.li[:, 16:32], ["lj"], ["lu3"])
     ts(T.madd[:], T.rr[:], pf(0), A.not_equal, ["rr", "pf"], ["madd"], -BIG, A.mult, cyc(H))
     ts(T.kb[:], T.cg[:], pf(1), A.is_equal, ["cg", "pf"], ["kb"], c=cyc(256))
     quant(T.kq[:], T.ks[:], T.kb[:], ["kb"], ["kq"], 128)
@@ -219,10 +224,10 @@ def rank_program(g, core, T, topo):
         for b in range(4):
             zero(plane(b, a, TK - H), TK - H, ["pad%d.%d" % (k, b)])
     ts(col(TH), pf(3), 8.0, A.not_equal, ["pg"], ["th"], -BIG, A.mult)
-    ts(col(AC), pf(3), 8.0, A.is_equal, ["pg"], ["ac"], -float(TK * 256), A.mult)
-    ts(col(C1), pf(3), 8.0, A.not_equal, ["pg", "ac"], ["c1c"], col(AC), A.add)
-    ts(col(RHO), col(AC), 255.0 / (TK * 65536.0), A.mult, ["ac"], ["rho"])
-    ts(col(INI), col(AC), ((256 - CAP - 1) * TK - H) / (TK * 256.0), A.mult, ["ac"], ["ini"], -float(H), A.add)
+    ts(col(NTH), pf(3), 8.0, A.not_equal, ["pg"], ["nth"], BIG, A.mult)
+    ts(col(AC), pf(3), 8.0, A.is_equal, ["pg"], ["ac"], float(TK * 256), A.mult)
+    ts(col(C1), col(AC), (255.0 * TK - 1) / (TK * 256.0), A.mult, ["ac"], ["c1c"], 1.0, A.add)
+    ts(col(INI), col(AC), -((256 - CAP - 1) * TK - H - 1) / (TK * 256.0), A.mult, ["ac"], ["ini"], -float(H + 1), A.add)
     ts(col(S0), pf(3), -TK / 4.0, A.mult, ["pg"], ["s0"], 3.0 * TK, A.add)
     ts(col(S1), pf(3), float(TK), A.mult, ["pg"], ["s1"], -3.0 * TK, A.add)
     tt(col(HI), col(S0), col(S1), A.min, ["s0", "s1"], ["hi"])
@@ -242,12 +247,13 @@ def rank_program(g, core, T, topo):
     for b in range(4):
         quant(T.eq[:, 128 * b:128 * b + 128], T.es[:, 128 * b:128 * b + 128], T.fb[:, 3 - b:515 - b], ["fb"], ["e%d" % b], 128)
     quant(T.uq[:], T.us[:], T.ub[:], ["ub"], ["uq"], 128)
+    for a in (0, 8):
+        quant(T.uwq[:, a:a + 128], T.uws[:, a:a + 128], T.ub[:], ["ub"], ["uwq"], 128)
     quant(T.vq[:], T.vs[:], T.vb[:], ["vb"], ["vq"], 128)
     cp(T.upq[:].bitcast(dt.uint32), T.uq[:].bitcast(dt.uint32).indirect(T.lu[:, 0:8]), ["uq", "lu0"], ["upq"], picked(128))
     act(T.ups[:], T.us[:].indirect(T.lu[:, 0:8]), AF.Copy, ["uq", "lu0"], ["ups"], picked(128))
-    ts(T.lu[:, 20:28], T.li[:, 0:8], 1.0, A.add, ["li0"], ["lu2"])
-    cp(T.uwq[:].bitcast(dt.uint32), T.uq[:].bitcast(dt.uint32).indirect(T.lu[:, 20:28]), ["uq", "lu2"], ["uwq"], picked(128))
-    act(T.uws[:], T.us[:].indirect(T.lu[:, 20:28]), AF.Copy, ["uq", "lu2"], ["uws"], picked(128))
+    cp(T.ueq[:].bitcast(dt.uint32), T.uq[:].bitcast(dt.uint32).indirect(T.lu[:, 28:44]), ["uq", "lu3"], ["ueq"], picked(256))
+    act(T.ues[:], T.us[:].indirect(T.lu[:, 28:44]), AF.Copy, ["uq", "lu3"], ["ues"], picked(256))
     for k in range(2):
         for b in range(4):
             act(plane(b, (XL, XU)[k]), T.xb[:, 4 * H * k + b:4 * H * (k + 1):4], AF.Copy, keys("x", k), ["p%d.%d" % (k, b)], cyc(H), scale=32.0)
@@ -272,58 +278,72 @@ def rank_program(g, core, T, topo):
             a, n = H * (3 * k + j), (128 if j else H)
             quant(T.cq[:, a + H - n:a + H], T.cs[:, a + H - n:a + H], T.ct[:, CT * k + tile0[j]:CT * k + tile0[j] + 4 * n],
                   ["ct%d.%d" % (k, 4 * j + s) for s in range(4)], ["cq%d.%d" % (k, j)], n)
-            mm(4 + k, T.kq[:], T.ks[:], T.cq[:, a:a + H], T.cs[:, a:a + H], ["kq", "cq%d.%d" % (k, j)], j == 0, first and j == 2)
+            mm(4 + k, T.kq[:], T.ks[:], T.cq[:, a:a + H], T.cs[:, a:a + H], ["kq", "cq%d.%d" % (k, j)], j == 0, j == 2)
 
     def rectangle():
-        for j in range(3):
-            a, z = 4 * H * j, 4 * H * (j + 1)
-            for s in range(4):
-                act(T.sg[:, a + s:z:4], bank(2), AF.Sign, ["sb0", "ps2"], ["sg%d.%d" % (j, s)], cyc(H), bias=score(0, 4 * j + s), scale=-1.0)
-            act(T.rt[:, a:z], T.sg[:, a:z], AF.Sign, keys("sg", j), ["rt%d" % j], cyc(4 * H), bias=1.0)
-            a, z = H * j, H * (j + 1)
-            quant(T.rq[:, a:z], T.rs[:, a:z], T.rt[:, 4 * a:4 * z], ["rt%d" % j], ["rq%d" % j], H)
-            mm(5, T.kq[:], T.ks[:], T.rq[:, a:z], T.rs[:, a:z], ["kq", "rq%d" % j], False, j == 2)
+        turn(T.su[:], bank(1), ["ps1"], ["su"], cyc(H))
+        for j in range(NH):
+            a, z, bk = H * j, H * (j + 1), (2, 7)[j % 2]
+            act(T.sg[:, a:z], bank(bk), AF.Sign, ["su", "ps%d" % bk], ["sg%d" % j], cyc(H), bias=T.su[:, 16 * j:16 * j + 1], scale=-1.0)
+            act(T.rt[:, a:z], T.sg[:, a:z], AF.Sign, ["sg%d" % j], ["rt%d" % j], cyc(H) + 20, bias=1.0, scale=-1.0, accum_out=T.rc[:, j:j + 1])
 
-    def taken():
-        ts(T.w1[:, 2:C + 2], bank(3, 0, C), col(TH), A.is_gt, ["th", "c1c"], ["w1", "ps3"], col(C1), A.mult, cyc(C))
-        ts(T.w2[:], T.w1[:, 2:C + 2], col(RHO), A.mult, ["w1", "rho"], ["w2"], c=cyc(H))
-        scan(T.raw[:], T.w1[:, 1:C + 1], T.w2[:], col(INI), A.add, A.add, ["w1", "w10", "w2", "ini"], ["raw"], cyc(H))
-        ts(T.src[:], T.raw[:], col(TH), A.max, ["raw", "th", "hi"], ["src"], col(HI), A.min, cyc(H))
-        turn(T.tt[:], T.src[:], ["src"], ["tt"], cyc(H))
-        ts(T.own[:, 0:4 * NH:2], T.tt[:, 8:C:16], 2.0, A.mult, ["tt"], ["own"])
+    def taken(k):
+        a, z, bk = H * k, H * (k + 1), 3 + 3 * k
+        if k == 0:
+            act(T.w0[:, a:z], bank(bk), AF.Sign, ["nth"], ["w0.%d" % k, "ps%d" % bk], cyc(H), bias=col(NTH))
+            act(T.w1[:, a + 2:z + 2], T.w0[:, a:z], AF.Relu, ["w0.%d" % k, "ac"], ["w1.%d" % k], cyc(H), scale=col(AC))
+            act(T.w2[:, a:z], T.w0[:, a:z], AF.Relu, ["w0.%d" % k, "c1c"], ["w2.%d" % k], cyc(H), scale=col(C1))
+        else:
+            ts(T.w0[:, a:z], bank(bk), col(TH), A.is_gt, ["th"], ["w0.%d" % k, "ps%d" % bk], c=cyc(H))
+            ts(T.w1[:, a + 2:z + 2], T.w0[:, a:z], col(AC), A.mult, ["w0.%d" % k, "ac"], ["w1.%d" % k], c=cyc(H // 2))
+            ts(T.w2[:, a:z], T.w0[:, a:z], col(C1), A.mult, ["w0.%d" % k, "c1c"], ["w2.%d" % k], c=cyc(H // 2))
+        scan(T.raw[:, a:z], T.w2[:, a:z], T.w1[:, a + 1:z + 1], T.raw[:, a - 1:a] if k else col(INI), A.add, A.subtract,
+             ["w1.0", "w1.%d" % k, "w10", "w2.%d" % k, "ini"] + ["raw0"] * k, ["raw%d" % k], cyc(H // 2))
+        ts(T.src[:, a:z], T.raw[:, a:z], col(TH), A.max, ["raw%d" % k, "th", "hi"], ["src%d" % k], col(HI), A.min, cyc(H // 2))
+        turn(T.tt[:, a:z], T.src[:, a:z], ["src%d" % k], ["tt%d" % k], cyc(H // 2))
+        ts(T.own[:, 2 * NH * k:2 * NH * (k + 1):2], T.tt[:, a + 9:z:16], 2.0, A.mult, ["tt%d" % k], ["tk%d" % k])
 
     def table(t, k):
         a, b = 2 * NH * k, 2 * NH * (2 * t + k)
         turn(T.lt[:, H * k:H * (k + 1)], bank(4 + k), [], ["lt%d" % k, "ps%d" % (4 + k)], cyc(H))
-        cp(T.tab[:, b + 1:b + 2 * NH:2], T.lt[:, H * k:H * (k + 1):16], ["lt%d" % k], ["tab%d.%d" % (t, k)])
+        if k:
+            tt(T.tab[:, b + 1:b + 2 * NH:2], T.lt[:, H:C:16], T.rc[:], A.add, ["lt1"] + ["rt%d" % j for j in range(NH)], ["tab%d.1" % t])
+        else:
+            cp(T.tab[:, b + 1:b + 2 * NH:2], T.lt[:, 0:H:16], ["lt0"], ["tab%d.0" % t])
         send(t, T.land[:, b:b + 2 * NH], T.tab[:, b:b + 2 * NH], ["tab%d.%d" % (t, k)], ["land%d.%d" % (t, k)], "arrT%d%d" % (k, t))
-        tt(T.own[:, a + 1:a + 2 * NH:2], T.lt[:, H * k:H * (k + 1):16], T.own[:, a:a + 2 * NH:2], A.subtract, ["lt%d" % k, "own"], ["own%d" % k])
+        tt(T.own[:, a + 1:a + 2 * NH:2], T.tab[:, b + 1:b + 2 * NH:2], T.own[:, a:a + 2 * NH:2], A.subtract, ["tab%d.%d" % (t, k), "tk%d" % k], ["own%d" % k])
+
+    def affine(q, out, in_, by, plus, R, W, c):
+        if q == "A":
+            act(out, in_, AF.Identity, R, W, c, bias=plus, scale=by)
+        else:
+            ts(out, in_, by, A.mult, R, W, plus, A.add, c)
 
     def places(t, k):
         a, b, f = 2 * NH * k, 2 * NH * (2 * t + k), NH * C * k
-        scan(T.mc[:, a:a + 2 * NH], T.land[:, b:b + 2 * NH], T.own[:, a:a + 2 * NH], 0.0, A.min, A.max, ["land%d.%d" % (t, k), "own", "own%d" % k], ["mc%d" % k])
-        act(T.bc[:, H * k:H * (k + 1)], T.mc[:, a:a + 2 * NH].indirect(T.lu[:, 8:20]), AF.Identity, ["mc%d" % k, "lu1"], ["bc%d" % k], picked(H), bias=-0.5, scale=2.0)
+        scan(T.mc[:, a:a + 2 * NH], T.land[:, b:b + 2 * NH], T.own[:, a:a + 2 * NH], 0.0, A.min, A.max, ["land%d.%d" % (t, k), "tk%d" % k, "own%d" % k], ["mc%d" % k])
+        affine(SPREAD[k], T.bc[:, H * k:H * (k + 1)], T.mc[:, a:a + 2 * NH].indirect(T.lu[:, 8:20]), 2.0, -0.5, ["mc%d" % k, "lu1"], ["bc%d" % k], picked(H))
         turn(T.ab[:, C * k + 1:C * (k + 1):2], T.bc[:, H * k:H * (k + 1)], ["bc%d" % k], ["b%d" % k], cyc(H))
-        act(T.ab[:, C * k:C * (k + 1):2], T.ab[:, C * k + 1:C * (k + 1):2], AF.Identity, ["b%d" % k], ["a%d" % k], cyc(H), bias=0.75, scale=-1.0)
+        affine(SPREAD[2 + k], T.ab[:, C * k:C * (k + 1):2], T.ab[:, C * k + 1:C * (k + 1):2], -1.0, 0.75, ["b%d" % k], ["a%d" % k], cyc(H))
         s1 = f + (NH - 1) * C
         for j, (a, z) in enumerate(((0, 128), (128, C))):
-            scan(T.fin[:, s1 + a:s1 + z], T.c1[:, a:z], T.ab[:, C * k + a:C * k + z], 2.0 ** 24, A.add, A.add, ["c1a", "c1b", "a%d" % k, "b%d" % k], ["s%d.%d" % (k, j)], cyc(z - a))
+            scan(T.fin[:, s1 + a:s1 + z], T.c1[:, a:z], T.ab[:, C * k + a:C * k + z], 2.0 ** 24, A.add, A.add, ["c1a", "c1b", "a%d" % k, "b%d" % k], [("sx%d", "sy%d")[j] % k], cyc(z - a))
         for c in range(NH - 1):
             a, end = 16 * (c + 1), f + C * (c + 1)
             scan(T.fin[:, end - (H - a):end], T.ab[:, C * k + 2 * a:C * (k + 1):2], T.ab[:, C * k + 2 * a + 1:C * (k + 1):2],
-                 T.fin[:, s1 + 32 * c + 31:s1 + 32 * c + 32], A.add, A.add, ["s%d.%d" % (k, c > 3), "a%d" % k, "b%d" % k], ["fin%d.%d" % (k, c)], cyc(H - a))
-        ts(T.pl[:, NH * k:NH * (k + 1)], T.fin[:, f + C - 1:f + NH * C:C], 0.5, A.mult, ["fin%d.%d" % (k, c) for c in range(NH - 1)] + ["pk", "s%d.1" % k], ["pl%d" % k], col(PK), A.add)
+                 T.fin[:, s1 + 32 * c + 31:s1 + 32 * c + 32], A.add, A.add, [("sx%d", "sy%d")[c > 3] % k, "a%d" % k, "b%d" % k], ["fin%d.%d" % (k, c)], cyc(H - a))
+        ts(T.pl[:, NH * k:NH * (k + 1)], T.fin[:, f + C - 1:f + NH * C:C], 0.5, A.mult, ["fin%d.%d" % (k, c) for c in range(NH - 1)] + ["pk", "sy%d" % k], ["pl%d" % k], col(PK), A.add)
 
     def choose(k, row, a, key):
         turn(T.nt[:, C * k:C * k + H], row[:, a:a + H], [key], ["nt0.%d" % k], cyc(H // 2))
         turn(T.nt[:, C * k + H:C * (k + 1)], row[:, a + 16:a + H + 16], [key], ["nt1.%d" % k], cyc(H // 2))
         a = 4 * NH * k
-        scan(T.pick[:, a:a + 4 * NH], T.nt[:, C * k:C * (k + 1):8], T.nt[:, C * k + 4:C * (k + 1):8], 0.0, A.add, A.max, ["nt0.%d" % k, "nt1.%d" % k], ["pick%d" % k])
+        scan(T.pick[:, a:a + 4 * NH], T.nt[:, C * k + 1:C * (k + 1):8], T.nt[:, C * k + 5:C * (k + 1):8], 0.0, A.add, A.max, ["nt0.%d" % k, "nt1.%d" % k], ["pick%d" % k])
         ts(T.off[:, 16 * k:16 * (k + 1)], T.pick[:, a:a + 4 * NH].indirect(T.sel[:, 0:1]), float(H), A.add, ["pick%d" % k, "sel"], ["off%d" % k], c=picked(16))
 
     def unpack(t, k):
         lq, ls = T["lq%d" % t], T["ls%d" % t]
-        for b, bk in enumerate((6, 7, 6, 7)):
+        for b, bk in enumerate((3, 0, 3, 0)):
             mm(bk, T.eq[:, 128 * b:128 * b + 128], T.es[:, 128 * b:128 * b + 128], lq[:, H * k:H * (k + 1)], ls[:, H * k:H * (k + 1)], ["e%d" % b, "ls%d" % t, "lq%d.0" % t, "lq%d.%d" % (t, k)])
             act(plane(b, (DL, DU)[k]), bank(bk), AF.Copy, [], ["d%d.%d" % (k, b), "ps%d" % bk], cyc(H), scale=32.0)
 
@@ -338,33 +358,39 @@ def rank_program(g, core, T, topo):
         for k in range(2):
             stage[0] = "LU"[k]
             pack(t, k)
-        for k, bk in ((0, 0), (1, 2), (1, 1)):
-            mm(bk, T.upq[:], T.ups[:], xq[:, H * k:H * (k + 1)], xs[:, H * k:H * (k + 1)], ["upq", "ups", "xq%d.%d" % (t, k)])
-        mm(3, T.uwq[:], T.uws[:], xq[:], xs[:], ["uwq", "uws", "xq%d.0" % t, "xq%d.1" % t], n=C)
+        for k in range(2):
+            mm(k, T.upq[:], T.ups[:], xq[:, H * k:H * (k + 1)], xs[:, H * k:H * (k + 1)], ["upq", "ups", "xq%d.%d" % (t, k)])
+        for e in range(2):
+            mm((2, 7)[e], T.ueq[:, 128 * e:128 * e + 128], T.ues[:, 128 * e:128 * e + 128], xq[:, 0:H], xs[:, 0:H], ["ueq", "ues", "xq%d.0" % t])
+        for k in range(2):
+            mm(3 + 3 * k, T.uwq[:, 0:128], T.uws[:, 0:128], xq[:, H * k:H * (k + 1)], xs[:, H * k:H * (k + 1)], ["uwq", "xq%d.%d" % (t, k)])
         send(t, lq[:, 0:H].bitcast(dt.uint8), xq[:, 0:H].bitcast(dt.uint8), ["xq%d.0" % t], ["lq%d.0" % t], "arrQ0%d" % t, 2, 2 * REMOTE)
         send(t, ls[:], xs[:], ["xq%d.0" % t, "xq%d.1" % t], ["ls%d" % t], "arrQ0%d" % t, 2, 2 * REMOTE)
-        send(t, lq[:, H:C].bitcast(dt.uint8), xq[:, H:C].bitcast(dt.uint8), ["xq%d.1" % t], ["lq%d.1" % t], "arrQ1%d" % t, 1, 2 * REMOTE)
-        stage[0] = "x"
-        taken()
         stage[0] = "L"
+        taken(0)
         triangle(0, True)
         table(t, 0)
         stage[0] = "U"
+        taken(1)
         triangle(1, False)
         rectangle()
         table(t, 1)
+        send(t, lq[:, H:C].bitcast(dt.uint8), xq[:, H:C].bitcast(dt.uint8), ["xq%d.1" % t, "tab%d.1" % t], ["lq%d.1" % t], "arrQ1%d" % t, 1, 2 * REMOTE)
+        if t == 1:
+            iota(T.nw[:, 0:512], [[C, 2], [1, TK]], 0, 0, ["nw0"], 512, ["lq1.1"])
+            iota(T.nw[:, XU:XU + 512], [[C, 2], [1, TK]], H, 0, ["nw2"], 512, ["lq1.1"])
         stage[0] = "L"
         places(t, 0)
-        cp(T.nl[:].indirect(T.pl[:, 0:NH]), T.src[:, 0:H], ["src", "pl0"], ["nl"], 50 + 2.5 * H)
+        cp(T.nl[:].indirect(T.pl[:, 0:NH]), T.src[:, 0:H], ["src0", "pl0"], ["nl"], 50 + 2.5 * H)
         choose(2, T.nl, 0, "nl")
         unpack(t, 0)
         for b in range(4):
-            act(plane(b, LS), plane(b, XL, LS).indirect(T.off[:, 32:32 + NH]), AF.Copy, ["p0.%d" % b, "d0.%d" % b, "pad0.%d" % b, "off2"], ["ls.%d" % b], picked(H))
+            scaled(SORTS[b], plane(b, LS), plane(b, XL, LS).indirect(T.off[:, 32:32 + NH]), 1.0, ["p0.%d" % b, "d0.%d" % b, "pad0.%d" % b, "off2"], ["ls.%d" % b], picked(H))
         stage[0] = "U"
         unpack(t, 1)
         dma("S", T.nm[:], T.pre[:], ["pre"], ["nm"], "dn")
         places(t, 1)
-        cp(T.nm[:].indirect(T.pl[:, NH:2 * NH]), T.src[:, H:C], ["src", "pl1"], ["nm"], 50 + 2.5 * H)
+        cp(T.nm[:].indirect(T.pl[:, NH:2 * NH]), T.src[:, H:C], ["src1", "pl1"], ["nm"], 50 + 2.5 * H)
         scan(T.nu[:], T.keep[:], T.nm[:], col(KI), A.mult, A.add, ["keep", "nm", "ki"], ["nu"], cyc(H + 8))
         for k in range(2):
             stage[0] = "ab"[k]
@@ -373,17 +399,19 @@ def rank_program(g, core, T, topo):
             a, z = H * k, H * (k + 1)
             stage[0] = "LU"[k]
             for b in range(4):
-                scaled("VA"[b % 2], T.z[:, 4 * a + b:4 * z:4], plane(b, LS, PL - LS).indirect(T.off[:, 16 * k:16 * k + NH]), 0.03125,
+                scaled(PARTS[4 * k + b], T.z[:, 4 * a + b:4 * z:4], plane(b, LS, PL - LS).indirect(T.off[:, 16 * k:16 * k + NH]), 0.03125,
                        ["ls.%d" % b, "p1.%d" % b, "d1.%d" % b, "pad1.%d" % b, "off%d" % k], ["z%d.%d" % (k, b)], picked(H))
             quant(T.zq[:, a:z], T.zs[:, a:z], T.z[:, 4 * a:4 * z], keys("z", k), ["zq%d" % k], H)
-            scaled("VA"[k], T.z32[:, 4 * a:4 * z], T.z[:, 4 * a:4 * z], 32.0, keys("z", k), ["z32%d" % k], cyc(2 * H * (k + 1)))
+            for b in range(4):
+                q = TIMES32[4 * k + b]
+                scaled(q, T.z32[:, 4 * a + b:4 * z:4], T.z[:, 4 * a + b:4 * z:4], 32.0, ["z%d.%d" % (k, b)], ["zz%d.%d" % (k, b)], cyc(H if q == "A" else H // 2))
         for k in range(2):
             a, z = H * k, H * (k + 1)
             stage[0] = "LU"[k]
             for b in range(4):
                 mm(4 * k + b, T.wq[:, 128 * b:128 * b + 128], T.wsc[:, 128 * b:128 * b + 128], T.zq[:, a:z], T.zs[:, a:z], ["wq", "wsc", "zq%d" % k])
-                tt(plane(b, (XL, XU)[k]), bank(4 * k + b), T.z32[:, 4 * a + b:4 * z:4], A.add, ["z32%d" % k, "ps%d" % (4 * k + b)], ["p%d.%d" % (k, b)], cyc(H))
-                q = "V" if k and b > 1 else "A"
+                tt(plane(b, (XL, XU)[k]), bank(4 * k + b), T.z32[:, 4 * a + b:4 * z:4], A.add, ["zz%d.%d" % (k, b), "ps%d" % (4 * k + b)], ["p%d.%d" % (k, b)], cyc(H))
+                q = BY32[4 * k + b]
                 scaled(q, T.xb[:, 4 * a + b:4 * z:4], plane(b, (XL, XU)[k]), 0.03125, ["p%d.%d" % (k, b)], ["x%d.%d" % (k, b)], cyc(H if q == "A" else H // 2))
 
     stage[0] = "end"
@@ -401,11 +429,17 @@ def rank_program(g, core, T, topo):
     for k in range(4):
         dma("A" if k < 3 else "S", T.osc[4 * k:4 * k + 4, :], T.xs3[32 * k:32 * k + 4, :], ["xq3.0", "xq3.1"], ["osc%d" % k], "dout", 80)
 
-    know, count = {q: {} for q in Q}, {}
-    for c in arrange(calls):
-        q = c["q"]
+    know, count, done = {q: {} for q in Q}, {}, {}
+    order, end = arrange(calls)
+    for c in order:
+        q, at = c["q"], end[c["n"]] - c["lag"] - c["cost"]
+        if not c["sem"]:
+            done.setdefault("c" + q, []).append(c)
         for src, n, snap in sorted([d["mark"] for d in c["deps"] if not (c["group"] and d["q"] == "P")], key=lambda m: -m[1]):
             if know[q].get(src, 0) < n:
+                for d in done.get(src, [])[n:]:
+                    if end[d["n"]] + LONG <= at:
+                        n, snap = d["mark"][1:]
                 Q[q].wait_ge(T.sem[src], n)
                 know[q][src] = n
                 for k, x in snap.items():

from concourse.mybir import dt, AluOpType, ActivationFunctionType

C, CAP, MASK = 384, 160, [1, 2, 4]
H = C // 2
NH = H // 16
TK = 256
PL = 1088
XL, DL, LS, XU, DU = 0, TK, 448, 640, 640 + TK
BIG = 2.0 ** 96
CODES, PLANE = "float8_e4m3fn_x4", "uint8"
F32, BF, U16, I32 = "float32", "bfloat16", "uint16", "int32"
CT = 4 * 448
SAME, OTHER, LOCAL, REMOTE = 240.0, 250.0, 2000.0, 1700.0
LONG = 350.0
TIMES32 = "VVVVAAAA"
BY32 = "AAAAAAVV"
SPREAD = "AAAA"
PARTS = "VAVAVAVA"
SORTS = "AAAA"
URGE = {'cq:start': 1000, 'e:start': -3000, 'w:L': 2000, 'lt:L': 1000, 'sx:U': 3000, 'ct:L': 1000, 'cq:L': 3000, 'w:U': -1000, 'sb:U': 1000, 'ct:U': -1000, 'pj:start': 2000, 'ki:start': 2000, 'uwq:start': -2000, 'sa:U': -1000, 'one:start': 500, 'th:start': -3000, 'w:start': -1000, 'cq:U': -2000, 'pg:start': 5000, 'raw:L': -2000, 'src:U': -2000, 'nt:b': -3000, 'sx:L': 1000, 'rst:start': -1000, 'nt:L': -2000, 'p:U': 2000, 'hi:start': -1000, 'fin:U': -500}


def _sb(n, d):
    return ("sbuf", [128, n], d)


SCRATCH = {
    "win": _sb(4 * PL, BF), "xb": _sb(4 * C, BF), "ub": _sb(512, BF), "vb": _sb(512, BF),
    "uq": _sb(128, CODES), "us": _sb(128, PLANE), "upq": _sb(128, CODES), "ups": _sb(128, PLANE),
    "uwq": _sb(136, CODES), "uws": _sb(136, PLANE), "vq": _sb(128, CODES), "vs": _sb(128, PLANE), "wq": _sb(512, CODES), "wsc": _sb(512, PLANE),
    "tab": _sb(12 * NH, F32), "land": _sb(12 * NH, F32),
    "sa": _sb(C, F32), "sb": _sb(C, F32), "madd": _sb(H, F32), "rst": _sb(H, BF),
    "ct": _sb(2 * CT, BF), "cq": _sb(6 * H, CODES), "cs": _sb(6 * H, PLANE),
    "sg": _sb(12 * H, BF), "rt": _sb(12 * H, BF), "su": _sb(H, F32), "rc": _sb(NH, F32), "ueq": _sb(256, CODES), "ues": _sb(256, PLANE),
    "lt": _sb(C, F32), "w1": _sb(C + 2, BF), "w0": _sb(C, BF), "w2": _sb(C, BF), "raw": _sb(C, BF), "src": _sb(C, BF), "tt": _sb(C, BF),
    "own": _sb(4 * NH, F32), "mc": _sb(4 * NH, F32), "bc": _sb(C, F32), "ab": _sb(2 * C, F32), "c1": _sb(C, BF), "fin": _sb(2 * NH * C, F32),
    "pl": _sb(2 * NH, U16), "nl": _sb(H + 16, BF), "nm": _sb(C + 16, BF), "nu": _sb(C + 16, BF), "pre": _sb(C + 16, BF), "keep": _sb(C + 16, BF),
    "nt": _sb(3 * C, BF), "pick": _sb(12 * NH, F32), "off": _sb(48, U16),
    "z": _sb(4 * C, BF), "zq": _sb(C, CODES), "zs": _sb(C, PLANE), "z32": _sb(4 * C, BF),
    "nw": _sb(1152, F32), "odr": _sb(C, F32), "ysb": _sb(C, F32), "nil": _sb(512, BF),
    "pi": _sb(8, I32), "pj": _sb(8, I32), "pf": _sb(8, F32), "pk": _sb(16, F32), "li": _sb(32, I32), "lu": _sb(44, U16),
    "sel": _sb(4, U16), "rr": _sb(H, F32), "cg": _sb(512, BF), "kb": _sb(512, BF), "kq": _sb(128, CODES), "ks": _sb(128, PLANE),
    "one": _sb(516, BF), "fb": _sb(516, BF), "eq": _sb(512, CODES), "es": _sb(512, PLANE),
    "ps": ("psum", [128, 4096], F32),
}
for _t in range(4):
    SCRATCH["xq%d" % _t] = _sb(C, CODES)
    SCRATCH["xs%d" % _t] = _sb(C, PLANE)
for _t in range(3):
    SCRATCH["lq%d" % _t] = _sb(C, CODES)
    SCRATCH["ls%d" % _t] = _sb(C, PLANE)

SEMAPHORES = (["cV", "cA", "cP", "cG", "left", "dx", "dx2", "du", "dv", "dw", "dod", "dout", "dy", "dn", "dy2", "do2"]
              + ["arr%s%d" % (k, t) for t in range(3) for k in ("T0", "T1", "Q0", "Q1")])


def arrange(calls):
    def gap(a, b):
        return 0.0 if a["lag"] or (b["group"] and a["q"] == "P") else SAME if a["q"] == b["q"] else OTHER

    for c in calls:
        c["next"] = []
    for c in calls:
        for d in c["deps"]:
            d["next"].append(c)

    def sweep(before, after, way, back):
        free, order, left, at, end = {}, [], {c["n"]: len(c[before]) for c in calls}, {}, {}
        ready = [c for c in calls if not c[before]]
        for c in ready:
            at[c["n"]] = c["lag"] if back else 0.0
        while ready:
            c = min(ready, key=lambda c: (int(max(at[c["n"]], free.get(c["q"], 0.0))), -way[c["n"]]))
            ready.remove(c)
            order.append(c)
            free[c["q"]] = max(at[c["n"]], free.get(c["q"], 0.0)) + c["cost"]
            end[c["n"]] = free[c["q"]] + (0.0 if back else c["lag"])
            for n in c[after]:
                left[n["n"]] -= 1
                if not left[n["n"]]:
                    at[n["n"]] = max(end[d["n"]] + (gap(n, d) + n["lag"] if back else gap(d, n)) for d in n[before])
                    ready.append(n)
        return order, end

    way = {}
    for c in reversed(calls):
        way[c["n"]] = c["cost"] + c["lag"] + max([gap(c, n) + way[n["n"]] for n in c["next"]] + [0.0])
    way = sweep("next", "deps", sweep("deps", "next", way, False)[1], True)[1]
    return sweep("deps", "next", {c["n"]: way[c["n"]] + URGE.get(c["tag"], 0) for c in calls}, False)


def rank_program(g, core, T, topo):
    rank = T.rank_of(core)
    if rank is None:
        return
    A, AF = AluOpType, ActivationFunctionType
    Q = {"V": g.vector, "A": g.scalar, "P": g.tensor, "G": g, "S": g.sync}
    calls, wrote, read, stage = [], {}, {}, ["start"]

    def op(q, call, R, W, cost, lag=0.0, sem=None, total=None, group=False, far=False):
        deps = [wrote[k] for k in list(R) + list(W) if k in wrote]
        for k in W:
            deps += read.get(k, [])
        me = {"q": q, "call": call, "cost": cost, "lag": lag, "sem": sem, "total": total, "group": group, "far": far, "n": len(calls),
              "tag": W[0].rstrip("0123456789.") + ":" + stage[0]}
        me["deps"] = list({d["n"]: d for d in deps}.values())
        calls.append(me)
        for k in R:
            read.setdefault(k, []).append(me)
        for k in W:
            wrote[k] = me
            read[k] = []

    def cyc(n):
        return 0.83 * max(64, n)

    def picked(n):
        return 60 + 1.25 * n

    def bank(k, a=0, b=H):
        return T.ps[:, 512 * k + a:512 * k + b]

    def ts(out, in0, s1, op0, R, W, s2=None, op1=None, c=53.0):
        if op1 is None:
            op("V", lambda: g.vector.tensor_scalar(out, in0, s1, None, op0), R, W, c)
        else:
            op("V", lambda: g.vector.tensor_scalar(out, in0, s1, s2, op0, op1), R, W, c)

    def tt(out, in0, in1, o, R, W, c=53.0):
        op("V", lambda: g.vector.tensor_tensor(out, in0, in1, o), R, W, c)

    def cp(out, in_, R, W, c=53.0):
        op("V", lambda: g.vector.tensor_copy(out, in_), R, W, c)

    def fill(ap, x, W, c=53.0):
        op("V", lambda: g.vector.memset(ap, x), [], W, c)

    def scan(out, d0, d1, init, op0, op1, R, W, c=53.0):
        op("V", lambda: g.vector.tensor_tensor_scan(out, d0, d1, init, op0, op1), R, W, c)

    def turn(out, in_, R, W, c):
        op("V", lambda: g.vector.transpose(out, in_), R, W, c)

    def quant(q, s, in_, R, W, n):
        op("V", lambda: g.vector.quantize_mx(q, s, in_), R, W, 12 + 0.88 * n)

    def act(out, in_, f, R, W, c, **kw):
        op("A", lambda: g.scalar.activation(out, in_, f, **kw), R, W, c)

    def mm(k, wq, wsc, xq, xs, R, start=True, stop=True, n=H):
        op("P", lambda: g.tensor.matmul_mx(bank(k, 0, n), wq, wsc, xq, xs, start, stop), R, ["ps%d" % k], 0.5 * (n + 16), group=not start)

    def iota(out, pat, base, cm, W, n, R=()):
        op("G", lambda: g.iota(out, pat, base, cm, allow_small_or_imprecise_dtypes=True), R, W, 130 + 1.66 * n)

    def dma(q, out, in_, R, W, sem, total=None):
        op(q, lambda: Q[q].dma_start(out, in_), R, W, 60.0, LOCAL * (1.2 if sem in ("dx", "dx2") else 1.0), sem, total)

    partners = [T.cores[rank ^ m] for m in MASK]
    mask = topo.mask(core, partners[0])
    for p in partners:
        mask &= topo.mask(core, p)
    width = len([k for k in topo.engines(core, partners[0]) if mask >> k & 1])

    def send(t, out, in_, R, W, sem, writes=1, lag=REMOTE):
        rid, pid, _ = topo.addr(partners[t])
        op("G", lambda: g.remote_dma(out, in_, T.sem[sem], T.sem.left, pid, rid, mask), R, W, 300.0, lag, sem, writes * width, far=True)

    def col(k):
        return T.pk[:, k:k + 1]

    def pf(k):
        return T.pf[:, k:k + 1]

    def plane(b, a, n=H):
        return T.win[:, PL * b + a:PL * b + a + n]

    def keys(name, k):
        return ["%s%d.%d" % (name, k, b) for b in range(4)]

    def zero(out, n, W):
        act(out, T.nil[:, 0:n], AF.Copy, ["nil"], W, cyc(n))

    TH, AC, C1, NTH, INI, HI, E3, PRE, KI, PK, S0, S1, PR2, S2, S3, S4 = range(16)
    tile0 = (0, 4 * H, 4 * H + 512)

    dma("A", T.ub[:], T.u[:], [], ["ub"], "du")
    dma("S", T.xb[:, 0:4 * H], T.x[:, 0:4 * H], [], keys("x", 0) + ["in0"], "dx")
    dma("S", T.xb[:, 4 * H:4 * C], T.x[:, 4 * H:4 * C], [], keys("x", 1) + ["in1"], "dx2")
    dma("S", T.wq[:].bitcast(dt.uint8), T.wc[:], ["in0", "in1"], ["wq"], "dw", 32)
    dma("S", T.wsc[:], T.ws[:], ["in0", "in1"], ["wsc"], "dw", 32)
    dma("S", T.vb[:], T.v[:], ["in0", "in1"], ["vb"], "dv")
    iota(T.pi[:], [[0, 8]], 0, 1, ["pi"], 8)
    iota(T.li[:, 0:NH], [[1, NH]], 0, 0, ["li"], NH)
    iota(T.li[:, 16:32], [[16, 2], [32, 4], [0, 2]], 0, 0, ["lj"], 16)
    iota(T.rr[:], [[0, NH], [1, 16]], 0, 0, ["rr"], H)
    iota(T.cg[:], [[1, 8], [0, 64]], 0, 0, ["cg"], 512)
    fill(T.nil[:], 0.0, ["nil"], cyc(256))
    fill(T.one[:], 1.0, ["one"], cyc(258))
    fill(T.rst[:], 0.0, ["rst"], cyc(96))
    fill(T.rst[:, 0:H:16], -BIG, ["rst"])
    fill(T.w1[:, 0:2], 0.0, ["w10"])
    op("G", lambda: g.affine_select(T.fb[:], T.one[:], [[1, 516]], A.is_equal, 0.0, -3, -4), ["one"], ["fb"], 1030.0)
    ts(T.pj[:, 1:2], T.pi[:, 1:2], 4, A.arith_shift_right, ["pi"], ["pj1"])
    for k, bits in ((0, 15), (2, 16), (3, 12), (4, 1)):
        ts(T.pj[:, k:k + 1], T.pi[:, k:k + 1], bits, A.bitwise_and, ["pi"], ["pj%d" % k])
    cp(T.pf[:, 0:2], T.pj[:, 0:2], ["pj0", "pj1"], ["pf"])
    cp(T.pf[:, 2:5], T.pj[:, 2:5], ["pj%d" % k for k in range(2, 5)], ["pg"])
    ts(T.lu[:, 0:8], T.li[:, 0:8], 16.0, A.mult, ["li"], ["lu0"])
    ts(T.lu[:, 8:20], T.li[:, 0:NH], 2.0, A.mult, ["li"], ["lu1"], 1.0, A.add)
    cp(T.lu[:, 28:44], T.li[:, 16:32], ["lj"], ["lu3"])
    ts(T.madd[:], T.rr[:], pf(0), A.not_equal, ["rr", "pf"], ["madd"], -BIG, A.mult, cyc(H))
    ts(T.kb[:], T.cg[:], pf(1), A.is_equal, ["cg", "pf"], ["kb"], c=cyc(256))
    quant(T.kq[:], T.ks[:], T.kb[:], ["kb"], ["kq"], 128)
    for k in range(2):
        for j, n in enumerate((192, 192, 448)):
            zero(T.ct[:, CT * k + tile0[j]:CT * k + tile0[j] + n], n, ["ct%d.%d" % (k, 4 * j + s) for s in range(4)])
            if j:
                a = H * (3 * k + j)
                quant(T.cq[:, a:a + 128], T.cs[:, a:a + 128], T.nil[:], ["nil"], ["cq%d.%d" % (k, j)], 128)
    zero(T.tab[:], 12 * NH, ["tab%d.%d" % (i, k) for i in range(3) for k in range(2)])
    zero(T.nl[:], H + 16, ["nl"])
    for k, a in enumerate((XL + H, XU + H)):
        for b in range(4):
            zero(plane(b, a, TK - H), TK - H, ["pad%d.%d" % (k, b)])
    ts(col(TH), pf(3), 8.0, A.not_equal, ["pg"], ["th"], -BIG, A.mult)
    ts(col(NTH), pf(3), 8.0, A.not_equal, ["pg"], ["nth"], BIG, A.mult)
    ts(col(AC), pf(3), 8.0, A.is_equal, ["pg"], ["ac"], float(TK * 256), A.mult)
    ts(col(C1), col(AC), (255.0 * TK - 1) / (TK * 256.0), A.mult, ["ac"], ["c1c"], 1.0, A.add)
    ts(col(INI), col(AC), -((256 - CAP - 1) * TK - H - 1) / (TK * 256.0), A.mult, ["ac"], ["ini"], -float(H + 1), A.add)
    ts(col(S0), pf(3), -TK / 4.0, A.mult, ["pg"], ["s0"], 3.0 * TK, A.add)
    ts(col(S1), pf(3), float(TK), A.mult, ["pg"], ["s1"], -3.0 * TK, A.add)
    tt(col(HI), col(S0), col(S1), A.min, ["s0", "s1"], ["hi"])
    ts(col(E3), pf(3), 12.0, A.is_equal, ["pg"], ["e3"])
    ts(col(PRE), pf(3), TK / 2.0, A.mult, ["pg"], ["pre0"], -3.0 * TK, A.add)
    ts(col(PR2), col(E3), col(PRE), A.min, ["e3", "pre0"], ["pre1"])
    ts(col(PK), pf(2), -(2.0 ** 23 + 1), A.add, ["pg"], ["pk"])
    ts(col(KI), pf(2), -1.0, A.mult, ["pg"], ["ki"], -float(H + 1), A.add)
    ts(col(S2), pf(4), 2.0 * NH - 2, A.mult, ["pg"], ["s2"], 1.0, A.add)
    ts(col(S3), pf(0), 2.0, A.mult, ["pf", "s2"], ["s3"], col(S2), A.add)
    ts(col(S4), col(S3), 4.0 * NH - 3, A.min, ["s3"], ["s4"])
    ts(T.sel[:, 0:1], pf(2), 0.125, A.mult, ["pg", "s4"], ["sel"], col(S4), A.add)
    act(T.c1[:, 0:C:2], T.madd[:], AF.Identity, ["madd"], ["c1a"], cyc(H), bias=2.0 ** 36, scale=2.0 ** -60)
    act(T.c1[:, 1:C:2], T.madd[:], AF.Identity, ["madd"], ["c1b"], cyc(H), bias=-2.0 ** 36, scale=-2.0 ** -60)
    act(T.keep[:], T.nil[:, 0:C + 16], AF.Identity, ["nil", "e3"], ["keep"], cyc(C + 16), bias=col(E3))
    act(T.pre[:], T.nil[:, 0:C + 16], AF.Identity, ["nil", "pre1"], ["pre"], cyc(C + 16), bias=col(PR2))
    for b in range(4):
        quant(T.eq[:, 128 * b:128 * b + 128], T.es[:, 128 * b:128 * b + 128], T.fb[:, 3 - b:515 - b], ["fb"], ["e%d" % b], 128)
    quant(T.uq[:], T.us[:], T.ub[:], ["ub"], ["uq"], 128)
    for a in (0, 8):
        quant(T.uwq[:, a:a + 128], T.uws[:, a:a + 128], T.ub[:], ["ub"], ["uwq"], 128)
    quant(T.vq[:], T.vs[:], T.vb[:], ["vb"], ["vq"], 128)
    cp(T.upq[:].bitcast(dt.uint32), T.uq[:].bitcast(dt.uint32).indirect(T.lu[:, 0:8]), ["uq", "lu0"], ["upq"], picked(128))
    act(T.ups[:], T.us[:].indirect(T.lu[:, 0:8]), AF.Copy, ["uq", "lu0"], ["ups"], picked(128))
    cp(T.ueq[:].bitcast(dt.uint32), T.uq[:].bitcast(dt.uint32).indirect(T.lu[:, 28:44]), ["uq", "lu3"], ["ueq"], picked(256))
    act(T.ues[:], T.us[:].indirect(T.lu[:, 28:44]), AF.Copy, ["uq", "lu3"], ["ues"], picked(256))
    for k in range(2):
        for b in range(4):
            act(plane(b, (XL, XU)[k]), T.xb[:, 4 * H * k + b:4 * H * (k + 1):4], AF.Copy, keys("x", k), ["p%d.%d" % (k, b)], cyc(H), scale=32.0)

    def score(k, c):
        return T.sb[:, H * k + 16 * c + 15:H * k + 16 * c + 16]

    def pack(t, k):
        a, b = H * k, H * (k + 1)
        quant(T["xq%d" % t][:, a:b], T["xs%d" % t][:, a:b], T.xb[:, 4 * a:4 * b], keys("x", k), ["xq%d.%d" % (t, k)], H)

    def triangle(k, first):
        a, z = H * k, H * (k + 1)
        tt(T.sa[:, a:z], bank(k), T.madd[:], A.add, ["madd", "ps%d" % k], ["sa%d" % k], cyc(H))
        scan(T.sb[:, a:z], T.rst[:], T.sa[:, a:z], 0.0, A.add, A.max, ["rst", "sa%d" % k], ["sb%d" % k], cyc(H))
        tt(T.ct[:, CT * k:CT * k + 4 * H:4], bank(k), T.sb[:, a:z], A.is_le, ["sb%d" % k, "ps%d" % k], ["ct%d.0" % k], cyc(H))
        for c in range(1, NH):
            j = c // 4
            at = CT * k + tile0[j] - (256 if j else 0)
            ts(T.ct[:, at + 64 * c + c % 4:at + 4 * H:4], bank(k, 16 * c), score(k, c - 1), A.is_le, ["sb%d" % k, "ps%d" % k], ["ct%d.%d" % (k, c)], c=cyc(H - 16 * c))
        for j in range(3):
            a, n = H * (3 * k + j), (128 if j else H)
            quant(T.cq[:, a + H - n:a + H], T.cs[:, a + H - n:a + H], T.ct[:, CT * k + tile0[j]:CT * k + tile0[j] + 4 * n],
                  ["ct%d.%d" % (k, 4 * j + s) for s in range(4)], ["cq%d.%d" % (k, j)], n)
            mm(4 + k, T.kq[:], T.ks[:], T.cq[:, a:a + H], T.cs[:, a:a + H], ["kq", "cq%d.%d" % (k, j)], j == 0, j == 2)

    def rectangle():
        turn(T.su[:], bank(1), ["ps1"], ["su"], cyc(H))
        for j in range(NH):
            a, z, bk = H * j, H * (j + 1), (2, 7)[j % 2]
            act(T.sg[:, a:z], bank(bk), AF.Sign, ["su", "ps%d" % bk], ["sg%d" % j], cyc(H), bias=T.su[:, 16 * j:16 * j + 1], scale=-1.0)
            act(T.rt[:, a:z], T.sg[:, a:z], AF.Sign, ["sg%d" % j], ["rt%d" % j], cyc(H) + 20, bias=1.0, scale=-1.0, accum_out=T.rc[:, j:j + 1])

    def taken(k):
        a, z, bk = H * k, H * (k + 1), 3 + 3 * k
        if k == 0:
            act(T.w0[:, a:z], bank(bk), AF.Sign, ["nth"], ["w0.%d" % k, "ps%d" % bk], cyc(H), bias=col(NTH))
            act(T.w1[:, a + 2:z + 2], T.w0[:, a:z], AF.Relu, ["w0.%d" % k, "ac"], ["w1.%d" % k], cyc(H), scale=col(AC))
            act(T.w2[:, a:z], T.w0[:, a:z], AF.Relu, ["w0.%d" % k, "c1c"], ["w2.%d" % k], cyc(H), scale=col(C1))
        else:
            ts(T.w0[:, a:z], bank(bk), col(TH), A.is_gt, ["th"], ["w0.%d" % k, "ps%d" % bk], c=cyc(H))
            ts(T.w1[:, a + 2:z + 2], T.w0[:, a:z], col(AC), A.mult, ["w0.%d" % k, "ac"], ["w1.%d" % k], c=cyc(H // 2))
            ts(T.w2[:, a:z], T.w0[:, a:z], col(C1), A.mult, ["w0.%d" % k, "c1c"], ["w2.%d" % k], c=cyc(H // 2))
        scan(T.raw[:, a:z], T.w2[:, a:z], T.w1[:, a + 1:z + 1], T.raw[:, a - 1:a] if k else col(INI), A.add, A.subtract,
             ["w1.0", "w1.%d" % k, "w10", "w2.%d" % k, "ini"] + ["raw0"] * k, ["raw%d" % k], cyc(H // 2))
        ts(T.src[:, a:z], T.raw[:, a:z], col(TH), A.max, ["raw%d" % k, "th", "hi"], ["src%d" % k], col(HI), A.min, cyc(H // 2))
        turn(T.tt[:, a:z], T.src[:, a:z], ["src%d" % k], ["tt%d" % k], cyc(H // 2))
        ts(T.own[:, 2 * NH * k:2 * NH * (k + 1):2], T.tt[:, a + 9:z:16], 2.0, A.mult, ["tt%d" % k], ["tk%d" % k])

    def table(t, k):
        a, b = 2 * NH * k, 2 * NH * (2 * t + k)
        turn(T.lt[:, H * k:H * (k + 1)], bank(4 + k), [], ["lt%d" % k, "ps%d" % (4 + k)], cyc(H))
        if k:
            tt(T.tab[:, b + 1:b + 2 * NH:2], T.lt[:, H:C:16], T.rc[:], A.add, ["lt1"] + ["rt%d" % j for j in range(NH)], ["tab%d.1" % t])
        else:
            cp(T.tab[:, b + 1:b + 2 * NH:2], T.lt[:, 0:H:16], ["lt0"], ["tab%d.0" % t])
        send(t, T.land[:, b:b + 2 * NH], T.tab[:, b:b + 2 * NH], ["tab%d.%d" % (t, k)], ["land%d.%d" % (t, k)], "arrT%d%d" % (k, t))
        tt(T.own[:, a + 1:a + 2 * NH:2], T.tab[:, b + 1:b + 2 * NH:2], T.own[:, a:a + 2 * NH:2], A.subtract, ["tab%d.%d" % (t, k), "tk%d" % k], ["own%d" % k])

    def affine(q, out, in_, by, plus, R, W, c):
        if q == "A":
            act(out, in_, AF.Identity, R, W, c, bias=plus, scale=by)
        else:
            ts(out, in_, by, A.mult, R, W, plus, A.add, c)

    def places(t, k):
        a, b, f = 2 * NH * k, 2 * NH * (2 * t + k), NH * C * k
        scan(T.mc[:, a:a + 2 * NH], T.land[:, b:b + 2 * NH], T.own[:, a:a + 2 * NH], 0.0, A.min, A.max, ["land%d.%d" % (t, k), "tk%d" % k, "own%d" % k], ["mc%d" % k])
        affine(SPREAD[k], T.bc[:, H * k:H * (k + 1)], T.mc[:, a:a + 2 * NH].indirect(T.lu[:, 8:20]), 2.0, -0.5, ["mc%d" % k, "lu1"], ["bc%d" % k], picked(H))
        turn(T.ab[:, C * k + 1:C * (k + 1):2], T.bc[:, H * k:H * (k + 1)], ["bc%d" % k], ["b%d" % k], cyc(H))
        affine(SPREAD[2 + k], T.ab[:, C * k:C * (k + 1):2], T.ab[:, C * k + 1:C * (k + 1):2], -1.0, 0.75, ["b%d" % k], ["a%d" % k], cyc(H))
        s1 = f + (NH - 1) * C
        for j, (a, z) in enumerate(((0, 128), (128, C))):
            scan(T.fin[:, s1 + a:s1 + z], T.c1[:, a:z], T.ab[:, C * k + a:C * k + z], 2.0 ** 24, A.add, A.add, ["c1a", "c1b", "a%d" % k, "b%d" % k], [("sx%d", "sy%d")[j] % k], cyc(z - a))
        for c in range(NH - 1):
            a, end = 16 * (c + 1), f + C * (c + 1)
            scan(T.fin[:, end - (H - a):end], T.ab[:, C * k + 2 * a:C * (k + 1):2], T.ab[:, C * k + 2 * a + 1:C * (k + 1):2],
                 T.fin[:, s1 + 32 * c + 31:s1 + 32 * c + 32], A.add, A.add, [("sx%d", "sy%d")[c > 3] % k, "a%d" % k, "b%d" % k], ["fin%d.%d" % (k, c)], cyc(H - a))
        ts(T.pl[:, NH * k:NH * (k + 1)], T.fin[:, f + C - 1:f + NH * C:C], 0.5, A.mult, ["fin%d.%d" % (k, c) for c in range(NH - 1)] + ["pk", "sy%d" % k], ["pl%d" % k], col(PK), A.add)

    def choose(k, row, a, key):
        turn(T.nt[:, C * k:C * k + H], row[:, a:a + H], [key], ["nt0.%d" % k], cyc(H // 2))
        turn(T.nt[:, C * k + H:C * (k + 1)], row[:, a + 16:a + H + 16], [key], ["nt1.%d" % k], cyc(H // 2))
        a = 4 * NH * k
        scan(T.pick[:, a:a + 4 * NH], T.nt[:, C * k + 1:C * (k + 1):8], T.nt[:, C * k + 5:C * (k + 1):8], 0.0, A.add, A.max, ["nt0.%d" % k, "nt1.%d" % k], ["pick%d" % k])
        ts(T.off[:, 16 * k:16 * (k + 1)], T.pick[:, a:a + 4 * NH].indirect(T.sel[:, 0:1]), float(H), A.add, ["pick%d" % k, "sel"], ["off%d" % k], c=picked(16))

    def unpack(t, k):
        lq, ls = T["lq%d" % t], T["ls%d" % t]
        for b, bk in enumerate((3, 0, 3, 0)):
            mm(bk, T.eq[:, 128 * b:128 * b + 128], T.es[:, 128 * b:128 * b + 128], lq[:, H * k:H * (k + 1)], ls[:, H * k:H * (k + 1)], ["e%d" % b, "ls%d" % t, "lq%d.0" % t, "lq%d.%d" % (t, k)])
            act(plane(b, (DL, DU)[k]), bank(bk), AF.Copy, [], ["d%d.%d" % (k, b), "ps%d" % bk], cyc(H), scale=32.0)

    def scaled(q, out, in_, by, R, W, c):
        if q == "A":
            act(out, in_, AF.Copy, R, W, c, scale=by)
        else:
            ts(out, in_, by, A.mult, R, W, c=c)

    for t in range(3):
        xq, xs, lq, ls = T["xq%d" % t], T["xs%d" % t], T["lq%d" % t], T["ls%d" % t]
        for k in range(2):
            stage[0] = "LU"[k]
            pack(t, k)
        for k in range(2):
            mm(k, T.upq[:], T.ups[:], xq[:, H * k:H * (k + 1)], xs[:, H * k:H * (k + 1)], ["upq", "ups", "xq%d.%d" % (t, k)])
        for e in range(2):
            mm((2, 7)[e], T.ueq[:, 128 * e:128 * e + 128], T.ues[:, 128 * e:128 * e + 128], xq[:, 0:H], xs[:, 0:H], ["ueq", "ues", "xq%d.0" % t])
        for k in range(2):
            mm(3 + 3 * k, T.uwq[:, 0:128], T.uws[:, 0:128], xq[:, H * k:H * (k + 1)], xs[:, H * k:H * (k + 1)], ["uwq", "xq%d.%d" % (t, k)])
        send(t, lq[:, 0:H].bitcast(dt.uint8), xq[:, 0:H].bitcast(dt.uint8), ["xq%d.0" % t], ["lq%d.0" % t], "arrQ0%d" % t, 2, 2 * REMOTE)
        send(t, ls[:], xs[:], ["xq%d.0" % t, "xq%d.1" % t], ["ls%d" % t], "arrQ0%d" % t, 2, 2 * REMOTE)
        stage[0] = "L"
        taken(0)
        triangle(0, True)
        table(t, 0)
        stage[0] = "U"
        taken(1)
        triangle(1, False)
        rectangle()
        table(t, 1)
        send(t, lq[:, H:C].bitcast(dt.uint8), xq[:, H:C].bitcast(dt.uint8), ["xq%d.1" % t, "tab%d.1" % t], ["lq%d.1" % t], "arrQ1%d" % t, 1, 2 * REMOTE)
        if t == 1:
            iota(T.nw[:, 0:512], [[C, 2], [1, TK]], 0, 0, ["nw0"], 512, ["lq1.1"])
            iota(T.nw[:, XU:XU + 512], [[C, 2], [1, TK]], H, 0, ["nw2"], 512, ["lq1.1"])
        stage[0] = "L"
        places(t, 0)
        cp(T.nl[:].indirect(T.pl[:, 0:NH]), T.src[:, 0:H], ["src0", "pl0"], ["nl"], 50 + 2.5 * H)
        choose(2, T.nl, 0, "nl")
        unpack(t, 0)
        for b in range(4):
            scaled(SORTS[b], plane(b, LS), plane(b, XL, LS).indirect(T.off[:, 32:32 + NH]), 1.0, ["p0.%d" % b, "d0.%d" % b, "pad0.%d" % b, "off2"], ["ls.%d" % b], picked(H))
        stage[0] = "U"
        unpack(t, 1)
        dma("S", T.nm[:], T.pre[:], ["pre"], ["nm"], "dn")
        places(t, 1)
        cp(T.nm[:].indirect(T.pl[:, NH:2 * NH]), T.src[:, H:C], ["src1", "pl1"], ["nm"], 50 + 2.5 * H)
        scan(T.nu[:], T.keep[:], T.nm[:], col(KI), A.mult, A.add, ["keep", "nm", "ki"], ["nu"], cyc(H + 8))
        for k in range(2):
            stage[0] = "ab"[k]
            choose(k, T.nu, H * k, "nu")
        for k in range(2):
            a, z = H * k, H * (k + 1)
            stage[0] = "LU"[k]
            for b in range(4):
                scaled(PARTS[4 * k + b], T.z[:, 4 * a + b:4 * z:4], plane(b, LS, PL - LS).indirect(T.off[:, 16 * k:16 * k + NH]), 0.03125,
                       ["ls.%d" % b, "p1.%d" % b, "d1.%d" % b, "pad1.%d" % b, "off%d" % k], ["z%d.%d" % (k, b)], picked(H))
            quant(T.zq[:, a:z], T.zs[:, a:z], T.z[:, 4 * a:4 * z], keys("z", k), ["zq%d" % k], H)
            for b in range(4):
                q = TIMES32[4 * k + b]
                scaled(q, T.z32[:, 4 * a + b:4 * z:4], T.z[:, 4 * a + b:4 * z:4], 32.0, ["z%d.%d" % (k, b)], ["zz%d.%d" % (k, b)], cyc(H if q == "A" else H // 2))
        for k in range(2):
            a, z = H * k, H * (k + 1)
            stage[0] = "LU"[k]
            for b in range(4):
                mm(4 * k + b, T.wq[:, 128 * b:128 * b + 128], T.wsc[:, 128 * b:128 * b + 128], T.zq[:, a:z], T.zs[:, a:z], ["wq", "wsc", "zq%d" % k])
                tt(plane(b, (XL, XU)[k]), bank(4 * k + b), T.z32[:, 4 * a + b:4 * z:4], A.add, ["zz%d.%d" % (k, b), "ps%d" % (4 * k + b)], ["p%d.%d" % (k, b)], cyc(H))
                q = BY32[4 * k + b]
                scaled(q, T.xb[:, 4 * a + b:4 * z:4], plane(b, (XL, XU)[k]), 0.03125, ["p%d.%d" % (k, b)], ["x%d.%d" % (k, b)], cyc(H if q == "A" else H // 2))

    stage[0] = "end"
    act(T.nw[:, LS:LS + H], T.nw[:, 0:LS].indirect(T.off[:, 32:32 + NH]), AF.Copy, ["nw0", "off2"], ["nw1"], picked(H))
    for k in range(2):
        act(T.odr[:, H * k:H * (k + 1)], T.nw[:, LS:PL].indirect(T.off[:, 16 * k:16 * k + NH]), AF.Copy, ["nw1", "nw2", "off%d" % k], ["odr%d" % k], picked(H))
    dma("S", T.od[:], T.odr[0:128:16, :], ["odr0", "odr1"], ["od"], "dod")
    for k in range(2):
        a, z = H * k, H * (k + 1)
        pack(3, k)
        mm(k, T.vq[:], T.vs[:], T.xq3[:, a:z], T.xs3[:, a:z], ["vq", "xq3.%d" % k])
        dma("S", T.oc[:, 4 * a:4 * z], T.xq3[:, a:z].bitcast(dt.uint8), ["xq3.%d" % k], ["oc%d" % k], ("do2", "dout")[k], (16, 80)[k])
        scaled("AV"[k], T.ysb[:, a:z], bank(k), 1.0, [], ["ysb%d" % k, "ps%d" % k], cyc(H))
        dma("AS"[k], T.y[:, a:z], T.ysb[:, a:z], ["ysb%d" % k], ["y%d" % k], ("dy2", "dy")[k])
    for k in range(4):
        dma("A" if k < 3 else "S", T.osc[4 * k:4 * k + 4, :], T.xs3[32 * k:32 * k + 4, :], ["xq3.0", "xq3.1"], ["osc%d" % k], "dout", 80)

    know, count, done = {q: {} for q in Q}, {}, {}
    order, end = arrange(calls)
    for c in order:
        q, at = c["q"], end[c["n"]] - c["lag"] - c["cost"]
        if not c["sem"]:
            done.setdefault("c" + q, []).append(c)
        for src, n, snap in sorted([d["mark"] for d in c["deps"] if not (c["group"] and d["q"] == "P")], key=lambda m: -m[1]):
            if know[q].get(src, 0) < n:
                for d in done.get(src, [])[n:]:
                    if end[d["n"]] + LONG <= at:
                        n, snap = d["mark"][1:]
                Q[q].wait_ge(T.sem[src], n)
                know[q][src] = n
                for k, x in snap.items():
                    know[q][k] = max(know[q].get(k, 0), x)
        ins = c["call"]()
        if c["far"]:
            count["left"] = count.get("left", 0) + width
            c["mark"] = (c["sem"], c["total"], {})
            continue
        src, step = (c["sem"], 16) if c["sem"] else ("c" + q, 1)
        count[src] = count.get(src, 0) + step
        ins.then_inc(T.sem[src], step)
        c["mark"] = (src, c["total"] or count[src], dict(know[q]))
    for name in count:
        g.wait_ge(T.sem[name], count[name])
